import numpy as np, ml_dtypes
CORES = [8,136,40,168]
N = 4
BF = ml_dtypes.bfloat16
V, NT, A, S, RO, CAP, VO, L = 2048, 64, 5, 9, 2, 48, 512, 256
def parts(rng):
    par = np.zeros((N, 8, 16, NT), np.int64)
    for j in range(1, A): par[:, :, j] = rng.integers(0, j, (N, 8, NT))
    share = rng.choice(np.array([0.0, 0.3, 0.5, 0.7, 1.0]), (N, 8, 1, NT))
    return {"x": rng.integers(0, 256, (N, 8, 16, V)), "nb": rng.integers(0, V, (N, 8, 16, V)), "feat": rng.integers(0, 256, (N, 8, 16, (A - 1) * NT)), "chg": rng.integers(0, 256, (N, 8, 16, A * NT)),
            "par": par, "swp": (rng.random((N, 8, 16, NT)) < share).astype(np.int64), "wt": rng.integers(0, 64, (N, 8, 16, 1)), "beg": rng.integers(0, V, (N, 8, L)), "tau": rng.integers(0, NT, (N, 8, L))}
def limits(rng, p):
    base = np.array([650, 800, 950, 1100])[(np.arange(8)[None, :] + rng.integers(0, 4, (N, 1))) % 4]
    p["par"][:, :, 9:8 + A] = base[:, :, None, None] + rng.integers(0, 400, (N, 8, A - 1, NT))
    return p
def spell(rng, d):
    a = (d[None, :] + rng.permuted(np.tile(np.arange(16)[:, None], (1, V)), axis=0)) // 16
    t = np.floor(rng.random((8, V)) * (np.minimum(a[::2], 255 - a[1::2]) + 1)).astype(np.int64)
    a[::2] -= t; a[1::2] += t
    return a
def pack(p):
    o = {}
    for k in ("x", "nb", "feat", "chg", "par", "swp", "wt"):
        a = np.ascontiguousarray(p[k]).reshape(N, 128, -1)
        o[k] = a.astype(np.float32).astype(BF) if k in ("x", "feat", "chg", "swp") else a.astype(np.int32)
    o["beg"] = p["beg"].astype(np.int32); o["tau"] = p["tau"].astype(np.int32)
    return o
def setup_inputs(rng):
    return pack(limits(rng, parts(rng)))
def setup_inputs_brim(rng):
    p = parts(rng); p["x"] = np.minimum(p["x"], 254); h = V // 16
    for q in range(N):
        for g in range(8): p["nb"][q, g] = rng.permutation(16)[:, None] * h + rng.integers(0, h, (16, V))
    p["par"][:, :, 9:8 + A] = 4080; odd = np.arange(1, NT, 2); f = rng.integers(1, A, NT // 2)
    p["par"][:, :, 8 + f, odd] = 0; p["feat"][:, :, :, (f - 1) * NT + odd] = 255
    for q in range(N):
        for g in range(8):
            n = int(rng.choice(np.array([0, 1, CAP - 1, CAP, CAP + 1, L])))
            if q == 0: n = (CAP, CAP + 1, L, CAP - 1, 1, 0, CAP, CAP + 1)[g]
            if q == 1 and g < 2: n = CAP
            t = 2 * rng.integers(0, NT // 2, L); t[rng.permutation(L)[n:]] += 1; p["tau"][q, g] = t
    return pack(p)
def setup_inputs_clash(rng):
    p = parts(rng); p["par"][:, :, 9:8 + A] = rng.choice(np.array([4080, 1300]), (N, 8, 1, NT))
    for q in range(N):
        few = rng.permutation(V)[:64]; few[0] = 0; few[1] = V - 1
        p["nb"][q, 0] = few[rng.integers(0, 64, (16, V))]; p["beg"][q, 0] = few[rng.integers(0, 64, L)]
        a = p["tau"][q, 0, 0]; p["beg"][q, 0, 0] = V - 1; p["par"][q, 0, 9:8 + A, a] = 4080; p["swp"][q, 0, :, a] = 1
        p["nb"][q, 1] = p["nb"][q, 1, :1]
        for g in (2, 6): p["nb"][q, g] = np.where(rng.random((16, V)) < 0.5, np.arange(V)[None, :], p["nb"][q, g])
        s = rng.integers(0, V, 24); s[0] = 0; s[1] = V - 1; p["beg"][q, 3] = s[rng.integers(0, 24, L)]
        p["nb"][q, 4] = (V // 8) * rng.integers(0, 8, (16, V)); p["beg"][q, 4] = (V // 8) * rng.integers(0, 8, L)
        for g in (5, 7):
            o = rng.permutation(V); p["nb"][q, g, 0, o] = np.roll(o, -1)
            p["par"][q, g, 1:A] = np.arange(A - 1)[:, None]; p["par"][q, g, 9:8 + A] = 4080
            if g == 5:
                n = 256 // A; s = rng.integers(0, A, L); s[:n] = 0; s[n] = A - 256 % A; s[n + 1] = 0
                p["tau"][q, g] = int(p["tau"][q, g, 0])
            else: s = A * np.arange(L)
            p["beg"][q, g] = o[s % V]
    return pack(p)
def setup_inputs_ties(rng):
    p = parts(rng); p["x"] = rng.integers(0, 4, p["x"].shape); p["feat"] = rng.integers(0, 4, p["feat"].shape)
    p["chg"] = rng.choice(np.array([0, 1, 2, 255]), p["chg"].shape)
    p["par"][:, :, 9:8 + A] = rng.integers(12, 22, (N, 8, A - 1, NT))
    for q in range(N):
        two = rng.integers(0, 256, (16, 2)); p["x"][q, 1] = two[:, rng.integers(0, 2, V)]; p["feat"][q, 1] = two[:, rng.integers(0, 2, (A - 1) * NT)]
        p["par"][q, 1, 9:8 + A] = rng.choice(np.array([4080, 0]), (A - 1, NT))
        p["nb"][q, 1] = np.where(rng.random((16, V)) < 0.5, np.arange(V)[None, :], p["nb"][q, 1])
        for g, e in ((3, (2048, 2049, 2050, 2051, 2052)), (5, (3839, 3840, 3841, 3900, 4078, 4079, 4080))):
            t = np.array(e); s = spell(rng, np.minimum(t[rng.integers(0, len(e), V)] + rng.integers(-1, 2, V), 4080))
            m = rng.integers(0, 2 if g == 3 else 1, (16, 1))
            p["x"][q, g] = np.where(m == 1, 255 - s, s); p["feat"][q, g] = 255 * m
            p["par"][q, g, 9:8 + A] = t[rng.integers(0, len(e), (A - 1, NT))]
        p["wt"][q, 5] = rng.integers(60, 64, (16, 1))
    return pack(p)
def setup_inputs_walk(rng):
    p = limits(rng, parts(rng))
    for q in range(N):
        for g in range(0, 8, 2):
            v = np.zeros((A, NT), np.int64); v[0] = rng.integers(0, V, NT); v[0, 0] = 0; v[0, 1] = V - 1; a = np.arange(NT)
            for j in range(1, A):
                k = rng.integers(0, 16, NT); e = rng.random(NT); k = np.where(e < 0.25, 0, np.where(e < 0.5, 15, k))
                v[j] = p["nb"][q, g][k, v[p["par"][q, g, j], a]]
                p["feat"][q, g, :, (j - 1) * NT:j * NT] = p["x"][q, g][:, v[j]]; p["par"][q, g, 8 + j] = 0
            t = rng.permutation(np.arange(L) % NT); p["tau"][q, g] = t
            p["beg"][q, g] = np.where(rng.random(L) < 0.3, rng.integers(0, V, L), v[0][t])
    return pack(p)
def setup_inputs_spread(rng):
    p = parts(rng)
    for k in ("x", "feat", "chg"):
        s = p[k].shape; p[k] = np.floor(np.exp2(8 * rng.random((N, 8, 1, s[3]))) * rng.random(s)).astype(np.int64)
    e = rng.permuted(np.tile(np.array([0.5, 0.5, 1.0, 1.0, 2.0, 2.0, 4.0, 4.0]), (N, 1)), axis=1)
    p["par"][:, :, 9:8 + A] = np.minimum(np.floor(4081 * rng.random((N, 8, A - 1, NT)) ** e[:, :, None, None]), 4080).astype(np.int64)
    p["nb"] = np.floor(V * rng.random(p["nb"].shape) ** 2).astype(np.int64); p["beg"] = np.floor(V * rng.random((N, 8, L)) ** 3).astype(np.int64)
    p["wt"] = np.floor(np.exp2(6 * rng.random((N, 8, 16, 1))) * (0.5 + 0.5 * rng.random((N, 8, 16, 1)))).astype(np.int64)
    return pack(p)
def check_inputs(d):
    bad = []
    def test(k, a, lo, hi):
        a = np.asarray(a).astype(np.float64)
        if not (np.all(a >= lo) and np.all(a <= hi) and np.all(a == np.floor(a))): bad.append("range of " + k)
    for k, hi in (("x", 255), ("nb", V - 1), ("feat", 255), ("chg", 255), ("swp", 1), ("wt", 63), ("beg", V - 1), ("tau", NT - 1)): test(k, d[k], 0, hi)
    p = np.asarray(d["par"]).reshape(N, 8, 16, NT); rest = list(range(16))
    for j in range(1, A):
        test("parents in par", p[:, :, j], 0, j - 1); test("thresholds in par", p[:, :, 8 + j], 0, 4080); rest.remove(j); rest.remove(8 + j)
    test("other rows of par", p[:, :, rest], 0, 0)
    return bad
def reference(x, nb, feat, chg, par, swp, wt, beg, tau):
    B = N * 8; b = np.arange(B)[:, None]; b3 = b[:, :, None]; lane = np.arange(L); li = lane[None, :]
    def items(a, ty): return np.array(a.astype(np.float32).reshape(B, 16, -1).transpose(0, 2, 1), dtype=ty, order="C")
    X = items(x, np.int16); NB = items(nb, np.int32); F = items(feat, np.int16); C = items(chg, np.int16); P = items(par, np.int64); H = items(swp, np.int64) == 1
    W = wt.astype(np.int64).reshape(B, 1, 16); m0 = beg.astype(np.int64).reshape(B, L); T = tau.astype(np.int64).reshape(B, L)
    for rnd in range(RO):
        M = np.full((B, L, A), -1, np.int64); M[:, :, 0] = m0; K = np.zeros((B, L, A), np.int64); j = np.ones((B, L), np.int64)
        for step in range(S):
            jj = np.minimum(j, A - 1)
            c = NB[b, M[b, li, P[b, T, jj]]]
            dist = np.add.reduce(np.abs(X[b3, c] - F[b, (jj - 1) * NT + T][:, :, None, :]), axis=3, dtype=np.int32)
            good = (dist <= P[b, T, 8 + jj][:, :, None]) & (np.arange(16) >= K[b, li, jj][:, :, None])
            for i in range(A - 1): good &= (c != M[:, :, i:i + 1]) | (i >= jj)[:, :, None]
            found = np.any(good, axis=2); k = np.argmax(good, axis=2); ck = np.take_along_axis(c, k[:, :, None], 2)[:, :, 0]
            up = (j < A) & found; down = (j < A) & ~found
            bb, ll = np.nonzero(up); M[bb, ll, j[up]] = ck[up]; K[bb, ll, j[up]] = k[up] + 1
            j = np.where(up, j + 1, np.where(down, np.maximum(j - 1, 1), j))
            fresh = up & (j < A); bb, ll = np.nonzero(fresh); K[bb, ll, j[fresh]] = 0
        full = j == A; slot = np.argsort(~full, axis=1, kind="stable")[:, :CAP]
        got = np.take_along_axis(full, slot, 1); Ms = M[b, slot]; Ts = T[b, slot]
        same = np.any(Ms[:, :, None, :, None] == Ms[:, None, :, None, :], axis=(3, 4))
        lower = np.arange(CAP)[None, :] < np.arange(CAP)[:, None]
        go = got & ~np.any(same & lower & got[:, None, :], axis=2)
        bb, ss = np.nonzero(go); mm = Ms[bb, ss]; tt = Ts[bb, ss]; h = H[bb, tt]
        for i in range(0, A - 1, 2):
            p = NB[bb, mm[:, i]]; q = NB[bb, mm[:, i + 1]]
            NB[bb, mm[:, i]] = np.where(h, q, p); NB[bb, mm[:, i + 1]] = np.where(h, p, q)
        new = (X[bb[:, None], mm] + C[bb[:, None], np.arange(A)[None, :] * NT + tt[:, None]]) & 255
        X[bb[:, None], mm] = new
        Z = np.zeros((B, CAP, 16), np.int16); Z[bb, ss] = np.maximum.reduce(new, axis=1)
        Zr = Z.reshape(N, 8, CAP, 16); t = np.arange(CAP)
        come = np.stack([Zr[(r - 1 - t % (N - 1)) % N, :, t].transpose(1, 0, 2) for r in range(N)])
        u = np.add.reduce(X[b, M[b, li, j - 1]].astype(np.int64) * W, axis=2)
        u[:, :CAP] = np.add.reduce(come.reshape(B, CAP, 16).astype(np.int64) * W, axis=2)
        u = u & 4095
        T = (((u * u) >> 5) + li) & (NT - 1); m0 = (37 * u + li) & (V - 1)
    ym = np.where(np.arange(A)[None, None, :] < j[:, :, None], M, -1).transpose(0, 2, 1).reshape(N, 8, A * L)
    yx = X[:, :VO].transpose(0, 2, 1).reshape(N, 128, VO); yz = come.transpose(0, 1, 3, 2).reshape(N, 128, CAP)
    return {"yx": yx.astype(np.float32).astype(BF), "ym": ym.astype(np.float32), "yz": yz.astype(np.float32).astype(BF)}

@@ -1,0 +1,666 @@
+from concourse.bass import DstId, RemoteDMATransfer
+from concourse.mybir import AluOpType as OP, ActivationFunctionType as AF
+
+F, H, B, I, U = "float32", "float16", "bfloat16", "int32", "uint16"
+LV = 1 << 19
+SC = float(1 << 22)
+DEPTH = {1: 4, 2: 3, 3: 3, 4: 2, 5: 1, 6: 0}
+GC, PE = 1.56, 0.6
+HOP, SELF = 140, 70
+
+
+def _scratch():
+    s = {}
+
+    def sb(n, dt, *sh):
+        s[n] = ("sbuf", [128] + list(sh), dt)
+    sb("X", B, 2304); sb("NB", I, 2304); sb("WT", B, 512); sb("TH", B, 512); sb("CH", B, 320); sb("SW", B, 64)
+    sb("PA", I, 64); sb("PB", I, 64); sb("WI", I, 4); sb("BG", I, 256); sb("TA", I, 256)
+    sb("q1", I, 192); sb("q4", F, 64); sb("ci", I, 8); sb("cf", F, 64); sb("io1", F, 168); sb("io2", F, 160); sb("io3", F, 160)
+    sb("t1", F, 160); sb("t2", F, 160); sb("t3", F, 160); sb("own", F, 160); sb("r16", F, 16)
+    sb("IH", H, 128); sb("IB", B, 128); sb("BD", B, 128); sb("SEL", H, 768); sb("BIG", H, 288); sb("I2", H, 128)
+    sb("RI", H, 160); sb("RN", B, 168); sb("RS", B, 16); sb("REW", B, 168); sb("RET", B, 168); sb("RP", B, 160)
+    sb("KN", F, 32); sb("KL", F, 32); sb("KI", I, 32); sb("LI", U, 16); sb("UT", H, 128); sb("ON", H, 128)
+    sb("WD", B, 8); sb("S0", H, 8); sb("THR", F, 240); sb("JJ", F, 16); sb("CJ", F, 16); sb("pw", F, 48)
+    for h in "01":
+        sb("G" + h, B, 2048); sb("A" + h, B, 2048); sb("CU" + h, U, 128); sb("CF" + h, H, 128); sb("W" + h, B, 128)
+        sb("TG" + h, B, 128); sb("EQ" + h, B, 512); sb("P" + h, F, 160); sb("BB" + h, F, 160); sb("RK" + h, F, 640)
+        sb("RW" + h, H, 384); sb("L" + h, U, 16); sb("SM" + h, H, 17, 8); sb("JQ" + h, H, 17, 8); sb("M" + h, H, 8, 16)
+        sb("FU" + h, H, 128); sb("MC" + h, I, 8, 5); sb("YO" + h, I, 32); sb("TT" + h, I, 8)
+        sb("s" + h, F, 160); sb("n" + h, I, 128); sb("VA" + h, F, 8, 6); sb("XG" + h, B, 128)
+        sb("ZS" + h, B, 48); sb("LD" + h, B, 48)
+    sb("MX", F, 272); sb("SG", B, 256); sb("AC", F, 4); sb("LN", U, 4); sb("MS", H, 48); sb("BR", H, 480)
+    sb("LF", F, 32); sb("LU", U, 48); sb("DD", F, 32); sb("OF", U, 16); sb("EW", B, 3600); sb("OK", H, 240)
+    sb("GO", H, 192); sb("CG", B, 240); sb("XS", F, 128); sb("XT", I, 240); sb("XN", I, 240); sb("ZM", B, 192)
+    sb("NG", I, 192); sb("HG", F, 48); sb("ND", F, 192); sb("YZ", B, 48)
+    for k in range(8):
+        s["ps%d" % k] = ("psum", [128, 512], F)
+    return s
+
+
+SCRATCH = _scratch()
+SEMAPHORES = ["cV", "cS", "cP", "cG", "sent", "arr0", "arr1"] + ["d%d" % k for k in range(20)]
+ALL = slice(None)
+WP, EB, PPS, MBS = ("ps0", "ps1"), ("ps2", "ps3"), ("ps4", "ps5"), ("ps6", "ps7")
+
+
+def a(n, lo=None, hi=None, st=None):
+    return (n, (ALL, slice(lo, hi, st)))
+
+
+def a3(n, lo, hi):
+    return (n, (ALL, ALL, slice(lo, hi)))
+
+
+def a2(n, lo, hi):
+    return (n, (ALL, slice(1, 17, 2), slice(lo, hi)))
+
+
+def col(n, c):
+    return a(n, c, c + 1)
+
+
+def ind(win, off):
+    return ("*", win, off)
+
+
+def _span(ap):
+    n, ix = ap
+    sh = SCRATCH[n][1]
+    lo = hi = 0
+    cnt = 1
+    for d in range(1, len(sh)):
+        r = range(sh[d])[ix[d]] if d < len(ix) else range(sh[d])
+        lo = lo * sh[d] + r[0]
+        hi = hi * sh[d] + r[-1]
+        cnt *= len(r)
+    return n, lo, hi, cnt
+
+
+def program():
+    ops = []
+    nd = [0]
+
+    def rec(eng, call, args, outs, ins, cost, **kw):
+        ops.append(dict(eng=eng, call=call, args=args, outs=outs, ins=ins, cost=cost, kw=kw))
+
+    def parts(ap):
+        return [ap[1], ap[2]] if ap[0] == "*" else [ap]
+
+    def cnt(ap):
+        return 16 * _span(ap[2])[3] if ap[0] == "*" else _span(ap)[3]
+
+    def two(*aps):
+        return all(p[0] != "*" and SCRATCH[p[0]][2] in (H, B, U) for p in aps)
+
+    def vcost(out, src, m):
+        if out[0] == "*":
+            return 60 + 3.5 * cnt(out)
+        if src[0] == "*":
+            return 60 + GC * cnt(src)
+        return max(64, m * cnt(src)) + 10
+
+    def sides(out, *srcs):
+        o = parts(out)
+        return o[:1], o[1:] + [p for s in srcs if isinstance(s, tuple) for p in parts(s)]
+
+    def cp(out, src):
+        o, i = sides(out, src)
+        rec("V", "tensor_copy", (out, src), o, i, vcost(out, src, 0.5 if two(out, src) else 1))
+
+    def tt(out, x, y, op):
+        o, i = sides(out, x, y)
+        rec("V", "tensor_tensor", (out, x, y, op), o, i, vcost(out, x, 1 if "ps" in (x[0][:2], y[0][:2]) else 2))
+
+    def ts(out, x, s1, op0, s2=None, op1=None):
+        o, i = sides(out, x, s1, s2)
+        rec("V", "tensor_scalar", (out, x, s1, s2, op0) + ((op1,) if op1 is not None else ()), o, i,
+            vcost(out, x, 0.5 if two(out, x) else 1))
+
+    def scan(out, d0, d1, init, op0, op1):
+        rec("V", "tensor_tensor_scan", (out, d0, d1, init, op0, op1), [out], [d0, d1], vcost(out, d0, 1))
+
+    def ms(out, v):
+        rec("V", "memset", (out, v), [out], [], max(64, cnt(out) * (0.5 if two(out) else 1)))
+
+    def act(out, src, f=AF.Copy, **kw):
+        o, i = sides(out, src, *[kw[k] for k in kw if k != "accum_out"])
+        if "accum_out" in kw:
+            o = o + [kw["accum_out"]]
+        rec("S", "activation", (out, src, f), o, i, 78 + GC * cnt(src) if src[0] == "*" else max(64, cnt(src)) + 10, **kw)
+
+    def mm(out, l, r, st=True, sp=True):
+        rec("P", "matmul", (out, l, r, st, sp), [out], [l, r], PE * max(64, cnt(r)))
+
+    def iota(out, pat, base=0, cm=0):
+        kw = {} if SCRATCH[out[0]][2] == I else {"allow_small_or_imprecise_dtypes": True}
+        rec("G", "iota", (out, pat, base, cm), [out], [], 160 + 2 * cnt(out), **kw)
+
+    def gcopy(out, src):
+        rec("G", "affine_select", (out, src, [[0, cnt(src)]], OP.is_ge, 0.0, 0, 0), [out], [src], 210 + 2 * cnt(src))
+
+    def dma(eng, out, src, cost):
+        rec(eng, "dma_start", (out, src), [out] if out[0] in SCRATCH else [], [src] if src[0] in SCRATCH else [], 70)
+        ops[-1]["sem"] = "d%d" % nd[0]
+        ops[-1]["lat"] = cost
+        nd[0] += 1
+
+    row0 = (slice(0, 128, 16), ALL)
+    ms(a("BG"), 0); ms(a("TA"), 0); ms(a("PB"), 0)
+    dma("Y", a("NB", 0, 2048), ("nb", (ALL, ALL)), 6000)
+    dma("Y", ("BG", row0), ("beg", (ALL, ALL)), 2600)
+    dma("Y", ("TA", row0), ("tau", (ALL, ALL)), 2600)
+    dma("S", a("X", 0, 2048), ("x", (ALL, ALL)), 6200)
+    dma("S", a("PA"), ("par", (ALL, ALL)), 2800)
+    dma("Y", ("PB", (slice(0, 124), ALL)), ("par", (slice(4, 128), ALL)), 2800)
+    dma("S", a("WT", 256, 320), ("feat", (ALL, slice(0, 64))), 3000)
+    dma("S", a("WT", 0, 192), ("feat", (ALL, slice(64, 256))), 3000)
+    dma("Y", a("CH"), ("chg", (ALL, ALL)), 7000)
+    dma("Y", a("SW"), ("swp", (ALL, ALL)), 7000)
+    dma("Y", col("WI", 0), ("wt", (ALL, ALL)), 7000)
+
+    iota(col("ci", 4), [[0, 1]], 0, 1)
+    iota(a("io1"), [[1, 168]])
+    iota(a("t1", 0, 128), [[1, 8], [0, 16]])
+    iota(a("io2"), [[1, 8], [0, 20]])
+    iota(a("io3"), [[0, 8], [1, 20]])
+    iota(a("KN"), [[0, 8], [LV // 32, 4]], LV // 32)
+    iota(a("KI"), [[0, 8], [4096, 4]])
+    iota(a("XS"), [[8, 2], [16, 8], [1, 8]])
+    ts(col("ci", 0), col("ci", 4), 15, OP.bitwise_and)
+    ts(col("ci", 1), col("ci", 4), 4, OP.logical_shift_right)
+    ts(col("ci", 2), col("ci", 4), 12, OP.bitwise_and)
+    cp(col("cf", 0), col("ci", 4))
+    cp(a("cf", 1, 4), a("ci", 0, 3))
+    pp, rr, pg = col("cf", 0), col("cf", 1), col("cf", 2)
+    ts(col("cf", 4), pg, 16.0, OP.mult, 15.0, OP.add)
+    ts(a("BIG", 0, 144), a("io1", 0, 144), col("cf", 4), OP.is_equal)
+    ts(col("cf", 38), rr, 7.5, OP.is_lt, -8.0, OP.mult)
+    ts(col("cf", 39), col("cf", 38), col("cf", 4), OP.add)
+    ts(a("BIG", 144, 288), a("io1", 0, 144), col("cf", 39), OP.is_equal)
+    ts(a("I2"), a("XS"), pp, OP.is_equal)
+    ts(a("r16"), a("io1", 0, 16), rr, OP.is_equal)
+
+    def r(k):
+        return col("r16", k)
+    ts(col("cf", 5), r(0), 256.0, OP.mult)
+    for h in range(2):
+        rw = "RW%d" % h
+        cp(a(rw, 0, 128), a("BG", 128 * h, 128 * h + 128))
+        ts(a(rw, 128, 256), a("TA", 128 * h, 128 * h + 128), col("cf", 5), OP.add)
+        act(a(rw, 256, 384), a(rw, 0, 128))
+    ts(a("IB"), a("io1", 0, 128), pp, OP.is_equal)
+    act(a("IH"), a("IB"))
+    ts(a("BD"), a("t1", 0, 128), pg, OP.is_equal)
+    for i in range(6):
+        act(a("SEL", 128 * i, 128 * i + 128), a("BD"), AF.Identity, scale=r(i))
+    ts(a("q1", 0, 64), a("PA"), 0xF00, OP.bitwise_and)
+    ts(a("q1", 64, 128), a("PB"), 0xFF, OP.bitwise_and)
+    ts(a("q1", 128, 192), a("PA"), 3, OP.bitwise_and)
+    ts(col("cf", 6), rr, 4.5, OP.is_lt)
+    ts(col("cf", 7), rr, 4.5, OP.is_gt)
+    ts(a("q4"), a("q1", 128, 192), col("cf", 6), OP.mult)
+    ts(a("s0", 0, 64), a("q1", 64, 128), col("cf", 7), OP.mult)
+    tt(a("s0", 64, 128), a("q4"), a("q1", 0, 64), OP.add)
+    tt(a("q4"), a("s0", 64, 128), a("s0", 0, 64), OP.add)
+    tt(a("cf", 24, 28), a("r16", 5, 9), a("r16", 9, 13), OP.add)
+    cp(col("cf", 12), col("cf", 27))
+    tt(a("cf", 9, 12), a("cf", 24, 27), a("r16", 2, 5), OP.add)
+    ts(a("cf", 16, 24), a("io1", 2, 10), r(13), OP.mult, r(14), OP.add)
+    ts(col("cf", 20), r(13), r(14), OP.add)
+    ts(col("cf", 28), r(15), -16384.0, OP.mult)
+    ts(a("cf", 19, 24, 4), a("cf", 19, 24, 4), col("cf", 28), OP.add)
+    for b in range(8):
+        j = {0: 2, 1: 3, 2: 4, 4: 1}.get(b)
+        act(a("TH", 64 * b, 64 * b + 64), a("q4"), AF.Identity, scale=col("cf", 8 + j) if j else 0.0, bias=col("cf", 16 + b))
+    ms(a("WT", 192, 256), 0.0); ms(a("WT", 320, 512), 0.0)
+    ts(col("cf", 13), pg, 20.0, OP.mult, 19.0, OP.add)
+    tt(col("cf", 29), col("cf", 13), rr, OP.subtract)
+    ts(a("RI"), a("io1", 0, 160), col("cf", 29), OP.is_equal)
+    ts(a("RN"), a("io1"), col("cf", 29), OP.is_equal, -SC * 8192, OP.mult)
+    ts(a("RS", 0, 8), a("io1", 0, 8), pg, OP.is_equal, SC, OP.mult)
+    ts(a("RS", 8, 16), a("io1", 0, 8), pg, OP.is_equal, -2 * SC, OP.mult)
+    ts(a("S0"), a("io1", 0, 8), pg, OP.is_equal, r(0), OP.mult)
+    ms(a("REW", 160, 168), 0.0); ms(a("RET", 160, 168), 0.0)
+    ts(a("own"), a("io2"), pg, OP.is_equal)
+    ts(a("t2"), a("io3"), 3.5, OP.is_gt, SC, OP.mult)
+    tt(a("REW", 0, 160), a("t2"), a("own"), OP.mult)
+    ts(col("cf", 30), rr, 13.0, OP.not_equal, col("cf", 7), OP.mult)
+    ts(col("cf", 31), r(14), SC, OP.mult)
+    act(a("s1"), a("REW", 0, 160), AF.Identity, scale=col("cf", 30))
+    act(a("t3"), a("own"), AF.Identity, scale=col("cf", 31))
+    tt(a("RET", 0, 160), a("s1"), a("t3"), OP.max)
+    ts(col("cf", 32), col("cf", 6), 4096.0 / SC, OP.mult)
+    ts(col("cf", 33), r(13), LV / SC, OP.mult, col("cf", 32), OP.add)
+    ts(a("t2"), a("io3"), -4.0, OP.add, 0.0, OP.max)
+    ts(a("t3"), a("own"), r(14), OP.mult, 16384.0, OP.mult)
+    tt(a("t1"), a("t2"), a("t3"), OP.mult)
+    act(a("io2"), a("REW", 0, 160), AF.Identity, scale=col("cf", 33))
+    tt(a("RP"), a("t1"), a("io2"), OP.add)
+    act(a("KN"), a("KN"), AF.Identity, scale=32.0)
+    ts(col("cf", 14), col("cf", 3), 5.0, OP.mult, 19.0, OP.add)
+    ts(a("LI", 0, 2), a("io1", 0, 2), 80.0, OP.mult, col("cf", 14), OP.add)
+    ts(a("LI", 2, 10), a("io1", 0, 8), 20.0, OP.mult, 19.0, OP.add)
+    for h in "01":
+        for n in ("SM", "JQ", "M"):
+            ms((n + h, (ALL,)), 0.0)
+
+    def late_constants():
+        act(a("KL"), a("KN"))
+        ms(a("KL", 0, 32, 4), -SC)
+        ms(a("KL", 1, 32, 4), 2.5 * LV)
+        ms(("VA0", (ALL,)), 0.0); ms(("VA1", (ALL,)), 0.0)
+        ts(a("UT"), a("io1", 0, 128), pp, OP.is_ge)
+        ms(a("ON"), 1.0)
+        cp(col("cf", 34), col("WI", 0))
+        ts(a("WD"), a("io1", 0, 8), pg, OP.is_equal, col("cf", 34), OP.mult)
+        ts(col("cf", 35), pp, 128.0, OP.add)
+        ts(col("cf", 36), rr, 0.5, OP.add)
+        ts(a("cf", 40, 43), a("io1", 0, 3), 16.0, OP.mult, col("cf", 36), OP.add)
+        ms(a("t1", 0, 48), 0.25); ms(a("t2", 0, 48), 0.0)
+        scan(a("pw"), a("t1", 0, 48), a("t2", 0, 48), 4.0, OP.mult, OP.add)
+        for j in range(5):
+            act(a("THR", 48 * j, 48 * j + 48), a("pw"), AF.Identity, scale=2.0)
+        tt(a("t3", 0, 16), a("pw", 0, 16), a("r16"), OP.mult)
+        scan(a("t3", 16, 32), a("t3", 0, 16), a("t2", 0, 16), 0.0, OP.add, OP.add)
+        ts(a("cf", 44, 47), a("pw", 0, 48, 16), col("t3", 31), OP.mult)
+        ts(col("cf", 37), rr, 2048.0, OP.add)
+        ts(a("JJ"), a("io1", 0, 16), 16.0, OP.mult, col("cf", 37), OP.add)
+        iota(a("CJ", 0, 15), [[64, 5], [0, 3]])
+        ts(a("MX", 256, 272), a("io1", 0, 16), 0.0, OP.mult, col("cf", 6), OP.subtract)
+        ts(a("ci", 5, 8), a("cf", 40, 43), -1.5, OP.add, 1.0 / 3, OP.mult)
+        ts(a("cf", 48, 51), a("ci", 5, 8), -47.0, OP.mult, -8.0, OP.add)
+        ts(a("cf", 52, 55), a("cf", 40, 43), 16.0, OP.mult)
+        tt(a("cf", 56, 59), a("cf", 48, 51), a("cf", 52, 55), OP.add)
+        cp(a("LI", 10, 13), a("cf", 56, 59))
+
+    def to_list(bank, src, lo, hi, out_lo):
+        n = (hi - lo) // 16
+        for b in range(16):
+            mm(a(bank, out_lo, out_lo + n), a("BIG", 15 - b, 143 - b), a(src, lo + b, hi, 16), b == 0, b == 15)
+
+    def rows(h, names):
+        n = min(len(names), 2)
+        RB, LB = WP[int(h)], PPS[int(h)]
+        for q in range(n):
+            mm(a(RB, 64 * q, 64 * q + 64), (names[q] + h, (ALL, slice(1, 17))), a("I2", 0, 64), True, False)
+            mm(a(RB, 64 * q, 64 * q + 64), (names[q] + h, (ALL, slice(0, 16))), a("I2", 64, 128), False, True)
+        cp(a("RW" + h, 0, 64 * n), a(RB, 0, 64 * n))
+        for b in range(8):
+            mm(a(LB, 0, 8 * n), a("BIG", 151 - b, 279 - b), a("RW" + h, b, 64 * n, 8), b == 0, b == 7)
+        cp(a("L" + h, 0, 8 * n), a(LB, 0, 8 * n))
+        if len(names) > 2:
+            mm(a(MBS[int(h)], 0, 128), (names[2] + h, (ALL,)), a("IH"))
+            act(a("RW" + h, 256, 384), a(MBS[int(h)], 0, 128))
+
+    def prep(h, e):
+        E, Wp, PP, MB = EB[int(h)], WP[int(h)], PPS[int(h)], MBS[int(h)]
+        cp(a("CU" + h), ind(a("NB", 0, 2048), a("L" + h, 0, 8)))
+        act(a("W" + h), ind(a("WT"), a("L" + h, 8, 16)))
+        for q in range(4):
+            mm(a(Wp, q, 512, 4), a("IB"), a("W" + h))
+        for c in range(4):
+            act(a("G" + h, 512 * c, 512 * c + 512), ind(a("X", 0, 2048), a("CU" + h, 32 * c, 32 * c + 32)))
+            ops[-1]["stage"] = 1
+            if c == 0:
+                act(a("TG" + h), ind(a("TH"), a("L" + h, 8, 16)))
+                ops[-1]["stage"] = 1
+        cp(a("CF" + h), a("CU" + h))
+        ne = min(e, 4)
+        for i in range(ne):
+            mm(a(MB, 128 * i, 128 * i + 128), a("SEL", 128 * i, 128 * i + 128), a("RW" + h, 256, 384))
+        for i in range(ne):
+            tt(a("EQ" + h, 128 * i, 128 * i + 128), a("CF" + h), a(MB, 128 * i, 128 * i + 128), OP.is_equal)
+        mm(a(PP, 0, 160), a("CF" + h), a("RI"), True, False)
+        mm(a(PP, 0, 160), a("TG" + h), a("RP"), False, True)
+        act(a("P" + h), a(PP, 0, 160))
+        for rk in range(2, DEPTH[e - 1] + 2 if e > 1 else 0):
+            src = a("RK" + h, 160 * (rk - 2) + 20 - rk, 160 * (rk - 1), 20)
+            if e > 4 and rk == 2:
+                tt(a("P" + h, 3, 160, 20), src, a("s" + h, 96, 104), OP.max)
+            else:
+                gcopy(a("P" + h, 5 - rk, 160, 20), src)
+        mm(a(E, 0, 168), a("W" + h), a("REW"), True, False)
+        mm(a(E, 0, 168), a("TG" + h), a("RET"), False, False)
+        for i in range(ne):
+            mm(a(E, 0, 168), a("EQ" + h, 128 * i, 128 * i + 128), a("RN"), False, False)
+
+    def heavy(h):
+        E, Wp = EB[int(h)], WP[int(h)]
+        for c in range(4):
+            for m in range(4):
+                tt(a("A" + h, 512 * m + 128 * c, 512 * m + 128 * c + 128), a("G" + h, 512 * c + m, 512 * c + 512, 4),
+                   a(Wp, 128 * c, 128 * c + 128), OP.max)
+        for k in range(16):
+            mm(a(E, 19 - k, 160, 20), a("G" + h, k, 2048, 16), a("RS", 0, 8), False, False)
+        for m in range(4):
+            for q in range(4):
+                mm(a(E, 19 - m - 4 * q, 160, 20), a("A" + h, 512 * m + q, 512 * m + 512, 4), a("RS", 8, 16), False, m + q == 6)
+
+    def post(h, e, rnd):
+        E = EB[int(h)]
+        s, n, MC, BB = "s" + h, "n" + h, "MC" + h, "BB" + h
+        scan(a(BB), a(E, 0, 160), a("P" + h), 0.0, OP.max, OP.min)
+        tt(a(n, 0, 32), ind(a(BB), a("LI", 0, 2)), a("KL" if e == 6 else "KN"), OP.subtract)
+        tt(a(n, 32, 64), a(n, 0, 32), a("YO" + h), OP.min)
+        ts(a3(MC, 1, 5), a(n, 32, 64), (1 << 21) | 2047, OP.bitwise_and)
+        if e < 6:
+            ts(a(n, 64, 96), a(n, 0, 32), 0x3000, OP.bitwise_and)
+            tt(a(s, 0, 32), a(n, 64, 96), a("KI"), OP.is_equal)
+            ts(a(n, 96, 104), a(n, 0, 32, 4), 13, OP.logical_shift_right, 0x1C0, OP.bitwise_and)
+            tt(a2("SM" + h, 0, 4), a3(MC, 0, 4), a(s, 0, 32), OP.mult)
+            tt(a2("JQ" + h, 0, 1), a(n, 96, 104), a("TT" + h), OP.add)
+            ts(a3("M" + h, 1, 4), a3(MC, 1, 4), 4096.0, OP.min)
+            rows(h, ["SM", "JQ", "M"])
+            ts(a("YO" + h), a(n, 32, 64), (1 << 22) - 1, OP.bitwise_and)
+            prev = a(BB)
+            for rk in range(2, DEPTH[e] + 2):
+                out = a("RK" + h, 160 * (rk - 2), 160 * (rk - 1))
+                scan(out, a(E, rk - 1, rk + 159), prev, 0.0, OP.max, OP.min)
+                prev = out
+            if e >= 4:
+                ts(a(s, 96, 104), a(BB, 19, 160, 20), 4.0 * LV, OP.is_ge, 4.5 * LV, OP.mult)
+            return
+        ts(a("FU" + h), ind(a(BB), a("LI", 2, 10)), 4.0 * LV, OP.is_ge)
+        ts(a(s, 0, 32), a3(MC, 1, 5), 4096.0, OP.min)
+        ts(a(s, 32, 64), a3(MC, 1, 5), 4096.0, OP.is_ge, -4097.0, OP.mult)
+        tt(a3("M" + h, 1, 5), a(s, 0, 32), a(s, 32, 64), OP.add)
+        o = 128 * int(h)
+        mm(a(MBS[int(h)], 0, 128), ("M" + h, (ALL,)), a("IH"))
+        act(a("MX", o, o + 128), a(MBS[int(h)], 0, 128))
+        if rnd == 0:
+            ts(a3("VA" + h, 0, 5), a3(MC, 0, 5), 4096.0, OP.is_lt)
+            tt(a(s, 64, 104), a3("VA" + h, 0, 5), a3("VA" + h, 1, 6), OP.subtract)
+            tt(a2("SM" + h, 0, 5), a3("M" + h, 0, 5), a(s, 64, 104), OP.mult)
+            rows(h, ["SM"])
+
+    def commit(rnd):
+        z = str(rnd)
+        MB, RB, LB, PP = EB[0], EB[1], MBS[0], MBS[1]
+        mm(a(MB, 0, 128), a("FU0"), a("UT"))
+        mm(a(MB, 128, 256), a("FU0"), a("ON"), True, False)
+        mm(a(MB, 128, 256), a("FU1"), a("UT"), False, True)
+        for c in range(3):
+            act(a("SG"), a(MB, 0, 256), AF.Sign, bias=col("cf", 40 + c), scale=-1.0, accum_out=col("AC", c))
+        ts(a("LN", 0, 3), a("AC", 0, 3), 0.5, OP.mult, 128.0, OP.add)
+        cp(a("MS"), ind(a("MX"), a("LN", 0, 3)))
+        if rnd == 1:
+            for j in range(5):
+                dma("Y", ("ym", (ALL, slice(256 * j, 256 * j + 256))), ("MX", (slice(j, 128, 16), slice(0, 256))), 2500)
+        for j in range(5):
+            mm(a(RB, 48 * j, 48 * j + 48), a("SEL", 128 * j, 128 * j + 128), a("MS"))
+        cp(a("BR", 0, 240), a(RB, 0, 240))
+        to_list(LB, "BR", 0, 240, 0)
+        ts(a("LF", 0, 15), a(LB, 0, 15), 0.0625, OP.mult)
+        for j in range(5):
+            mm(a(WP[0], 48 * j, 48 * j + 48), a("SEL", 640, 768), a("MS"))
+        act(a("BR", 240, 480), a(WP[0], 0, 240))
+        to_list(WP[1], "BR", 240, 480, 0)
+        act(a("LF", 16, 31), a(WP[1], 0, 15), AF.Identity, scale=0.0625)
+        for c in range(15):
+            ts(a("EW", 240 * c, 240 * c + 240), a("BR", 0, 240), col("LF", c), OP.is_equal, col("cf", 44 + c % 3), OP.mult)
+            mm(a(PP, 0, 240), a("BD"), a("EW", 240 * c, 240 * c + 240), c == 0, c == 14)
+        cp(a("LU", 0, 15), a("LF", 0, 15))
+        tt(a("DD", 16, 31), a("LF", 16, 31), a("CJ", 0, 15), OP.add)
+        cp(a("LU", 16, 31), a("DD", 16, 31))
+        act(a("CG"), ind(a("CH"), a("LU", 16, 31)))
+        tt(a("XT"), ind(a("X", 0, 2048), a("LU", 0, 15)), a("CG"), OP.add)
+        ts(a("XN"), a("XT"), 255, OP.bitwise_and)
+        tt(a("LF", 0, 15), a("LF", 0, 15), a("JJ", 0, 15), OP.subtract)
+        tt(a("ZM", 0, 96), a("XN", 0, 96), a("XN", 96, 192), OP.max)
+        tt(a("ZM", 96, 144), a("ZM", 0, 48), a("ZM", 48, 96), OP.max)
+        tt(a("ZM", 144, 192), a("ZM", 96, 144), a("XN", 192, 240), OP.max)
+        if rnd == 0:
+            act(a("HG"), ind(a("SW"), a("LU", 16, 19)))
+            cp(a("NG"), ind(a("NB", 0, 2048), a("LU", 0, 12)))
+            for p in range(2):
+                x0, x1 = a("NG", 96 * p, 96 * p + 48), a("NG", 96 * p + 48, 96 * p + 96)
+                d0, d1 = a("ND", 96 * p, 96 * p + 48), a("ND", 96 * p + 48, 96 * p + 96)
+                tt(d0, x1, x0, OP.subtract)
+                tt(d1, d0, a("HG"), OP.mult)
+                tt(x0, x0, d1, OP.add)
+                tt(x1, x1, d1, OP.subtract)
+        tt(a("OK"), a(PP, 0, 240), a("THR"), OP.is_lt)
+        tt(a("GO", 0, 96), a("OK", 0, 96), a("OK", 96, 192), OP.min)
+        tt(a("GO", 96, 144), a("GO", 0, 48), a("GO", 48, 96), OP.min)
+        tt(a("GO", 144, 192), a("GO", 96, 144), a("OK", 192, 240), OP.min)
+        to_list(LB, "GO", 144, 192, 32)
+        for m in range(3):
+            tt(a("ZS" + z, 16 * m, 16 * m + 16), a("ZM", 144 + m, 192, 3), a("GO", 144 + m, 192, 3), OP.mult)
+        rec("G", "send", (rnd,), [], [a("ZS" + z)], 1500)
+        for c in range(3):
+            ts(a("DD", c, 15, 3), a("LF", c, 15, 3), col(LB, 32 + c), OP.mult, 0.0625, OP.mult)
+        tt(a("DD", 16, 31), a("DD", 0, 15), a("JJ", 0, 15), OP.add)
+        cp(a("OF", 0, 15), a("DD", 16, 31))
+        cp(ind(a("X"), a("OF", 0, 15)), a("XN"))
+        if rnd == 0:
+            cp(ind(a("NB"), a("OF", 0, 12)), a("NG"))
+        rec("R", "arrive", (rnd,), [a("LD" + z)], [a("ZS" + z)], 0)
+        ops[-1]["sem"] = "arr" + z
+        ops[-1]["lat"] = 5000
+        if rnd == 1:
+            dma("Y", ("yx", (ALL, ALL)), a("X", 0, 512), 2500)
+            act(a("YZ"), ind(a("LD1"), a("LI", 10, 13)))
+            dma("S", ("yz", (ALL, ALL)), a("YZ"), 2500)
+
+    def new_lanes(h):
+        n, MC, LB = "n" + h, "MC" + h, PPS[int(h)]
+        act(a("XG" + h), ind(a("X", 0, 2048), a("L" + h, 0, 8)))
+        if h == "0":
+            act(a("XG0", 0, 48), ind(a("LD0"), a("LI", 10, 13)))
+        mm(a(LB, 64, 72), a("XG" + h), a("WD"))
+
+        def k(c):
+            return a(n, 8 * c, 8 * c + 8)
+        lane = col("cf", 35 if h == "1" else 0)
+        cp(k(0), a(LB, 64, 72))
+        ts(k(1), k(0), 4095, OP.bitwise_and)
+        tt(k(2), k(1), k(1), OP.mult)
+        ts(k(3), k(1), 37.0, OP.mult, lane, OP.add)
+        ts(k(4), k(2), 5, OP.logical_shift_right)
+        ts(a3(MC, 0, 1), k(3), 2047, OP.bitwise_and)
+        ts(k(5), k(4), lane, OP.add)
+        ms(a2("SM" + h, 1, 5), 0.0)
+        cp(a2("SM" + h, 0, 1), a3(MC, 0, 1))
+        ts(a("TT" + h), k(5), 63, OP.bitwise_and)
+        cp(a3("M" + h, 0, 1), a3(MC, 0, 1))
+        ts(a2("JQ" + h, 0, 1), a("TT" + h), 256.0, OP.add)
+        rows(h, ["SM", "JQ", "M"])
+        cp(a3("M" + h, 5, 6), a("TT" + h))
+
+    for h in "01":
+        to_list(PPS[int(h)], "RW" + h, 0, 256, 0)
+        cp(a("L" + h), a(PPS[int(h)], 0, 16))
+    for h in "01":
+        RB = EB[int(h)]
+        mm(a(RB, 0, 8), a("RW" + h, 0, 128), a("S0"))
+        mm(a(RB, 8, 16), a("RW" + h, 128, 256), a("S0"))
+        cp(a3("MC" + h, 0, 1), a(RB, 0, 8))
+        cp(a3("M" + h, 0, 1), a(RB, 0, 8))
+        ts(a("TT" + h), a(RB, 8, 16), -256.0, OP.add)
+        ts(a3("M" + h, 5, 6), a(RB, 8, 16), -256.0, OP.add)
+    for rnd in range(2):
+        order = "01" if rnd == 0 else "10"
+        for h in order:
+            if rnd:
+                new_lanes(h)
+            ms(a("YO" + h), 1 << 21)
+            prep(h, 1)
+        for e in range(1, 7):
+            for h in order:
+                heavy(h)
+                post(h, e, rnd)
+                if e < 6:
+                    prep(h, e + 1)
+            if rnd == 0 and e == 1:
+                late_constants()
+        commit(rnd)
+    return ops
+
+
+def plan():
+    ops = program()
+    hist = {}
+    prevg = []
+    for k, o in enumerate(ops):
+        deps = {}
+        acc = [(_span(p), True) for p in o["outs"]] + [(_span(p), False) for p in o["ins"]]
+        for (n, lo, hi, c), wr in acc:
+            ps = SCRATCH[n][0] == "psum"
+            for (j, l2, h2, w2) in hist.get(n, []):
+                same = ops[j]["eng"] == o["eng"]
+                if ps:
+                    if same and o["eng"] == "P":
+                        deps.setdefault(j, False)
+                    elif not same or ((wr or w2) and lo <= h2 and l2 <= hi):
+                        deps[j] = True
+                elif (wr or w2) and lo <= h2 and l2 <= hi:
+                    deps[j] = True
+        for (n, lo, hi, c), wr in acc:
+            old = hist.get(n, [])
+            if SCRATCH[n][0] == "psum":
+                old = [] if o["eng"] == "P" else [t for t in old if t[3] or ops[t[0]]["eng"] == o["eng"]]
+            elif wr and c == hi - lo + 1 and "sem" not in o:
+                old = [t for t in old if not (lo <= t[1] and t[2] <= hi)]
+            hist[n] = old + [(k, lo, hi, wr)]
+        if "stage" in o:
+            if prevg:
+                deps.setdefault(prevg[-1], False)
+            prevg.append(k)
+        deps.pop(k, None)
+        o["deps"] = deps
+    n = len(ops)
+    kids = [[] for _ in range(n)]
+    for k, o in enumerate(ops):
+        for j in o["deps"]:
+            kids[j].append(k)
+    prio = [0.0] * n
+    for k in range(n - 1, -1, -1):
+        o = ops[k]
+        prio[k] = o["cost"] + o.get("lat", 0) + max([prio[c] + (HOP if ops[c]["deps"][k] else 0) for c in kids[k]] + [0.0])
+    left = [len(o["deps"]) for o in ops]
+    ready = [0.0] * n
+    pool = {e: [] for e in "VSPGYR"}
+    free = {e: 0.0 for e in pool}
+    order = {e: [] for e in pool}
+    busy = {e: 0.0 for e in pool}
+    for k, o in enumerate(ops):
+        if left[k] == 0:
+            pool[o["eng"]].append(k)
+    end = 0.0
+    for _ in range(n):
+        best = None
+        for e in pool:
+            if pool[e]:
+                t0 = max(free[e], min(ready[k] for k in pool[e]))
+                k = max((k for k in pool[e] if ready[k] <= t0 + 30), key=lambda k: ("stage" not in ops[k], prio[k], -k))
+                if best is None or t0 < best[0]:
+                    best = (t0, e, k)
+        t0, e, k = best
+        o = ops[k]
+        o["t"] = max(free[e], ready[k])
+        free[e] = o["t"] + o["cost"]
+        busy[e] += o["cost"]
+        fin = free[e] + o.get("lat", 0)
+        end = max(end, fin)
+        pool[e].remove(k)
+        order[e].append(k)
+        for c in kids[k]:
+            lat = 0 if not ops[c]["deps"][k] else (SELF if ops[c]["eng"] == e and "sem" not in o else HOP)
+            ready[c] = max(ready[c], fin + lat)
+            left[c] -= 1
+            if left[c] == 0:
+                pool[ops[c]["eng"]].append(c)
+    pos = {}
+    for e in order:
+        for p, k in enumerate(order[e]):
+            pos[k] = p
+    need = set()
+    for e in "VSPGY":
+        seen = {}
+        for k in order[e]:
+            last = {}
+            for j, hard in ops[k]["deps"].items():
+                if hard:
+                    key = ops[j].get("sem", ops[j]["eng"])
+                    if pos[j] > seen.get(key, -1) and pos[j] > pos.get(last.get(key), -1):
+                        last[key] = j
+            for key in last:
+                seen[key] = pos[last[key]]
+                need.add(last[key])
+            ops[k]["waits"] = list(last.values())
+    total = {}
+    for e in "VSPG":
+        c = 0
+        for k in order[e]:
+            if k in need and "sem" not in ops[k]:
+                c += 1
+                ops[k]["mark"] = c
+        total["c" + e] = c
+    return ops, order, total, end, busy
+
+
+PLAN = []
+
+
+def rank_program(g, core, T, topo):
+    rank = T.rank_of(core)
+    if rank is None:
+        return
+    if not PLAN:
+        PLAN.append(plan())
+    ops, order, total, end, busy = PLAN[0]
+    n = len(T.cores)
+    peers = [T.cores[(rank + 1 + m) % n] for m in range(n - 1)]
+    per = 2
+
+    def real(x):
+        if not isinstance(x, tuple):
+            return x
+        if x[0] == "*":
+            return real(x[1]).indirect(real(x[2]))
+        return T[x[0]][x[1]]
+
+    queue = {"V": g.vector, "S": g.scalar, "P": g.tensor, "G": g, "Y": g.sync}
+    for e in "YGVSP":
+        q = queue[e]
+        for k in order[e]:
+            o = ops[k]
+            for j in o["waits"]:
+                p = ops[j]
+                if p["eng"] == "R":
+                    q.wait_ge(T.sem[p["sem"]], per * (n - 1))
+                elif "sem" in p:
+                    q.wait_ge(T.sem[p["sem"]], 16)
+                else:
+                    q.wait_ge(T.sem["c" + p["eng"]], p["mark"])
+            c, args = o["call"], [real(x) for x in o["args"]]
+            kw = {key: real(v) for key, v in o["kw"].items()}
+            if c == "send":
+                z = str(args[0])
+                tr = []
+                for m, d in enumerate(peers):
+                    rid, pid = topo.addr(d, core)
+                    eng = topo.engines(core, d)[per * m:per * m + per]
+                    tr.append(RemoteDMATransfer(dst_ids=[DstId(rid=rid, pnc=pid)], dma_engine_mask=sum(1 << x for x in eng),
+                                                remote_sem=T.sem["arr" + z], src=T["ZS" + z][:, 16 * m:16 * m + 16],
+                                                dst=T["LD" + z][:, 16 * m:16 * m + 16]))
+                g.remote_dma_fused(tr, local_sem=T.sem.sent)
+                continue
+            if c == "dma_start":
+                q.dma_start(*args).then_inc(T.sem[o["sem"]], 16)
+                continue
+            f = {"tensor_copy": lambda: q.tensor_copy(*args), "tensor_tensor": lambda: q.tensor_tensor(*args),
+                 "tensor_scalar": lambda: q.tensor_scalar(*args), "memset": lambda: q.memset(*args),
+                 "tensor_tensor_scan": lambda: q.tensor_tensor_scan(*args), "activation": lambda: q.activation(*args, **kw),
+                 "matmul": lambda: q.matmul(*args), "iota": lambda: q.iota(*args, **kw),
+                 "affine_select": lambda: q.affine_select(*args)}[c]()
+            if "mark" in o:
+                f.then_inc(T.sem["c" + e], 1)
+    for o in ops:
+        if o["call"] == "dma_start":
+            g.wait_ge(T.sem[o["sem"]], 16)
+    for s in total:
+        if total[s]:
+            g.wait_ge(T.sem[s], total[s])
+    g.wait_ge(T.sem.sent, 2 * per * (n - 1))

@@ -1,3 +1,4 @@
+import numpy as np
 from concourse.bass import DstId, RemoteDMATransfer
 from concourse.mybir import AluOpType as OP, ActivationFunctionType as AF
 
@@ -5,8 +6,11 @@ F, H, B, I, U = "float32", "float16", "bfloat16", "int32", "uint16"
 LV = 1 << 19
 SC = float(1 << 22)
 DEPTH = {1: 4, 2: 3, 3: 3, 4: 2, 5: 1, 6: 0}
-GC, PE = 1.56, 0.6
-HOP, SELF = 140, 70
+RAMP = [float(1 << 32), float(1 << 24), float(1 << 16), 256.0, 1.0]
+GC, PE = 1.56, 0.5
+HOP, SELF = 240, 120
+CFG = {"scan": 0, "fix": 10, "rw": "S", "mw": "S", "pw": "S", "one": 1, "one1": 0, "g1": 2, "g6": 1, "gv": 0, "look": "V",
+       "wt": "SS", "th": "VVVV", "up": {"SG": -4000}}
 
 
 def _scratch():
@@ -14,38 +18,45 @@ def _scratch():
 
     def sb(n, dt, *sh):
         s[n] = ("sbuf", [128] + list(sh), dt)
-    sb("X", B, 2304); sb("NB", I, 2304); sb("WT", B, 512); sb("TH", B, 512); sb("CH", B, 320); sb("SW", B, 64)
-    sb("PA", I, 64); sb("PB", I, 64); sb("WI", I, 4); sb("BG", I, 256); sb("TA", I, 256)
-    sb("q1", I, 192); sb("q4", F, 64); sb("ci", I, 8); sb("cf", F, 64); sb("io1", F, 168); sb("io2", F, 160); sb("io3", F, 160)
-    sb("t1", F, 160); sb("t2", F, 160); sb("t3", F, 160); sb("own", F, 160); sb("r16", F, 16)
-    sb("IH", H, 128); sb("IB", B, 128); sb("BD", B, 128); sb("SEL", H, 768); sb("BIG", H, 288); sb("I2", H, 128)
-    sb("RI", H, 160); sb("RN", B, 168); sb("RS", B, 16); sb("REW", B, 168); sb("RET", B, 168); sb("RP", B, 160)
-    sb("KN", F, 32); sb("KL", F, 32); sb("KI", I, 32); sb("LI", U, 16); sb("UT", H, 128); sb("ON", H, 128)
-    sb("WD", B, 8); sb("S0", H, 8); sb("THR", F, 240); sb("JJ", F, 16); sb("CJ", F, 16); sb("pw", F, 48)
+    sb("X", B, 2304); sb("NB", I, 2304); sb("WT", B, 1920); sb("TH", B, 1920); sb("CH", B, 320); sb("SW", B, 64)
+    sb("PA", I, 64); sb("PB", I, 64); sb("WI", I, 4); sb("BG", I, 128)
+    sb("q1", I, 192); sb("q4", F, 64); sb("ci", I, 12); sb("cf", F, 80); sb("io", F, 200); sb("gi", B, 9, 20)
+    sb("t1", F, 160); sb("t2", F, 160); sb("t3", F, 160); sb("own", B, 9, 20); sb("r16", F, 16)
+    sb("IH", H, 128); sb("NI", H, 128); sb("BD", B, 128); sb("SEL", H, 768); sb("BIG", H, 288); sb("I2", H, 256); sb("IB", B, 128)
+    sb("RI", H, 160); sb("RN", B, 160); sb("RS", B, 16); sb("RET", B, 9, 20); sb("RP", B, 8, 20)
+    sb("KN", F, 32); sb("KL", F, 32); sb("KI", I, 32); sb("LI", U, 16); sb("UT", H, 256)
+    sb("WD", B, 8); sb("JJ", F, 16); sb("CJ", B, 240); sb("pw", F, 96); sb("RZ", B, 240)
     for h in "01":
-        sb("G" + h, B, 2048); sb("A" + h, B, 2048); sb("CU" + h, U, 128); sb("CF" + h, H, 128); sb("W" + h, B, 128)
+        sb("G" + h, B, 2208); sb("A" + h, B, 2208); sb("CU" + h, U, 128); sb("CB" + h, H, 128); sb("CF" + h, H, 128)
+        sb("W" + h, B, 128)
         sb("TG" + h, B, 128); sb("EQ" + h, B, 512); sb("P" + h, F, 160); sb("BB" + h, F, 160); sb("RK" + h, F, 640)
-        sb("RW" + h, H, 384); sb("L" + h, U, 16); sb("SM" + h, H, 17, 8); sb("JQ" + h, H, 17, 8); sb("M" + h, H, 8, 16)
-        sb("FU" + h, H, 128); sb("MC" + h, I, 8, 5); sb("YO" + h, I, 32); sb("TT" + h, I, 8)
+        sb("RW" + h, H, 256); sb("L" + h, U, 16); sb("SM" + h, H, 17, 8); sb("JQ" + h, H, 17, 8); sb("M" + h, H, 8, 16)
+        sb("M2" + h, H, 8, 16)
+        sb("FU" + h, H, 128); sb("MC" + h, I, 8, 5); sb("YO" + h, I, 32)
         sb("s" + h, F, 160); sb("n" + h, I, 128); sb("VA" + h, F, 8, 6); sb("XG" + h, B, 128)
         sb("ZS" + h, B, 48); sb("LD" + h, B, 48)
-    sb("MX", F, 272); sb("SG", B, 256); sb("AC", F, 4); sb("LN", U, 4); sb("MS", H, 48); sb("BR", H, 480)
-    sb("LF", F, 32); sb("LU", U, 48); sb("DD", F, 32); sb("OF", U, 16); sb("EW", B, 3600); sb("OK", H, 240)
-    sb("GO", H, 192); sb("CG", B, 240); sb("XS", F, 128); sb("XT", I, 240); sb("XN", I, 240); sb("ZM", B, 192)
-    sb("NG", I, 192); sb("HG", F, 48); sb("ND", F, 192); sb("YZ", B, 48)
+    sb("MX", F, 272); sb("LN", U, 4); sb("MS", H, 48); sb("BR", H, 6, 80)
+    sb("LR", F, 64); sb("LU", U, 2, 16); sb("OF", U, 16); sb("EW", B, 15, 240)
+    sb("GO", H, 48); sb("CG", B, 240); sb("XT", I, 240); sb("XN", I, 240); sb("ZM", B, 144)
+    sb("NG", H, 192); sb("HG", F, 48); sb("DH", H, 96); sb("ND", I, 192); sb("ZZ", B, 96)
     for k in range(8):
         s["ps%d" % k] = ("psum", [128, 512], F)
     return s
 
 
 SCRATCH = _scratch()
-SEMAPHORES = ["cV", "cS", "cP", "cG", "sent", "arr0", "arr1"] + ["d%d" % k for k in range(20)]
+SEMAPHORES = ["cV", "cS", "cP", "cG", "sent", "arr0", "arr1"] + ["d%d" % k for k in range(24)]
 ALL = slice(None)
 WP, EB, PPS, MBS = ("ps0", "ps1"), ("ps2", "ps3"), ("ps4", "ps5"), ("ps6", "ps7")
+EE = (WP, EB)
 
 
 def a(n, lo=None, hi=None, st=None):
     return (n, (ALL, slice(lo, hi, st)))
+
+
+def ax(n, *ix):
+    return (n, (ALL,) + tuple(slice(*i) if isinstance(i, tuple) else i for i in ix))
 
 
 def a3(n, lo, hi):
@@ -64,22 +75,29 @@ def ind(win, off):
     return ("*", win, off)
 
 
+_SPANS = {}
+
+
 def _span(ap):
-    n, ix = ap
-    sh = SCRATCH[n][1]
-    lo = hi = 0
-    cnt = 1
-    for d in range(1, len(sh)):
-        r = range(sh[d])[ix[d]] if d < len(ix) else range(sh[d])
-        lo = lo * sh[d] + r[0]
-        hi = hi * sh[d] + r[-1]
-        cnt *= len(r)
-    return n, lo, hi, cnt
+    key = repr(ap)
+    if key not in _SPANS:
+        n, ix = ap
+        sh = SCRATCH[n][1][1:]
+        el = np.arange(int(np.prod(sh))).reshape(sh)[tuple(ix[1:])].reshape(-1)
+        bits = 0
+        for e in el.tolist():
+            bits |= 1 << e
+        if SCRATCH[n][0] == "sbuf":
+            bits = bits << 4096 if ix[0].start else bits if ix[0].stop == 16 else bits | bits << 4096
+        _SPANS[key] = (n, bits, len(el))
+    return _SPANS[key]
 
 
 def program():
     ops = []
+    SCAN = CFG["scan"]
     nd = [0]
+    fix = CFG["fix"]
 
     def rec(eng, call, args, outs, ins, cost, **kw):
         ops.append(dict(eng=eng, call=call, args=args, outs=outs, ins=ins, cost=cost, kw=kw))
@@ -88,7 +106,7 @@ def program():
         return [ap[1], ap[2]] if ap[0] == "*" else [ap]
 
     def cnt(ap):
-        return 16 * _span(ap[2])[3] if ap[0] == "*" else _span(ap)[3]
+        return 16 * _span(ap[2])[2] if ap[0] == "*" else _span(ap)[2]
 
     def two(*aps):
         return all(p[0] != "*" and SCRATCH[p[0]][2] in (H, B, U) for p in aps)
@@ -98,7 +116,7 @@ def program():
             return 60 + 3.5 * cnt(out)
         if src[0] == "*":
             return 60 + GC * cnt(src)
-        return max(64, m * cnt(src)) + 10
+        return max(64, m * cnt(src)) + fix
 
     def sides(out, *srcs):
         o = parts(out)
@@ -118,7 +136,8 @@ def program():
             vcost(out, x, 0.5 if two(out, x) else 1))
 
     def scan(out, d0, d1, init, op0, op1):
-        rec("V", "tensor_tensor_scan", (out, d0, d1, init, op0, op1), [out], [d0, d1], vcost(out, d0, 1))
+        rec("V", "tensor_tensor_scan", (out, d0, d1, init, op0, op1), [out], [d0, d1] + [init] * isinstance(init, tuple),
+            vcost(out, d0, 0.5 if two(out, d0, d1) else 1))
 
     def ms(out, v):
         rec("V", "memset", (out, v), [out], [], max(64, cnt(out) * (0.5 if two(out) else 1)))
@@ -127,10 +146,13 @@ def program():
         o, i = sides(out, src, *[kw[k] for k in kw if k != "accum_out"])
         if "accum_out" in kw:
             o = o + [kw["accum_out"]]
-        rec("S", "activation", (out, src, f), o, i, 78 + GC * cnt(src) if src[0] == "*" else max(64, cnt(src)) + 10, **kw)
+        rec("S", "activation", (out, src, f), o, i, 78 + GC * cnt(src) if src[0] == "*" else max(64, cnt(src)) + fix, **kw)
+
+    def mov(eng, out, src):
+        (cp if eng == "V" else act)(out, src)
 
     def mm(out, l, r, st=True, sp=True):
-        rec("P", "matmul", (out, l, r, st, sp), [out], [l, r], PE * max(64, cnt(r)))
+        rec("P", "matmul", (out, l, r, st, sp), [out], [l, r], PE * max(min(64, cnt(l)), cnt(r)))
 
     def iota(out, pat, base=0, cm=0):
         kw = {} if SCRATCH[out[0]][2] == I else {"allow_small_or_imprecise_dtypes": True}
@@ -145,52 +167,47 @@ def program():
         ops[-1]["lat"] = cost
         nd[0] += 1
 
-    row0 = (slice(0, 128, 16), ALL)
-    ms(a("BG"), 0); ms(a("TA"), 0); ms(a("PB"), 0)
+    ms(a("PB"), 0)
     dma("Y", a("NB", 0, 2048), ("nb", (ALL, ALL)), 6000)
-    dma("Y", ("BG", row0), ("beg", (ALL, ALL)), 2600)
-    dma("Y", ("TA", row0), ("tau", (ALL, ALL)), 2600)
+    dma("Y", ("BG", (slice(0, 16), ALL)), ("beg", (ALL, ALL)), 2600)
+    dma("Y", ("BG", (slice(16, 32), ALL)), ("tau", (ALL, ALL)), 2600)
     dma("S", a("X", 0, 2048), ("x", (ALL, ALL)), 6200)
     dma("S", a("PA"), ("par", (ALL, ALL)), 2800)
     dma("Y", ("PB", (slice(0, 124), ALL)), ("par", (slice(4, 128), ALL)), 2800)
-    dma("S", a("WT", 256, 320), ("feat", (ALL, slice(0, 64))), 3000)
-    dma("S", a("WT", 0, 192), ("feat", (ALL, slice(64, 256))), 3000)
+    dma("S", a("EQ1", 320, 384), ("feat", (ALL, slice(0, 64))), 3000)
+    dma("S", a("EQ1", 64, 256), ("feat", (ALL, slice(64, 256))), 3000)
     dma("Y", a("CH"), ("chg", (ALL, ALL)), 7000)
-    dma("Y", a("SW"), ("swp", (ALL, ALL)), 7000)
+    dma("Y", a("SW", 0, 64), ("swp", (ALL, ALL)), 7000)
     dma("Y", col("WI", 0), ("wt", (ALL, ALL)), 7000)
 
-    iota(col("ci", 4), [[0, 1]], 0, 1)
-    iota(a("io1"), [[1, 168]])
-    iota(a("t1", 0, 128), [[1, 8], [0, 16]])
-    iota(a("io2"), [[1, 8], [0, 20]])
-    iota(a("io3"), [[0, 8], [1, 20]])
+    def io(lo, hi, st=None):
+        return a("io", 32 + lo, 32 + hi, st)
+    iota(col("ci", 0), [[0, 1]], 0, 1)
+    iota(a("io"), [[1, 200]], -32)
+    iota(a("RK0", 0, 128), [[8, 2], [16, 8], [1, 8]])
+    iota(a("t1", 0, 128), [[16, 8], [0, 16]])
+    iota(("gi", (ALL,)), [[16, 9], [0, 20]])
     iota(a("KN"), [[0, 8], [LV // 32, 4]], LV // 32)
     iota(a("KI"), [[0, 8], [4096, 4]])
-    iota(a("XS"), [[8, 2], [16, 8], [1, 8]])
-    ts(col("ci", 0), col("ci", 4), 15, OP.bitwise_and)
-    ts(col("ci", 1), col("ci", 4), 4, OP.logical_shift_right)
-    ts(col("ci", 2), col("ci", 4), 12, OP.bitwise_and)
-    cp(col("cf", 0), col("ci", 4))
-    cp(a("cf", 1, 4), a("ci", 0, 3))
+    for c, m in enumerate((15, 112, 12, 120)):
+        ts(col("ci", 1 + c), col("ci", 0), m, OP.bitwise_and)
+    cp(a("cf", 0, 5), a("ci", 0, 5))
     pp, rr, pg = col("cf", 0), col("cf", 1), col("cf", 2)
-    ts(col("cf", 4), pg, 16.0, OP.mult, 15.0, OP.add)
-    ts(a("BIG", 0, 144), a("io1", 0, 144), col("cf", 4), OP.is_equal)
-    ts(col("cf", 38), rr, 7.5, OP.is_lt, -8.0, OP.mult)
-    ts(col("cf", 39), col("cf", 38), col("cf", 4), OP.add)
-    ts(a("BIG", 144, 288), a("io1", 0, 144), col("cf", 39), OP.is_equal)
-    ts(a("I2"), a("XS"), pp, OP.is_equal)
-    ts(a("r16"), a("io1", 0, 16), rr, OP.is_equal)
+    ts(a("BIG", 144, 288), io(-7, 137), col("cf", 4), OP.is_equal)
+    ts(a("I2", 0, 128), a("RK0", 0, 128), pp, OP.is_equal)
+    ts(a("r16"), io(0, 16), rr, OP.is_equal)
 
     def r(k):
         return col("r16", k)
-    ts(col("cf", 5), r(0), 256.0, OP.mult)
-    for h in range(2):
-        rw = "RW%d" % h
-        cp(a(rw, 0, 128), a("BG", 128 * h, 128 * h + 128))
-        ts(a(rw, 128, 256), a("TA", 128 * h, 128 * h + 128), col("cf", 5), OP.add)
-        act(a(rw, 256, 384), a(rw, 0, 128))
-    ts(a("IB"), a("io1", 0, 128), pp, OP.is_equal)
-    act(a("IH"), a("IB"))
+    ts(a("IH"), io(0, 128), pp, OP.is_equal)
+    if SCAN:
+        ts(col("ci", 9), pp, -2.0, OP.add, 0.2, OP.mult)
+        act(col("cf", 62), col("ci", 9), AF.Identity, scale=-5.0, bias=pp)
+        ts(col("cf", 63), col("cf", 62), 4.0, OP.is_equal)
+        act(col("cf", 68), col("ci", 9))
+        act(col("cf", 69), col("cf", 62), AF.Identity, scale=26.0, bias=col("cf", 68))
+        tt(col("cf", 70), col("cf", 69), col("cf", 63), OP.subtract)
+        ts(a("I2", 128, 256), a("RK0", 0, 128), col("cf", 70), OP.is_equal)
     ts(a("BD"), a("t1", 0, 128), pg, OP.is_equal)
     for i in range(6):
         act(a("SEL", 128 * i, 128 * i + 128), a("BD"), AF.Identity, scale=r(i))
@@ -199,143 +216,214 @@ def program():
     ts(a("q1", 128, 192), a("PA"), 3, OP.bitwise_and)
     ts(col("cf", 6), rr, 4.5, OP.is_lt)
     ts(col("cf", 7), rr, 4.5, OP.is_gt)
-    ts(a("q4"), a("q1", 128, 192), col("cf", 6), OP.mult)
-    ts(a("s0", 0, 64), a("q1", 64, 128), col("cf", 7), OP.mult)
+    act(a("q4"), a("q1", 128, 192), AF.Identity, scale=col("cf", 6))
+    act(a("s0", 0, 64), a("q1", 64, 128), AF.Identity, scale=col("cf", 7))
     tt(a("s0", 64, 128), a("q4"), a("q1", 0, 64), OP.add)
     tt(a("q4"), a("s0", 64, 128), a("s0", 0, 64), OP.add)
     tt(a("cf", 24, 28), a("r16", 5, 9), a("r16", 9, 13), OP.add)
-    cp(col("cf", 12), col("cf", 27))
+    act(col("cf", 12), col("cf", 27))
     tt(a("cf", 9, 12), a("cf", 24, 27), a("r16", 2, 5), OP.add)
-    ts(a("cf", 16, 24), a("io1", 2, 10), r(13), OP.mult, r(14), OP.add)
-    ts(col("cf", 20), r(13), r(14), OP.add)
-    ts(col("cf", 28), r(15), -16384.0, OP.mult)
-    ts(a("cf", 19, 24, 4), a("cf", 19, 24, 4), col("cf", 28), OP.add)
-    for b in range(8):
-        j = {0: 2, 1: 3, 2: 4, 4: 1}.get(b)
-        act(a("TH", 64 * b, 64 * b + 64), a("q4"), AF.Identity, scale=col("cf", 8 + j) if j else 0.0, bias=col("cf", 16 + b))
-    ms(a("WT", 192, 256), 0.0); ms(a("WT", 320, 512), 0.0)
-    ts(col("cf", 13), pg, 20.0, OP.mult, 19.0, OP.add)
-    tt(col("cf", 29), col("cf", 13), rr, OP.subtract)
-    ts(a("RI"), a("io1", 0, 160), col("cf", 29), OP.is_equal)
-    ts(a("RN"), a("io1"), col("cf", 29), OP.is_equal, -SC * 8192, OP.mult)
-    ts(a("RS", 0, 8), a("io1", 0, 8), pg, OP.is_equal, SC, OP.mult)
-    ts(a("RS", 8, 16), a("io1", 0, 8), pg, OP.is_equal, -2 * SC, OP.mult)
-    ts(a("S0"), a("io1", 0, 8), pg, OP.is_equal, r(0), OP.mult)
-    ms(a("REW", 160, 168), 0.0); ms(a("RET", 160, 168), 0.0)
-    ts(a("own"), a("io2"), pg, OP.is_equal)
-    ts(a("t2"), a("io3"), 3.5, OP.is_gt, SC, OP.mult)
-    tt(a("REW", 0, 160), a("t2"), a("own"), OP.mult)
-    ts(col("cf", 30), rr, 13.0, OP.not_equal, col("cf", 7), OP.mult)
-    ts(col("cf", 31), r(14), SC, OP.mult)
-    act(a("s1"), a("REW", 0, 160), AF.Identity, scale=col("cf", 30))
-    act(a("t3"), a("own"), AF.Identity, scale=col("cf", 31))
-    tt(a("RET", 0, 160), a("s1"), a("t3"), OP.max)
-    ts(col("cf", 32), col("cf", 6), 4096.0 / SC, OP.mult)
-    ts(col("cf", 33), r(13), LV / SC, OP.mult, col("cf", 32), OP.add)
-    ts(a("t2"), a("io3"), -4.0, OP.add, 0.0, OP.max)
-    ts(a("t3"), a("own"), r(14), OP.mult, 16384.0, OP.mult)
-    tt(a("t1"), a("t2"), a("t3"), OP.mult)
-    act(a("io2"), a("REW", 0, 160), AF.Identity, scale=col("cf", 33))
-    tt(a("RP"), a("t1"), a("io2"), OP.add)
+    ts(col("cf", 5), r(14), r(0), OP.add)
+    act(a("cf", 16, 21), io(1, 6), AF.Identity, scale=r(13), bias=col("cf", 5))
+    act(col("cf", 21), col("cf", 16))
+    act(col("cf", 28), r(15), AF.Identity, scale=-16384.0, bias=col("cf", 20))
+    for b in (5, 1, 2, 3, 0, 4):
+        j = {1: 2, 2: 3, 3: 4, 5: 1}.get(b)
+        act(a("TH", 64 * b, 64 * b + 64), a("q4"), AF.Identity, scale=col("cf", 8 + j) if j else 0.0,
+            bias=col("cf", 16 + b if j else 28))
+    ms(a("EQ1", 0, 64), 0.0); ms(a("EQ1", 256, 320), 0.0)
+    for m in (4, 0, 1, 2, 3)[:1 + 4 * SCAN]:
+        ts(a("WT", 384 * m, 384 * m + 384), a("EQ1", 0, 384), 1.0 * SCAN, OP.add, RAMP[m], OP.mult)
+    e0, e1 = a("EQ0", 0, 384), a("EQ1", 0, 384)
+    mm(a(WP[0], 0, 384), a("BD"), a("WT", 1536, 1920))
+    act(e0, a(WP[0], 0, 384))
+    tt(e1, a(WP[0], 0, 384), e0, OP.subtract)
+    act(a("IB"), a("IH"))
+    act(a("TG0"), a("IH"), AF.Identity, scale=r(1))
+    act(a("TG1"), a("IH"), AF.Identity, scale=r(0))
+    for i, (d, x) in enumerate((("IB", a("TH", 0, 384)), ("TG0", e0), ("TG1", e1))):
+        mm(a(WP[1], 0, 384), a(d), x, i == 0, i == 2)
+    ts(col("cf", 29), pg, 1.25, OP.mult, rr, OP.subtract)
+    ts(a("RI"), io(-19, 141), col("cf", 29), OP.is_equal)
+    act(a("RN", 0, 160), a("RI"), AF.Identity, scale=-float(1 << 72))
+    ts(a("RS", 0, 8), io(0, 128, 16), pg, OP.is_equal, SC, OP.mult)
+    act(a("RS", 8, 16), a("RS", 0, 8), AF.Identity, scale=-2.0)
+    ts(("own", (ALL,)), ("gi", (ALL,)), pg, OP.is_equal)
+    ts(col("cf", 30), col("cf", 7), r(13), OP.subtract, r(14), OP.subtract)
+    ts(col("cf", 15), r(0), r(1), OP.add)
+    ts(col("cf", 22), col("cf", 30), col("cf", 15), OP.add)
+    ts(a3("RET", 0, 4), a3("own", 0, 4), col("cf", 15), OP.mult, SC, OP.mult)
+    ts(a3("RET", 4, 20), a3("own", 4, 20), col("cf", 22), OP.mult, SC, OP.mult)
+    ts(col("cf", 32), col("cf", 6), col("cf", 15), OP.subtract, 4096.0, OP.mult)
+    act(col("cf", 33), r(13), AF.Identity, scale=float(LV), bias=col("cf", 32))
+    act(col("cf", 31), r(14), AF.Identity, scale=16384.0)
+    iota(a("t2", 0, 128), [[0, 8], [1, 16]])
+    act(a("t3", 0, 128), a("t2", 0, 128), AF.Identity, scale=col("cf", 31), bias=col("cf", 33))
+    ms(ax("RP", ALL, (0, 4)), 0.0)
+    tt(ax("RP", ALL, (4, 20)), a("t3", 0, 128), ax("own", (0, 8), (4, 20)), OP.mult)
     act(a("KN"), a("KN"), AF.Identity, scale=32.0)
-    ts(col("cf", 14), col("cf", 3), 5.0, OP.mult, 19.0, OP.add)
-    ts(a("LI", 0, 2), a("io1", 0, 2), 80.0, OP.mult, col("cf", 14), OP.add)
-    ts(a("LI", 2, 10), a("io1", 0, 8), 20.0, OP.mult, 19.0, OP.add)
+    act(col("cf", 14), col("cf", 3), AF.Identity, scale=5.0, bias=19.0)
+    ts(a("LI", 0, 2), io(0, 2), 80.0, OP.mult, col("cf", 14), OP.add)
+    act(a("TH", 1536, 1920), a(WP[1], 0, 384))
+    for m in range(4 * SCAN):
+        act(col("cf", 72 + m), col("cf", 22), AF.Identity, scale=RAMP[m] - 1.0, bias=1.0)
+        if CFG["th"][m] == "V":
+            ts(a("TH", 384 * m, 384 * m + 384), a("TH", 1536, 1920), col("cf", 72 + m), OP.mult)
+        else:
+            act(a("TH", 384 * m, 384 * m + 384), a("TH", 1536, 1920), AF.Identity, scale=col("cf", 72 + m))
+    if SCAN:
+        act(col("cf", 23), col("cf", 62), AF.Identity, scale=384.0)
     for h in "01":
         for n in ("SM", "JQ", "M"):
             ms((n + h, (ALL,)), 0.0)
 
     def late_constants():
+        ts(a("LI", 2, 10), io(0, 8), 20.0, OP.mult, 19.0, OP.add)
+        ts(a("BIG", 0, 144), io(-15, 129), pg, OP.is_equal, 0.0625, OP.mult)
+        act(a("NI"), a("IH"), AF.Identity, scale=-1.0)
         act(a("KL"), a("KN"))
-        ms(a("KL", 0, 32, 4), -SC)
-        ms(a("KL", 1, 32, 4), 2.5 * LV)
-        ms(("VA0", (ALL,)), 0.0); ms(("VA1", (ALL,)), 0.0)
-        ts(a("UT"), a("io1", 0, 128), pp, OP.is_ge)
-        ms(a("ON"), 1.0)
-        cp(col("cf", 34), col("WI", 0))
-        ts(a("WD"), a("io1", 0, 8), pg, OP.is_equal, col("cf", 34), OP.mult)
-        ts(col("cf", 35), pp, 128.0, OP.add)
-        ts(col("cf", 36), rr, 0.5, OP.add)
-        ts(a("cf", 40, 43), a("io1", 0, 3), 16.0, OP.mult, col("cf", 36), OP.add)
-        ms(a("t1", 0, 48), 0.25); ms(a("t2", 0, 48), 0.0)
-        scan(a("pw"), a("t1", 0, 48), a("t2", 0, 48), 4.0, OP.mult, OP.add)
-        for j in range(5):
-            act(a("THR", 48 * j, 48 * j + 48), a("pw"), AF.Identity, scale=2.0)
+        iota(a("KL", 0, 32, 4), [[0, 8]], -int(SC))
+        iota(a("KL", 1, 32, 4), [[0, 8]], 5 * LV // 2)
+        iota(("VA0", (ALL,)), [[0, 8], [0, 6]]); iota(("VA1", (ALL,)), [[0, 8], [0, 6]])
+        ms(("M20", (ALL,)), 0.0); ms(("M21", (ALL,)), 0.0)
+        ts(a("UT", 0, 128), io(0, 128), pp, OP.is_ge)
+        ms(a("UT", 128, 256), 1.0)
+        act(col("cf", 34), col("WI", 0), AF.Identity, scale=1.0 / SC)
+        act(a("WD"), a("RS", 0, 8), AF.Identity, scale=col("cf", 34))
+        iota(col("cf", 35), [[0, 1]], 128, 1)
+        iota(a("cf", 60, 62), [[4096, 2]], 0, 32)
+        act(col("cf", 36), rr, AF.Identity, bias=0.5)
+        act(a("cf", 40, 43), io(0, 3), AF.Identity, scale=16.0, bias=col("cf", 36))
+        iota(a("t2", 0, 48), [[0, 48]])
+        act(a("t1", 0, 48), a("t2", 0, 48), AF.Identity, bias=0.25)
+        scan(a("pw", 0, 48), a("t1", 0, 48), a("t2", 0, 48), 4.0, OP.mult, OP.add)
+        act(a("pw", 48, 96), a("pw", 0, 48), AF.Identity, scale=2.0)
         tt(a("t3", 0, 16), a("pw", 0, 16), a("r16"), OP.mult)
-        scan(a("t3", 16, 32), a("t3", 0, 16), a("t2", 0, 16), 0.0, OP.add, OP.add)
-        ts(a("cf", 44, 47), a("pw", 0, 48, 16), col("t3", 31), OP.mult)
-        ts(col("cf", 37), rr, 2048.0, OP.add)
-        ts(a("JJ"), a("io1", 0, 16), 16.0, OP.mult, col("cf", 37), OP.add)
-        iota(a("CJ", 0, 15), [[64, 5], [0, 3]])
-        ts(a("MX", 256, 272), a("io1", 0, 16), 0.0, OP.mult, col("cf", 6), OP.subtract)
-        ts(a("ci", 5, 8), a("cf", 40, 43), -1.5, OP.add, 1.0 / 3, OP.mult)
-        ts(a("cf", 48, 51), a("ci", 5, 8), -47.0, OP.mult, -8.0, OP.add)
-        ts(a("cf", 52, 55), a("cf", 40, 43), 16.0, OP.mult)
+        act(a("t3", 16, 32), a("t3", 0, 16), AF.Identity, accum_out=col("t3", 32))
+        act(a("cf", 44, 47), a("pw", 0, 48, 16), AF.Identity, scale=col("t3", 32))
+        act(col("cf", 37), rr, AF.Identity, bias=2048.0)
+        act(a("JJ"), io(0, 16), AF.Identity, scale=16.0, bias=col("cf", 37))
+        iota(a("CJ"), [[0, 48], [4, 5]])
+        iota(a("RZ"), [[0, 240]], 1)
+        iota(a("RZ", 0, 240, 5), [[0, 48]])
+        act(col("cf", 8), col("cf", 6), AF.Identity, scale=-1.0)
+        act(a("MX", 256, 272), io(0, 16), AF.Identity, scale=0.0, bias=col("cf", 8))
+        ts(a("ci", 6, 9), a("cf", 40, 43), -1.5, OP.add, 1.0 / 3, OP.mult)
+        act(a("cf", 48, 51), a("ci", 6, 9), AF.Identity, scale=-47.0, bias=-8.0)
+        act(a("cf", 52, 55), a("cf", 40, 43), AF.Identity, scale=16.0)
         tt(a("cf", 56, 59), a("cf", 48, 51), a("cf", 52, 55), OP.add)
         cp(a("LI", 10, 13), a("cf", 56, 59))
 
-    def to_list(bank, src, lo, hi, out_lo):
-        n = (hi - lo) // 16
-        for b in range(16):
-            mm(a(bank, out_lo, out_lo + n), a("BIG", 15 - b, 143 - b), a(src, lo + b, hi, 16), b == 0, b == 15)
+    def turn(bank, lo, name, o=0):
+        mm(a(bank, lo, lo + 64), (name, (ALL, slice(1, 17))), a("I2", o, o + 64), True, False)
+        mm(a(bank, lo, lo + 64), (name, (ALL, slice(0, 16))), a("I2", o + 64, o + 128), False, True)
 
-    def rows(h, names):
-        n = min(len(names), 2)
-        RB, LB = WP[int(h)], PPS[int(h)]
-        for q in range(n):
-            mm(a(RB, 64 * q, 64 * q + 64), (names[q] + h, (ALL, slice(1, 17))), a("I2", 0, 64), True, False)
-            mm(a(RB, 64 * q, 64 * q + 64), (names[q] + h, (ALL, slice(0, 16))), a("I2", 64, 128), False, True)
-        cp(a("RW" + h, 0, 64 * n), a(RB, 0, 64 * n))
+    def to_list(h, bank, lo, hi):
         for b in range(8):
-            mm(a(LB, 0, 8 * n), a("BIG", 151 - b, 279 - b), a("RW" + h, b, 64 * n, 8), b == 0, b == 7)
-        cp(a("L" + h, 0, 8 * n), a(LB, 0, 8 * n))
-        if len(names) > 2:
-            mm(a(MBS[int(h)], 0, 128), (names[2] + h, (ALL,)), a("IH"))
-            act(a("RW" + h, 256, 384), a(MBS[int(h)], 0, 128))
+            mm(a(bank, 256, 256 + hi - lo), a("BIG", 151 - b, 279 - b), a("RW" + h, 8 * lo + b, 8 * hi, 8), b == 0, b == 7)
+        cp(a("L" + h, lo, hi), a(bank, 256, 256 + hi - lo))
 
-    def prep(h, e):
-        E, Wp, PP, MB = EB[int(h)], WP[int(h)], PPS[int(h)], MBS[int(h)]
+    def rows(h, more=True, one=True):
+        RB, MB = PPS[int(h)], MBS[int(h)]
+        if more and one:
+            turn(RB, 64, "JQ" + h)
+            turn(RB, 0, "SM" + h, 128 * SCAN)
+            mov(CFG["rw"], a("RW" + h, 0, 128), a(RB, 0, 128))
+            to_list(h, RB, 0, 16)
+            mm(a(MB, 0, 128), ("M" + h, (ALL,)), a("IH"))
+            mov(CFG["mw"], a("RW" + h, 128, 256), a(MB, 0, 128))
+            return
+        turn(RB, 0, "SM" + h, 128 * SCAN if more else 0)
+        mov(CFG["rw"], a("RW" + h, 0, 64), a(RB, 0, 64))
+        to_list(h, RB, 0, 8)
+        if more:
+            turn(MB, 0, "JQ" + h)
+            mm(a(MB, 64, 192), ("M" + h, (ALL,)), a("IH"))
+            act(a("RW" + h, 64, 256), a(MB, 0, 192))
+            to_list(h, RB, 8, 16)
+
+    def prep(h, e, gv):
+        PP, MB, Wp = PPS[int(h)], MBS[int(h)], WP[int(h)]
         cp(a("CU" + h), ind(a("NB", 0, 2048), a("L" + h, 0, 8)))
-        act(a("W" + h), ind(a("WT"), a("L" + h, 8, 16)))
-        for q in range(4):
-            mm(a(Wp, q, 512, 4), a("IB"), a("W" + h))
-        for c in range(4):
-            act(a("G" + h, 512 * c, 512 * c + 512), ind(a("X", 0, 2048), a("CU" + h, 32 * c, 32 * c + 32)))
-            ops[-1]["stage"] = 1
-            if c == 0:
-                act(a("TG" + h), ind(a("TH"), a("L" + h, 8, 16)))
+        if not SCAN:
+            mov(CFG["wt"][0], a("W" + h), ind(a("WT", 1536, 1920), a("L" + h, 8, 16)))
+            for q in range(4):
+                mm(a(Wp, q, 512, 4), a("IB"), a("W" + h))
+            for c in range(4):
+                out, src = a("G" + h, 512 * c, 512 * c + 512), ind(a("X", 0, 2048), a("CU" + h, 32 * c, 32 * c + 32))
+                if c >= 4 - gv:
+                    cp(out, src)
+                else:
+                    act(out, src)
+                    ops[-1]["stage"] = 1
+            mov(CFG["wt"][1], a("TG" + h), ind(a("TH", 1536, 1920), a("L" + h, 8, 16)))
+            cp(a("CF" + h), a("CU" + h))
+        for m in range(5 * SCAN):
+            lo, n, at = ((0, 26, 80), (26, 26, 96), (52, 26, 112), (78, 25, 128), (102, 26, 64))[m]
+            nv = min(n, max(0, gv - 26 * (4 - m)))
+            if nv < n:
+                act(a("G" + h, at, at + 80 * (n - nv), 5), ind(a("X", 0, 2048), a("CU" + h, lo, lo + n - nv)),
+                    AF.Identity, scale=RAMP[m], bias=RAMP[m])
                 ops[-1]["stage"] = 1
-        cp(a("CF" + h), a("CU" + h))
+            if nv:
+                ts(a("G" + h, at + 80 * (n - nv), at + 80 * n, 5), ind(a("X", 0, 2048), a("CU" + h, lo + n - nv, lo + n)),
+                   RAMP[m], OP.mult, RAMP[m], OP.add)
+        if SCAN:
+            mov(CFG["wt"][0], a("W" + h), ind(a("WT"), a("L" + h, 8, 16)))
+            mov(CFG["wt"][1], a("TG" + h), ind(a("TH"), a("L" + h, 8, 16)))
+            for q in range(4):
+                mm(a(Wp, q, 104, 4), a("IB"), a("W" + h, 0, 128, 5))
+            cp(a("CB" + h), a("CU" + h))
+            for m, lo in enumerate((0, 26, 52, 78, 103)):
+                gcopy(a("CF" + h, m, 128, 5), a("CB" + h, lo, lo + (26 if m < 3 else 25)))
         ne = min(e, 4)
         for i in range(ne):
-            mm(a(MB, 128 * i, 128 * i + 128), a("SEL", 128 * i, 128 * i + 128), a("RW" + h, 256, 384))
+            mm(a(MB, 128 * i, 128 * i + 128), a("SEL", 128 * i, 128 * i + 128), a("RW" + h, 128, 256))
         for i in range(ne):
             tt(a("EQ" + h, 128 * i, 128 * i + 128), a("CF" + h), a(MB, 128 * i, 128 * i + 128), OP.is_equal)
         mm(a(PP, 0, 160), a("CF" + h), a("RI"), True, False)
         mm(a(PP, 0, 160), a("TG" + h), a("RP"), False, True)
-        act(a("P" + h), a(PP, 0, 160))
+        mov(CFG["pw"], a("P" + h), a(PP, 0, 160))
         for rk in range(2, DEPTH[e - 1] + 2 if e > 1 else 0):
             src = a("RK" + h, 160 * (rk - 2) + 20 - rk, 160 * (rk - 1), 20)
             if e > 4 and rk == 2:
                 tt(a("P" + h, 3, 160, 20), src, a("s" + h, 96, 104), OP.max)
             else:
                 gcopy(a("P" + h, 5 - rk, 160, 20), src)
-        mm(a(E, 0, 168), a("W" + h), a("REW"), True, False)
-        mm(a(E, 0, 168), a("TG" + h), a("RET"), False, False)
-        for i in range(ne):
-            mm(a(E, 0, 168), a("EQ" + h, 128 * i, 128 * i + 128), a("RN"), False, False)
 
-    def heavy(h):
+    def heavy(h, e):
         E, Wp = EB[int(h)], WP[int(h)]
-        for c in range(4):
+        k0 = len(ops)
+        mm(a(E, 0, 180), a("TG" + h), a("RET"), True, False)
+        for i in range(min(e, 4)):
+            mm(a(E, 0, 160), a("EQ" + h, 128 * i, 128 * i + 128), a("RN"), False, False)
+
+        def lanes(n, k):
+            return a(n + h, 80 + 5 * k, 80 + 5 * k + 2033, 16)
+        if not SCAN:
+            for c in range(4):
+                for m in range(4):
+                    tt(a("A" + h, 512 * m + 128 * c, 512 * m + 128 * c + 128), a("G" + h, 512 * c + m, 512 * c + 512, 4),
+                       a(Wp, 128 * c, 128 * c + 128), OP.max)
+            for k in range(16):
+                mm(a(E, 19 - k, 160, 20), a("G" + h, k, 2048, 16), a("RS", 0, 8), False, False)
             for m in range(4):
-                tt(a("A" + h, 512 * m + 128 * c, 512 * m + 128 * c + 128), a("G" + h, 512 * c + m, 512 * c + 512, 4),
-                   a(Wp, 128 * c, 128 * c + 128), OP.max)
-        for k in range(16):
-            mm(a(E, 19 - k, 160, 20), a("G" + h, k, 2048, 16), a("RS", 0, 8), False, False)
-        for m in range(4):
-            for q in range(4):
-                mm(a(E, 19 - m - 4 * q, 160, 20), a("A" + h, 512 * m + q, 512 * m + 512, 4), a("RS", 8, 16), False, m + q == 6)
+                for q in range(4):
+                    mm(a(E, 19 - m - 4 * q, 160, 20), a("A" + h, 512 * m + q, 512 * m + 512, 4), a("RS", 8, 16), False, m + q == 6)
+        for k in range(16 * SCAN):
+            mm(a(E, 19 - k, 160, 20), lanes("G", k), a("RS", 0, 8), False, False)
+        tops = []
+        for c in range(4 * SCAN):
+            for k in range(c, 16, 4):
+                scan(lanes("A", k), lanes("G", k), a("W" + h), ax("RP", 0, (0, 1)), OP.min, OP.max)
+                if c > 1:
+                    ops[-1]["after"] = tops[c - 2]
+            tt(a("A" + h, 80 + 5 * c, 2160, 20), a("G" + h, 80 + 5 * c, 2160, 20), a(Wp, 0, 104), OP.max)
+            tops.append(len(ops) - 1)
+            for k in range(c, 16, 4):
+                mm(a(E, 19 - k, 160, 20), lanes("A", k), a("RS", 8, 16), False, k == 15)
+        for o in ops[k0 + 1:-1]:
+            o["free"] = k0
 
     def post(h, e, rnd):
         E = EB[int(h)]
@@ -347,11 +435,10 @@ def program():
         if e < 6:
             ts(a(n, 64, 96), a(n, 0, 32), 0x3000, OP.bitwise_and)
             tt(a(s, 0, 32), a(n, 64, 96), a("KI"), OP.is_equal)
-            ts(a(n, 96, 104), a(n, 0, 32, 4), 13, OP.logical_shift_right, 0x1C0, OP.bitwise_and)
             tt(a2("SM" + h, 0, 4), a3(MC, 0, 4), a(s, 0, 32), OP.mult)
-            tt(a2("JQ" + h, 0, 1), a(n, 96, 104), a("TT" + h), OP.add)
+            ts(a2("JQ" + h, 1, 5), a(n, 0, 32), 0.0, OP.is_ge, 64.0, OP.mult)
             ts(a3("M" + h, 1, 4), a3(MC, 1, 4), 4096.0, OP.min)
-            rows(h, ["SM", "JQ", "M"])
+            rows(h, one=CFG["one"])
             ts(a("YO" + h), a(n, 32, 64), (1 << 22) - 1, OP.bitwise_and)
             prev = a(BB)
             for rk in range(2, DEPTH[e] + 2):
@@ -361,87 +448,104 @@ def program():
             if e >= 4:
                 ts(a(s, 96, 104), a(BB, 19, 160, 20), 4.0 * LV, OP.is_ge, 4.5 * LV, OP.mult)
             return
-        ts(a("FU" + h), ind(a(BB), a("LI", 2, 10)), 4.0 * LV, OP.is_ge)
-        ts(a(s, 0, 32), a3(MC, 1, 5), 4096.0, OP.min)
-        ts(a(s, 32, 64), a3(MC, 1, 5), 4096.0, OP.is_ge, -4097.0, OP.mult)
-        tt(a3("M" + h, 1, 5), a(s, 0, 32), a(s, 32, 64), OP.add)
+        act(a("FU" + h), ind(a(BB), a("LI", 2, 10)), AF.Sign, bias=0.5 - 4.0 * LV)
+        ts(a3("M" + h, 1, 5), a3(MC, 1, 5), 2047.0, OP.min)
         o = 128 * int(h)
-        mm(a(MBS[int(h)], 0, 128), ("M" + h, (ALL,)), a("IH"))
+        mm(a(MBS[int(h)], 0, 128), ("M" + h, (ALL,)), a("IH"), True, rnd == 0)
+        if rnd == 1:
+            ts(a3("M2" + h, 1, 5), a3(MC, 1, 5), 4096.0, OP.is_ge, -2048.0, OP.mult)
+            mm(a(MBS[int(h)], 0, 128), ("M2" + h, (ALL,)), a("IH"), False, True)
         act(a("MX", o, o + 128), a(MBS[int(h)], 0, 128))
         if rnd == 0:
             ts(a3("VA" + h, 0, 5), a3(MC, 0, 5), 4096.0, OP.is_lt)
             tt(a(s, 64, 104), a3("VA" + h, 0, 5), a3("VA" + h, 1, 6), OP.subtract)
             tt(a2("SM" + h, 0, 5), a3("M" + h, 0, 5), a(s, 64, 104), OP.mult)
-            rows(h, ["SM"])
+            rows(h, False)
 
     def commit(rnd):
         z = str(rnd)
-        MB, RB, LB, PP = EB[0], EB[1], MBS[0], MBS[1]
-        mm(a(MB, 0, 128), a("FU0"), a("UT"))
-        mm(a(MB, 128, 256), a("FU0"), a("ON"), True, False)
-        mm(a(MB, 128, 256), a("FU1"), a("UT"), False, True)
+        MB, RB, LB, PP = WP[0], EB[1], MBS[0], MBS[1]
+        mm(a(MB, 0, 256), a("UT", 128, 256), a("UT", 0, 256), True, False)
+        mm(a(MB, 128, 256), a("UT", 128, 256), a("UT", 0, 128), False, False)
+        mm(a(MB, 0, 256), a("FU0"), a("UT", 0, 256), False, False)
+        mm(a(MB, 128, 256), a("FU1"), a("UT", 0, 128), False, True)
         for c in range(3):
-            act(a("SG"), a(MB, 0, 256), AF.Sign, bias=col("cf", 40 + c), scale=-1.0, accum_out=col("AC", c))
-        ts(a("LN", 0, 3), a("AC", 0, 3), 0.5, OP.mult, 128.0, OP.add)
+            act(a("RK1", 0, 256), a(MB, 0, 256), AF.Sign, bias=col("cf", 40 + c), scale=-0.5, accum_out=col("cf", 64 + c))
+        ts(a("LN", 0, 3), a("cf", 64, 67), 0.5, OP.mult, 128.0, OP.add)
         cp(a("MS"), ind(a("MX"), a("LN", 0, 3)))
         if rnd == 1:
             for j in range(5):
                 dma("Y", ("ym", (ALL, slice(256 * j, 256 * j + 256))), ("MX", (slice(j, 128, 16), slice(0, 256))), 2500)
         for j in range(5):
-            mm(a(RB, 48 * j, 48 * j + 48), a("SEL", 128 * j, 128 * j + 128), a("MS"))
-        cp(a("BR", 0, 240), a(RB, 0, 240))
-        to_list(LB, "BR", 0, 240, 0)
-        ts(a("LF", 0, 15), a(LB, 0, 15), 0.0625, OP.mult)
+            mm(a(RB, j, 240, 5), a("SEL", 128 * j, 128 * j + 128), a("MS"))
+        cp(a("BR", 0, 6, 2), a(RB, 0, 240))
+        mm(a(EB[0], 0, 240), a("BD"), a("CJ"), True, False)
         for j in range(5):
-            mm(a(WP[0], 48 * j, 48 * j + 48), a("SEL", 640, 768), a("MS"))
-        act(a("BR", 240, 480), a(WP[0], 0, 240))
-        to_list(WP[1], "BR", 240, 480, 0)
-        act(a("LF", 16, 31), a(WP[1], 0, 15), AF.Identity, scale=0.0625)
-        for c in range(15):
-            ts(a("EW", 240 * c, 240 * c + 240), a("BR", 0, 240), col("LF", c), OP.is_equal, col("cf", 44 + c % 3), OP.mult)
-            mm(a(PP, 0, 240), a("BD"), a("EW", 240 * c, 240 * c + 240), c == 0, c == 14)
-        cp(a("LU", 0, 15), a("LF", 0, 15))
-        tt(a("DD", 16, 31), a("LF", 16, 31), a("CJ", 0, 15), OP.add)
-        cp(a("LU", 16, 31), a("DD", 16, 31))
-        act(a("CG"), ind(a("CH"), a("LU", 16, 31)))
-        tt(a("XT"), ind(a("X", 0, 2048), a("LU", 0, 15)), a("CG"), OP.add)
+            mm(a(EB[0], j, 240, 5), a("SEL", 640, 768), a("MS"), False, j == 4)
+        act(a("BR", 1, 6, 2), a(EB[0], 0, 240))
+        for b in range(16):
+            mm(a(LB, 0, 30), a("BIG", 15 - b, 143 - b), a3("BR", 5 * b, 5 * b + 5), b == 0, b == 15)
+        for c in range(3):
+            cp(ax("LU", ALL, (c, 15, 3)), a(LB, 10 * c, 10 * c + 10))
+        lv, lt = ax("LU", 0, (0, 15)), ax("LU", 1, (0, 15))
+        act(a("CG"), ind(a("CH"), lt))
+        if rnd == 0:
+            act(a("NG"), ind(a("NB", 0, 2048), ax("LU", 0, (0, 12))))
+            act(a("HG"), ind(a("SW"), ax("LU", 1, (0, 3))))
+        for c in range(3):
+            for j in range(5):
+                ew = ax("EW", 5 * c + j, (80 * c, 240))
+                ts(ew, a("BR", 2 * c, 6, 2), col(LB, 10 * c + j), OP.is_equal, col("cf", 44 + c), OP.mult)
+                mm(a(PP, 80 * c, 240), a("BD"), ew, c + j == 0, c + j == 6)
+        scan(a("RK0", 0, 240), a("RZ"), a(PP, 0, 240), 0.0, OP.mult, OP.max)
+        tt(a("GO"), a("RK0", 4, 240, 5), a("pw", 48, 96), OP.is_lt)
+        for b in range(16):
+            mm(a(LB, 32, 35), a("BIG", 15 - b, 143 - b), a("GO", b, 48, 16), b == 0, b == 15)
+        tt(a("XT"), ind(a("X", 0, 2048), lv), a("CG"), OP.add)
         ts(a("XN"), a("XT"), 255, OP.bitwise_and)
-        tt(a("LF", 0, 15), a("LF", 0, 15), a("JJ", 0, 15), OP.subtract)
+        act(a("LR", 32, 47), lv) if CFG.get("us") else cp(a("LR", 32, 47), lv)
+        tt(a("LR", 0, 15), a("LR", 32, 47), a("JJ", 0, 15), OP.subtract)
         tt(a("ZM", 0, 96), a("XN", 0, 96), a("XN", 96, 192), OP.max)
         tt(a("ZM", 96, 144), a("ZM", 0, 48), a("ZM", 48, 96), OP.max)
-        tt(a("ZM", 144, 192), a("ZM", 96, 144), a("XN", 192, 240), OP.max)
-        if rnd == 0:
-            act(a("HG"), ind(a("SW"), a("LU", 16, 19)))
-            cp(a("NG"), ind(a("NB", 0, 2048), a("LU", 0, 12)))
-            for p in range(2):
-                x0, x1 = a("NG", 96 * p, 96 * p + 48), a("NG", 96 * p + 48, 96 * p + 96)
-                d0, d1 = a("ND", 96 * p, 96 * p + 48), a("ND", 96 * p + 48, 96 * p + 96)
-                tt(d0, x1, x0, OP.subtract)
-                tt(d1, d0, a("HG"), OP.mult)
-                tt(x0, x0, d1, OP.add)
-                tt(x1, x1, d1, OP.subtract)
-        tt(a("OK"), a(PP, 0, 240), a("THR"), OP.is_lt)
-        tt(a("GO", 0, 96), a("OK", 0, 96), a("OK", 96, 192), OP.min)
-        tt(a("GO", 96, 144), a("GO", 0, 48), a("GO", 48, 96), OP.min)
-        tt(a("GO", 144, 192), a("GO", 96, 144), a("OK", 192, 240), OP.min)
-        to_list(LB, "GO", 144, 192, 32)
+        tt(a("ZZ", 0, 48), a("ZM", 96, 144), a("XN", 192, 240), OP.max)
         for m in range(3):
-            tt(a("ZS" + z, 16 * m, 16 * m + 16), a("ZM", 144 + m, 192, 3), a("GO", 144 + m, 192, 3), OP.mult)
+            tt(a("ZS" + z, 16 * m, 16 * m + 16), a("ZZ", m, 48, 3), a("GO", m, 48, 3), OP.mult)
         rec("G", "send", (rnd,), [], [a("ZS" + z)], 1500)
         for c in range(3):
-            ts(a("DD", c, 15, 3), a("LF", c, 15, 3), col(LB, 32 + c), OP.mult, 0.0625, OP.mult)
-        tt(a("DD", 16, 31), a("DD", 0, 15), a("JJ", 0, 15), OP.add)
-        cp(a("OF", 0, 15), a("DD", 16, 31))
+            ts(a("LR", 16 + c, 31, 3), a("LR", c, 15, 3), col(LB, 32 + c), OP.mult)
+        tt(a("LR", 48, 63), a("LR", 16, 31), a("JJ", 0, 15), OP.add)
+        cp(a("OF", 0, 15), a("LR", 48, 63))
         cp(ind(a("X"), a("OF", 0, 15)), a("XN"))
         if rnd == 0:
-            cp(ind(a("NB"), a("OF", 0, 12)), a("NG"))
+            D, N = WP[1], RB
+            for p in range(2):
+                mm(a(D, 48 * p, 48 * p + 48), a("IH"), a("NG", 96 * p + 48, 96 * p + 96), True, False)
+                mm(a(D, 48 * p, 48 * p + 48), a("NI"), a("NG", 96 * p, 96 * p + 48), False, True)
+            for p in range(2):
+                tt(a("DH", 48 * p, 48 * p + 48), a(D, 48 * p, 48 * p + 48), a("HG"), OP.mult)
+            mm(a(N, 0, 192), a("IH"), a("NG"), True, False)
+            for j in range(4):
+                mm(a(N, 48 * j, 48 * j + 48), a("NI" if j % 2 else "IH"), a("DH", 48 * (j // 2), 48 * (j // 2) + 48), False, j == 3)
+            act(a("ND"), a(N, 0, 192))
+            cp(ind(a("NB"), a("OF", 0, 12)), a("ND"))
         rec("R", "arrive", (rnd,), [a("LD" + z)], [a("ZS" + z)], 0)
         ops[-1]["sem"] = "arr" + z
         ops[-1]["lat"] = 5000
         if rnd == 1:
             dma("Y", ("yx", (ALL, ALL)), a("X", 0, 512), 2500)
-            act(a("YZ"), ind(a("LD1"), a("LI", 10, 13)))
-            dma("S", ("yz", (ALL, ALL)), a("YZ"), 2500)
+            act(a("ZZ", 48, 96), ind(a("LD1"), a("LI", 10, 13)))
+            dma("S", ("yz", (ALL, ALL)), a("ZZ", 48, 96), 2500)
+
+    def start(h, m0, t):
+        ms(a2("SM" + h, 1, 5), 0.0)
+        ms(a2("JQ" + h, 1, 5), 80.0)
+        if m0[0] != "MC" + h:
+            cp(a3("MC" + h, 0, 1), m0)
+        cp(a2("SM" + h, 0, 1), m0)
+        ts(a2("JQ" + h, 0, 1), t, col("cf", 23) if SCAN else 0.0, OP.add)
+        act(a3("M" + h, 0, 1), m0)
+        act(a3("M" + h, 5, 6), t)
+        rows(h, one=CFG["one1"])
 
     def new_lanes(h):
         n, MC, LB = "n" + h, "MC" + h, PPS[int(h)]
@@ -454,44 +558,33 @@ def program():
             return a(n, 8 * c, 8 * c + 8)
         lane = col("cf", 35 if h == "1" else 0)
         cp(k(0), a(LB, 64, 72))
+        ts(k(3), a(LB, 64, 72), 37.0, OP.mult, lane, OP.add)
         ts(k(1), k(0), 4095, OP.bitwise_and)
-        tt(k(2), k(1), k(1), OP.mult)
-        ts(k(3), k(1), 37.0, OP.mult, lane, OP.add)
-        ts(k(4), k(2), 5, OP.logical_shift_right)
         ts(a3(MC, 0, 1), k(3), 2047, OP.bitwise_and)
-        ts(k(5), k(4), lane, OP.add)
-        ms(a2("SM" + h, 1, 5), 0.0)
-        cp(a2("SM" + h, 0, 1), a3(MC, 0, 1))
-        ts(a("TT" + h), k(5), 63, OP.bitwise_and)
-        cp(a3("M" + h, 0, 1), a3(MC, 0, 1))
-        ts(a2("JQ" + h, 0, 1), a("TT" + h), 256.0, OP.add)
-        rows(h, ["SM", "JQ", "M"])
-        cp(a3("M" + h, 5, 6), a("TT" + h))
+        tt(k(2), k(1), k(1), OP.mult)
+        ts(k(4), k(2), col("cf", 60 + int(h)), OP.add)
+        ts(k(5), k(4), 5, OP.logical_shift_right, 63, OP.bitwise_and)
+        start(h, a3(MC, 0, 1), k(5))
 
+    low = (slice(0, 32), ALL)
+    cp(("CF0", low), ("BG", low))
+    mm(a(EB[0], 0, 32), ("CF0", low), ("IH", (slice(0, 32), slice(0, 32))))
+    cp(a("s0", 128, 160), a(EB[0], 0, 32))
     for h in "01":
-        to_list(PPS[int(h)], "RW" + h, 0, 256, 0)
-        cp(a("L" + h), a(PPS[int(h)], 0, 16))
-    for h in "01":
-        RB = EB[int(h)]
-        mm(a(RB, 0, 8), a("RW" + h, 0, 128), a("S0"))
-        mm(a(RB, 8, 16), a("RW" + h, 128, 256), a("S0"))
-        cp(a3("MC" + h, 0, 1), a(RB, 0, 8))
-        cp(a3("M" + h, 0, 1), a(RB, 0, 8))
-        ts(a("TT" + h), a(RB, 8, 16), -256.0, OP.add)
-        ts(a3("M" + h, 5, 6), a(RB, 8, 16), -256.0, OP.add)
+        start(h, a("s0", 128 + int(h), 144, 2), a("s0", 144 + int(h), 160, 2))
     for rnd in range(2):
         order = "01" if rnd == 0 else "10"
         for h in order:
             if rnd:
                 new_lanes(h)
             ms(a("YO" + h), 1 << 21)
-            prep(h, 1)
+            prep(h, 1, CFG["g1"] if h == order[0] else CFG["gv"])
         for e in range(1, 7):
             for h in order:
-                heavy(h)
+                heavy(h, e)
                 post(h, e, rnd)
                 if e < 6:
-                    prep(h, e + 1)
+                    prep(h, e + 1, CFG["g6"] if e == 5 and h == order[1] else CFG["gv"])
             if rnd == 0 and e == 1:
                 late_constants()
         commit(rnd)
@@ -505,28 +598,31 @@ def plan():
     for k, o in enumerate(ops):
         deps = {}
         acc = [(_span(p), True) for p in o["outs"]] + [(_span(p), False) for p in o["ins"]]
-        for (n, lo, hi, c), wr in acc:
+        for (n, bits, c), wr in acc:
             ps = SCRATCH[n][0] == "psum"
-            for (j, l2, h2, w2) in hist.get(n, []):
+            for (j, b2, w2) in hist.get(n, []):
                 same = ops[j]["eng"] == o["eng"]
                 if ps:
                     if same and o["eng"] == "P":
-                        deps.setdefault(j, False)
-                    elif not same or ((wr or w2) and lo <= h2 and l2 <= hi):
+                        if "free" not in o or ops[j].get("free") != o["free"]:
+                            deps.setdefault(j, False)
+                    elif not same or ((wr or w2) and bits & b2):
                         deps[j] = True
-                elif (wr or w2) and lo <= h2 and l2 <= hi:
+                elif (wr or w2) and bits & b2:
                     deps[j] = True
-        for (n, lo, hi, c), wr in acc:
+        for (n, bits, c), wr in acc:
             old = hist.get(n, [])
             if SCRATCH[n][0] == "psum":
-                old = [] if o["eng"] == "P" else [t for t in old if t[3] or ops[t[0]]["eng"] == o["eng"]]
-            elif wr and c == hi - lo + 1 and "sem" not in o:
-                old = [t for t in old if not (lo <= t[1] and t[2] <= hi)]
-            hist[n] = old + [(k, lo, hi, wr)]
+                old = (old if "free" in o else []) if o["eng"] == "P" else [t for t in old if t[2] or ops[t[0]]["eng"] == o["eng"]]
+            elif wr and "sem" not in o:
+                old = [t for t in old if t[1] & ~bits]
+            hist[n] = old + [(k, bits, wr)]
         if "stage" in o:
             if prevg:
                 deps.setdefault(prevg[-1], False)
             prevg.append(k)
+        if "after" in o:
+            deps.setdefault(o["after"], False)
         deps.pop(k, None)
         o["deps"] = deps
     n = len(ops)
@@ -534,43 +630,76 @@ def plan():
     for k, o in enumerate(ops):
         for j in o["deps"]:
             kids[j].append(k)
-    prio = [0.0] * n
+
+    def role(o):
+        x = o["args"][1 if o["eng"] == "P" else 0]
+        if not isinstance(x, tuple):
+            return ""
+        name = x[0].rstrip("01")
+        if name == "n":
+            name += str(x[1][1].start // 32)
+        if o["eng"] == "P" and name == "TG":
+            name += o["args"][2][0]
+        if name == "A" and o["call"] == "tensor_tensor":
+            name = "J"
+        return o["eng"] + name
+
+    def lat(j, k):
+        return ops[j].get("lat", 0) + (0 if not ops[k]["deps"][j] else SELF if ops[k]["eng"] == ops[j]["eng"] and "sem" not in ops[j] else HOP)
+
+    def run(prio):
+        left = [len(o["deps"]) for o in ops]
+        ready = [0.0] * n
+        t = [0.0] * n
+        pool = {e: [] for e in "VSPGYR"}
+        free = {e: 0.0 for e in pool}
+        order = {e: [] for e in pool}
+        for k, o in enumerate(ops):
+            if left[k] == 0:
+                pool[o["eng"]].append(k)
+        pick = {}
+        for _ in range(n):
+            best = None
+            for e in pool:
+                if pool[e]:
+                    if e not in pick:
+                        t0 = max(free[e], min(ready[k] for k in pool[e]))
+                        now = sorted((k for k in pool[e] if ready[k] <= t0 + 30), key=lambda k: (prio[k], -k))
+                        k = now[-1]
+                        if e in CFG["look"]:
+                            soon = [j for j in pool[e] if t0 + 30 < ready[j] < t0 + ops[k]["cost"] - 30
+                                    and prio[j] - prio[k] > ready[j] - t0 + 100]
+                            if soon:
+                                j = min(soon, key=lambda j: ready[j])
+                                fit = [i for i in now if t0 + ops[i]["cost"] <= ready[j] + 30]
+                                k = fit[-1] if fit else j
+                                t0 = max(t0, ready[k])
+                        pick[e] = (t0, e, k)
+                    if best is None or pick[e][0] < best[0]:
+                        best = pick[e]
+            t0, e, k = best
+            del pick[e]
+            t[k] = max(free[e], ready[k])
+            free[e] = t[k] + ops[k]["cost"]
+            pool[e].remove(k)
+            order[e].append(k)
+            for c in kids[k]:
+                ready[c] = max(ready[c], free[e] + lat(k, c))
+                left[c] -= 1
+                if left[c] == 0:
+                    pool[ops[c]["eng"]].append(c)
+                    pick.pop(ops[c]["eng"], None)
+        return max(t[k] + ops[k]["cost"] + ops[k].get("lat", 0) for k in range(n)), t, order
+    far = [0.0] * n
     for k in range(n - 1, -1, -1):
-        o = ops[k]
-        prio[k] = o["cost"] + o.get("lat", 0) + max([prio[c] + (HOP if ops[c]["deps"][k] else 0) for c in kids[k]] + [0.0])
-    left = [len(o["deps"]) for o in ops]
-    ready = [0.0] * n
-    pool = {e: [] for e in "VSPGYR"}
-    free = {e: 0.0 for e in pool}
-    order = {e: [] for e in pool}
-    busy = {e: 0.0 for e in pool}
-    for k, o in enumerate(ops):
-        if left[k] == 0:
-            pool[o["eng"]].append(k)
-    end = 0.0
-    for _ in range(n):
-        best = None
-        for e in pool:
-            if pool[e]:
-                t0 = max(free[e], min(ready[k] for k in pool[e]))
-                k = max((k for k in pool[e] if ready[k] <= t0 + 30), key=lambda k: ("stage" not in ops[k], prio[k], -k))
-                if best is None or t0 < best[0]:
-                    best = (t0, e, k)
-        t0, e, k = best
-        o = ops[k]
-        o["t"] = max(free[e], ready[k])
-        free[e] = o["t"] + o["cost"]
-        busy[e] += o["cost"]
-        fin = free[e] + o.get("lat", 0)
-        end = max(end, fin)
-        pool[e].remove(k)
-        order[e].append(k)
-        for c in kids[k]:
-            lat = 0 if not ops[c]["deps"][k] else (SELF if ops[c]["eng"] == e and "sem" not in o else HOP)
-            ready[c] = max(ready[c], fin + lat)
-            left[c] -= 1
-            if left[c] == 0:
-                pool[ops[c]["eng"]].append(c)
+        far[k] = ops[k]["cost"] + max([far[c] + lat(k, c) for c in kids[k]] + [ops[k].get("lat", 0)])
+    roles = [role(o) for o in ops]
+    if "hook" in CFG:
+        return CFG["hook"](run, far, roles)
+    end, t, order = run([p + CFG["up"].get(x, 0) for p, x in zip(far, roles)])
+    busy = {e: sum(ops[k]["cost"] for k in order[e]) for e in order}
+    for k in range(n):
+        ops[k]["t"] = t[k]
     pos = {}
     for e in order:
         for p, k in enumerate(order[e]):

@@ -1,16 +1,20 @@
 import numpy as np
 from concourse.bass import DstId, RemoteDMATransfer
-from concourse.mybir import AluOpType as OP, ActivationFunctionType as AF
+from concourse.mybir import AluOpType as OP, ActivationFunctionType as AF, AxisListType as AX
 
 F, H, B, I, U = "float32", "float16", "bfloat16", "int32", "uint16"
 LV = 1 << 19
 SC = float(1 << 22)
 DEPTH = {1: 4, 2: 3, 3: 3, 4: 2, 5: 1, 6: 0}
-RAMP = [float(1 << 32), float(1 << 24), float(1 << 16), 256.0, 1.0]
 GC, PE = 1.56, 0.5
-HOP, SELF = 240, 120
-CFG = {"scan": 0, "fix": 10, "rw": "S", "mw": "S", "pw": "S", "one": 1, "one1": 0, "g1": 2, "g6": 1, "gv": 0, "look": "V",
-       "wt": "SS", "th": "VVVV", "up": {"SG": -4000}}
+HOP, SELF = 210, 200
+CUTS, CUTS1 = (0, 64, 96), (0, 32, 64, 96)
+FIRST, LAST = (48, 64), (8, 32)
+URGE = {"SG": -4650, "SW": 700, "STG": 850, "SRW": 1050, "SCG_": -2100,
+        "VCF": 1500, "VJ": -800, "VJQ": -1450, "VEQ": 50, "VP": -3250, "VCU": -650, "VCU1": -900, "VFU_": 1450, "VBB_": -650,
+        "Vn1_": 550, "VMC_": 3650, "VSM_": -1400, "VJQ_": -1100, "VLR_": -3550, "Vcf_": 200, "VXT_": -500, "VL_": 500,
+        "PG": -550, "PA": -1000, "PEQ": 6000, "PSN": -1950, "PTGRET": 1050, "PBIG_": -800, "PIB_": 650, "PXG_": 1700}
+POLISH = 500
 
 
 def _scratch():
@@ -18,24 +22,22 @@ def _scratch():
 
     def sb(n, dt, *sh):
         s[n] = ("sbuf", [128] + list(sh), dt)
-    sb("X", B, 2304); sb("NB", I, 2304); sb("WT", B, 1920); sb("TH", B, 1920); sb("CH", B, 320); sb("SW", B, 64)
-    sb("PA", I, 64); sb("PB", I, 64); sb("WI", I, 4); sb("BG", I, 128)
-    sb("q1", I, 192); sb("q4", F, 64); sb("ci", I, 12); sb("cf", F, 80); sb("io", F, 200); sb("gi", B, 9, 20)
+    sb("X", B, 2304); sb("NB", I, 2304); sb("WT", B, 768); sb("TH", B, 384); sb("CH", B, 320); sb("SW", B, 64)
+    sb("PA", I, 64); sb("PB", I, 64); sb("WI", I, 4); sb("BG", I, 128); sb("CB", H, 128)
+    sb("q1", I, 192); sb("q4", F, 64); sb("ci", I, 28); sb("cf", F, 80); sb("io", F, 200); sb("gi", B, 9, 20)
     sb("t1", F, 160); sb("t2", F, 160); sb("t3", F, 160); sb("own", B, 9, 20); sb("r16", F, 16)
-    sb("IH", H, 128); sb("NI", H, 128); sb("BD", B, 128); sb("SEL", H, 768); sb("BIG", H, 288); sb("I2", H, 256); sb("IB", B, 128)
-    sb("RI", H, 160); sb("RN", B, 160); sb("RS", B, 16); sb("RET", B, 9, 20); sb("RP", B, 8, 20)
-    sb("KN", F, 32); sb("KL", F, 32); sb("KI", I, 32); sb("LI", U, 16); sb("UT", H, 256)
-    sb("WD", B, 8); sb("JJ", F, 16); sb("CJ", B, 240); sb("pw", F, 96); sb("RZ", B, 240)
+    sb("IH", H, 128); sb("NI", H, 128); sb("IB", B, 128); sb("BD", B, 128); sb("SEL", H, 768); sb("SN", H, 512)
+    sb("BIG", H, 288); sb("I2", H, 128); sb("RI", H, 160); sb("RN", B, 160); sb("RS", B, 16); sb("RET", B, 9, 20)
+    sb("RP", B, 8, 20); sb("KN", F, 32); sb("KL", F, 32); sb("KI", I, 32); sb("LI", U, 16); sb("UT", H, 256)
+    sb("WD", B, 16); sb("BW", B, 144); sb("JJ", F, 16); sb("CJ", B, 240); sb("pw", F, 96); sb("RZ", B, 240)
     for h in "01":
-        sb("G" + h, B, 2208); sb("A" + h, B, 2208); sb("CU" + h, U, 128); sb("CB" + h, H, 128); sb("CF" + h, H, 128)
-        sb("W" + h, B, 128)
+        sb("G" + h, B, 2048); sb("A" + h, B, 2048); sb("CU" + h, U, 128); sb("CF" + h, H, 128); sb("W" + h, B, 256)
         sb("TG" + h, B, 128); sb("EQ" + h, B, 512); sb("P" + h, F, 160); sb("BB" + h, F, 160); sb("RK" + h, F, 640)
-        sb("RW" + h, H, 256); sb("L" + h, U, 16); sb("SM" + h, H, 17, 8); sb("JQ" + h, H, 17, 8); sb("M" + h, H, 8, 16)
-        sb("M2" + h, H, 8, 16)
-        sb("FU" + h, H, 128); sb("MC" + h, I, 8, 5); sb("YO" + h, I, 32)
+        sb("RW" + h, H, 256); sb("L" + h, U, 24); sb("SM" + h, H, 17, 8); sb("JQ" + h, H, 17, 8); sb("M" + h, H, 8, 16)
+        sb("M2" + h, H, 8, 16); sb("FU" + h, H, 128); sb("MC" + h, I, 8, 5); sb("YO" + h, I, 32)
         sb("s" + h, F, 160); sb("n" + h, I, 128); sb("VA" + h, F, 8, 6); sb("XG" + h, B, 128)
         sb("ZS" + h, B, 48); sb("LD" + h, B, 48)
-    sb("MX", F, 272); sb("LN", U, 4); sb("MS", H, 48); sb("BR", H, 6, 80)
+    sb("MX", F, 272); sb("MY", F, 256); sb("LN", U, 4); sb("MS", H, 48); sb("BR", H, 6, 80)
     sb("LR", F, 64); sb("LU", U, 2, 16); sb("OF", U, 16); sb("EW", B, 15, 240)
     sb("GO", H, 48); sb("CG", B, 240); sb("XT", I, 240); sb("XN", I, 240); sb("ZM", B, 144)
     sb("NG", H, 192); sb("HG", F, 48); sb("DH", H, 96); sb("ND", I, 192); sb("ZZ", B, 96)
@@ -45,10 +47,9 @@ def _scratch():
 
 
 SCRATCH = _scratch()
-SEMAPHORES = ["cV", "cS", "cP", "cG", "sent", "arr0", "arr1"] + ["d%d" % k for k in range(24)]
+SEMAPHORES = ["cV", "cS", "cP", "cG", "sent", "arr0", "arr1"] + ["d%d" % k for k in range(20)]
 ALL = slice(None)
 WP, EB, PPS, MBS = ("ps0", "ps1"), ("ps2", "ps3"), ("ps4", "ps5"), ("ps6", "ps7")
-EE = (WP, EB)
 
 
 def a(n, lo=None, hi=None, st=None):
@@ -95,9 +96,7 @@ def _span(ap):
 
 def program():
     ops = []
-    SCAN = CFG["scan"]
     nd = [0]
-    fix = CFG["fix"]
 
     def rec(eng, call, args, outs, ins, cost, **kw):
         ops.append(dict(eng=eng, call=call, args=args, outs=outs, ins=ins, cost=cost, kw=kw))
@@ -116,7 +115,7 @@ def program():
             return 60 + 3.5 * cnt(out)
         if src[0] == "*":
             return 60 + GC * cnt(src)
-        return max(64, m * cnt(src)) + fix
+        return max(64, m * cnt(src))
 
     def sides(out, *srcs):
         o = parts(out)
@@ -136,8 +135,7 @@ def program():
             vcost(out, x, 0.5 if two(out, x) else 1))
 
     def scan(out, d0, d1, init, op0, op1):
-        rec("V", "tensor_tensor_scan", (out, d0, d1, init, op0, op1), [out], [d0, d1] + [init] * isinstance(init, tuple),
-            vcost(out, d0, 0.5 if two(out, d0, d1) else 1))
+        rec("V", "tensor_tensor_scan", (out, d0, d1, init, op0, op1), [out], [d0, d1], vcost(out, d0, 1))
 
     def ms(out, v):
         rec("V", "memset", (out, v), [out], [], max(64, cnt(out) * (0.5 if two(out) else 1)))
@@ -146,10 +144,7 @@ def program():
         o, i = sides(out, src, *[kw[k] for k in kw if k != "accum_out"])
         if "accum_out" in kw:
             o = o + [kw["accum_out"]]
-        rec("S", "activation", (out, src, f), o, i, 78 + GC * cnt(src) if src[0] == "*" else max(64, cnt(src)) + fix, **kw)
-
-    def mov(eng, out, src):
-        (cp if eng == "V" else act)(out, src)
+        rec("S", "activation", (out, src, f), o, i, 78 + GC * cnt(src) if src[0] == "*" else max(64, cnt(src)), **kw)
 
     def mm(out, l, r, st=True, sp=True):
         rec("P", "matmul", (out, l, r, st, sp), [out], [l, r], PE * max(min(64, cnt(l)), cnt(r)))
@@ -168,17 +163,22 @@ def program():
         nd[0] += 1
 
     ms(a("PB"), 0)
-    dma("Y", a("NB", 0, 2048), ("nb", (ALL, ALL)), 6000)
+    k0 = len(ops)
     dma("Y", ("BG", (slice(0, 16), ALL)), ("beg", (ALL, ALL)), 2600)
     dma("Y", ("BG", (slice(16, 32), ALL)), ("tau", (ALL, ALL)), 2600)
-    dma("S", a("X", 0, 2048), ("x", (ALL, ALL)), 6200)
-    dma("S", a("PA"), ("par", (ALL, ALL)), 2800)
-    dma("Y", ("PB", (slice(0, 124), ALL)), ("par", (slice(4, 128), ALL)), 2800)
-    dma("S", a("EQ1", 320, 384), ("feat", (ALL, slice(0, 64))), 3000)
-    dma("S", a("EQ1", 64, 256), ("feat", (ALL, slice(64, 256))), 3000)
+    dma("Y", a("NB", 0, 2048), ("nb", (ALL, ALL)), 6000)
     dma("Y", a("CH"), ("chg", (ALL, ALL)), 7000)
     dma("Y", a("SW", 0, 64), ("swp", (ALL, ALL)), 7000)
     dma("Y", col("WI", 0), ("wt", (ALL, ALL)), 7000)
+    k1 = len(ops)
+    dma("S", a("WT", 320, 384), ("feat", (ALL, slice(0, 64))), 3000)
+    dma("S", a("WT", 64, 256), ("feat", (ALL, slice(64, 256))), 3000)
+    dma("S", a("PA"), ("par", (ALL, ALL)), 2800)
+    dma("S", a("X", 0, 2048), ("x", (ALL, ALL)), 6200)
+    dma("S", ("PB", (slice(0, 124), ALL)), ("par", (slice(4, 128), ALL)), 3500)
+    for k in range(k0 + 1, len(ops)):
+        if k != k1:
+            ops[k]["after"] = k - 1
 
     def io(lo, hi, st=None):
         return a("io", 32 + lo, 32 + hi, st)
@@ -194,23 +194,16 @@ def program():
     cp(a("cf", 0, 5), a("ci", 0, 5))
     pp, rr, pg = col("cf", 0), col("cf", 1), col("cf", 2)
     ts(a("BIG", 144, 288), io(-7, 137), col("cf", 4), OP.is_equal)
-    ts(a("I2", 0, 128), a("RK0", 0, 128), pp, OP.is_equal)
+    ts(a("I2"), a("RK0", 0, 128), pp, OP.is_equal)
     ts(a("r16"), io(0, 16), rr, OP.is_equal)
 
     def r(k):
         return col("r16", k)
     ts(a("IH"), io(0, 128), pp, OP.is_equal)
-    if SCAN:
-        ts(col("ci", 9), pp, -2.0, OP.add, 0.2, OP.mult)
-        act(col("cf", 62), col("ci", 9), AF.Identity, scale=-5.0, bias=pp)
-        ts(col("cf", 63), col("cf", 62), 4.0, OP.is_equal)
-        act(col("cf", 68), col("ci", 9))
-        act(col("cf", 69), col("cf", 62), AF.Identity, scale=26.0, bias=col("cf", 68))
-        tt(col("cf", 70), col("cf", 69), col("cf", 63), OP.subtract)
-        ts(a("I2", 128, 256), a("RK0", 0, 128), col("cf", 70), OP.is_equal)
     ts(a("BD"), a("t1", 0, 128), pg, OP.is_equal)
-    for i in range(6):
-        act(a("SEL", 128 * i, 128 * i + 128), a("BD"), AF.Identity, scale=r(i))
+    ts(a("cf", 76, 80), a("r16", 0, 4), 1.0, OP.mult, r(15), OP.add)
+    for i in range(4):
+        act(a("SN", 128 * i, 128 * i + 128), a("BD"), AF.Identity, scale=col("cf", 76 + i))
     ts(a("q1", 0, 64), a("PA"), 0xF00, OP.bitwise_and)
     ts(a("q1", 64, 128), a("PB"), 0xFF, OP.bitwise_and)
     ts(a("q1", 128, 192), a("PA"), 3, OP.bitwise_and)
@@ -231,21 +224,19 @@ def program():
         j = {1: 2, 2: 3, 3: 4, 5: 1}.get(b)
         act(a("TH", 64 * b, 64 * b + 64), a("q4"), AF.Identity, scale=col("cf", 8 + j) if j else 0.0,
             bias=col("cf", 16 + b if j else 28))
-    ms(a("EQ1", 0, 64), 0.0); ms(a("EQ1", 256, 320), 0.0)
-    for m in (4, 0, 1, 2, 3)[:1 + 4 * SCAN]:
-        ts(a("WT", 384 * m, 384 * m + 384), a("EQ1", 0, 384), 1.0 * SCAN, OP.add, RAMP[m], OP.mult)
+    ms(a("WT", 0, 64), 0.0); ms(a("WT", 256, 320), 0.0)
     e0, e1 = a("EQ0", 0, 384), a("EQ1", 0, 384)
-    mm(a(WP[0], 0, 384), a("BD"), a("WT", 1536, 1920))
+    mm(a(WP[0], 0, 384), a("BD"), a("WT", 0, 384))
     act(e0, a(WP[0], 0, 384))
     tt(e1, a(WP[0], 0, 384), e0, OP.subtract)
     act(a("IB"), a("IH"))
     act(a("TG0"), a("IH"), AF.Identity, scale=r(1))
     act(a("TG1"), a("IH"), AF.Identity, scale=r(0))
-    for i, (d, x) in enumerate((("IB", a("TH", 0, 384)), ("TG0", e0), ("TG1", e1))):
+    for i, (d, x) in enumerate((("IB", a("TH")), ("TG0", e0), ("TG1", e1))):
         mm(a(WP[1], 0, 384), a(d), x, i == 0, i == 2)
     ts(col("cf", 29), pg, 1.25, OP.mult, rr, OP.subtract)
     ts(a("RI"), io(-19, 141), col("cf", 29), OP.is_equal)
-    act(a("RN", 0, 160), a("RI"), AF.Identity, scale=-float(1 << 72))
+    act(a("RN", 0, 160), a("RI"), AF.Identity, scale=-SC * 65536)
     ts(a("RS", 0, 8), io(0, 128, 16), pg, OP.is_equal, SC, OP.mult)
     act(a("RS", 8, 16), a("RS", 0, 8), AF.Identity, scale=-2.0)
     ts(("own", (ALL,)), ("gi", (ALL,)), pg, OP.is_equal)
@@ -264,20 +255,15 @@ def program():
     act(a("KN"), a("KN"), AF.Identity, scale=32.0)
     act(col("cf", 14), col("cf", 3), AF.Identity, scale=5.0, bias=19.0)
     ts(a("LI", 0, 2), io(0, 2), 80.0, OP.mult, col("cf", 14), OP.add)
-    act(a("TH", 1536, 1920), a(WP[1], 0, 384))
-    for m in range(4 * SCAN):
-        act(col("cf", 72 + m), col("cf", 22), AF.Identity, scale=RAMP[m] - 1.0, bias=1.0)
-        if CFG["th"][m] == "V":
-            ts(a("TH", 384 * m, 384 * m + 384), a("TH", 1536, 1920), col("cf", 72 + m), OP.mult)
-        else:
-            act(a("TH", 384 * m, 384 * m + 384), a("TH", 1536, 1920), AF.Identity, scale=col("cf", 72 + m))
-    if SCAN:
-        act(col("cf", 23), col("cf", 62), AF.Identity, scale=384.0)
+    act(a("WT", 384, 768), a(WP[1], 0, 384))
     for h in "01":
         for n in ("SM", "JQ", "M"):
             ms((n + h, (ALL,)), 0.0)
+        ms(a3("M" + h, 15, 16), 2048.0)
 
     def late_constants():
+        for i in range(6):
+            act(a("SEL", 128 * i, 128 * i + 128), a("BD"), AF.Identity, scale=r(i))
         ts(a("LI", 2, 10), io(0, 8), 20.0, OP.mult, 19.0, OP.add)
         ts(a("BIG", 0, 144), io(-15, 129), pg, OP.is_equal, 0.0625, OP.mult)
         act(a("NI"), a("IH"), AF.Identity, scale=-1.0)
@@ -289,7 +275,13 @@ def program():
         ts(a("UT", 0, 128), io(0, 128), pp, OP.is_ge)
         ms(a("UT", 128, 256), 1.0)
         act(col("cf", 34), col("WI", 0), AF.Identity, scale=1.0 / SC)
-        act(a("WD"), a("RS", 0, 8), AF.Identity, scale=col("cf", 34))
+        act(a("WD", 0, 8), a("RS", 0, 8), AF.Identity, scale=col("cf", 34))
+        act(col("cf", 39), col("WI", 0), AF.Identity, scale=16.0)
+        act(a("BW"), a("BIG", 0, 144), AF.Identity, scale=col("cf", 39))
+        iota(a("ci", 12, 20), [[pow(37, -1, 128), 8]])
+        ts(a("ci", 20, 28), a("ci", 12, 20), 127, OP.bitwise_and)
+        act(a("WD", 8, 16), a("ci", 20, 28))
+        act(col("cf", 38), rr, AF.Identity, bias=128.0)
         iota(col("cf", 35), [[0, 1]], 128, 1)
         iota(a("cf", 60, 62), [[4096, 2]], 0, 32)
         act(col("cf", 36), rr, AF.Identity, bias=0.5)
@@ -314,76 +306,59 @@ def program():
         tt(a("cf", 56, 59), a("cf", 48, 51), a("cf", 52, 55), OP.add)
         cp(a("LI", 10, 13), a("cf", 56, 59))
 
-    def turn(bank, lo, name, o=0):
-        mm(a(bank, lo, lo + 64), (name, (ALL, slice(1, 17))), a("I2", o, o + 64), True, False)
-        mm(a(bank, lo, lo + 64), (name, (ALL, slice(0, 16))), a("I2", o + 64, o + 128), False, True)
+    def turn(bank, lo, name):
+        mm(a(bank, lo, lo + 64), (name, (ALL, slice(1, 17))), a("I2", 0, 64), True, False)
+        mm(a(bank, lo, lo + 64), (name, (ALL, slice(0, 16))), a("I2", 64, 128), False, True)
 
     def to_list(h, bank, lo, hi):
         for b in range(8):
             mm(a(bank, 256, 256 + hi - lo), a("BIG", 151 - b, 279 - b), a("RW" + h, 8 * lo + b, 8 * hi, 8), b == 0, b == 7)
         cp(a("L" + h, lo, hi), a(bank, 256, 256 + hi - lo))
 
-    def rows(h, more=True, one=True):
+    def rows(h, parents, templates):
         RB, MB = PPS[int(h)], MBS[int(h)]
-        if more and one:
-            turn(RB, 64, "JQ" + h)
-            turn(RB, 0, "SM" + h, 128 * SCAN)
-            mov(CFG["rw"], a("RW" + h, 0, 128), a(RB, 0, 128))
-            to_list(h, RB, 0, 16)
-            mm(a(MB, 0, 128), ("M" + h, (ALL,)), a("IH"))
-            mov(CFG["mw"], a("RW" + h, 128, 256), a(MB, 0, 128))
-            return
-        turn(RB, 0, "SM" + h, 128 * SCAN if more else 0)
-        mov(CFG["rw"], a("RW" + h, 0, 64), a(RB, 0, 64))
-        to_list(h, RB, 0, 8)
-        if more:
+        if parents:
+            turn(RB, 0, "SM" + h)
+            act(a("RW" + h, 0, 64), a(RB, 0, 64))
+            to_list(h, RB, 0, 8)
+        if templates:
             turn(MB, 0, "JQ" + h)
             mm(a(MB, 64, 192), ("M" + h, (ALL,)), a("IH"))
             act(a("RW" + h, 64, 256), a(MB, 0, 192))
             to_list(h, RB, 8, 16)
 
-    def prep(h, e, gv):
+    def both_lists(h):
+        RB, MB = PPS[int(h)], MBS[int(h)]
+        turn(RB, 64, "JQ" + h)
+        turn(RB, 0, "SM" + h)
+        act(a("RW" + h, 0, 128), a(RB, 0, 128))
+        to_list(h, RB, 0, 16)
+        mm(a(MB, 0, 128), ("M" + h, (ALL,)), a("IH"))
+        act(a("RW" + h, 128, 256), a(MB, 0, 128))
+
+    def prep(h, e, gv, direct=False):
         PP, MB, Wp = PPS[int(h)], MBS[int(h)], WP[int(h)]
-        cp(a("CU" + h), ind(a("NB", 0, 2048), a("L" + h, 0, 8)))
-        if not SCAN:
-            mov(CFG["wt"][0], a("W" + h), ind(a("WT", 1536, 1920), a("L" + h, 8, 16)))
-            for q in range(4):
-                mm(a(Wp, q, 512, 4), a("IB"), a("W" + h))
-            for c in range(4):
-                out, src = a("G" + h, 512 * c, 512 * c + 512), ind(a("X", 0, 2048), a("CU" + h, 32 * c, 32 * c + 32))
-                if c >= 4 - gv:
-                    cp(out, src)
-                else:
-                    act(out, src)
-                    ops[-1]["stage"] = 1
-            mov(CFG["wt"][1], a("TG" + h), ind(a("TH", 1536, 1920), a("L" + h, 8, 16)))
-            cp(a("CF" + h), a("CU" + h))
-        for m in range(5 * SCAN):
-            lo, n, at = ((0, 26, 80), (26, 26, 96), (52, 26, 112), (78, 25, 128), (102, 26, 64))[m]
-            nv = min(n, max(0, gv - 26 * (4 - m)))
-            if nv < n:
-                act(a("G" + h, at, at + 80 * (n - nv), 5), ind(a("X", 0, 2048), a("CU" + h, lo, lo + n - nv)),
-                    AF.Identity, scale=RAMP[m], bias=RAMP[m])
-                ops[-1]["stage"] = 1
-            if nv:
-                ts(a("G" + h, at + 80 * (n - nv), at + 80 * n, 5), ind(a("X", 0, 2048), a("CU" + h, lo + n - nv, lo + n)),
-                   RAMP[m], OP.mult, RAMP[m], OP.add)
-        if SCAN:
-            mov(CFG["wt"][0], a("W" + h), ind(a("WT"), a("L" + h, 8, 16)))
-            mov(CFG["wt"][1], a("TG" + h), ind(a("TH"), a("L" + h, 8, 16)))
-            for q in range(4):
-                mm(a(Wp, q, 104, 4), a("IB"), a("W" + h, 0, 128, 5))
-            cp(a("CB" + h), a("CU" + h))
-            for m, lo in enumerate((0, 26, 52, 78, 103)):
-                gcopy(a("CF" + h, m, 128, 5), a("CB" + h, lo, lo + (26 if m < 3 else 25)))
+        cp(a("CU" + h), ind(a("NB", 0, 2048), a("L" + h, 16, 24) if direct else a("L" + h, 0, 8)))
+        act(a("W" + h, 0, 128), ind(a("WT", 0, 384), a("L" + h, 8, 16)))
+        act(a("W" + h, 128, 256), ind(a("WT", 384, 768), a("L" + h, 8, 16)))
+        for q in range(4):
+            mm(a(Wp, q, 512, 4), a("IB"), a("W" + h, 0, 128))
+        cuts = [c for c in (CUTS1 if e == 1 else CUTS) if c < 128 - gv] + [128 - gv]
+        for lo, hi in zip(cuts, cuts[1:]):
+            act(a("G" + h, 16 * lo, 16 * hi), ind(a("X", 0, 2048), a("CU" + h, lo, hi)))
+            ops[-1]["stage"] = 1
+        for lo in range(128 - gv, 128, 32):
+            hi = min(128, lo + 32)
+            cp(a("G" + h, 16 * lo, 16 * hi), ind(a("X", 0, 2048), a("CU" + h, lo, hi)))
+        cp(a("CF" + h), a("CU" + h))
         ne = min(e, 4)
         for i in range(ne):
-            mm(a(MB, 128 * i, 128 * i + 128), a("SEL", 128 * i, 128 * i + 128), a("RW" + h, 128, 256))
+            mm(a(MB, 128 * i, 128 * i + 128), a("SN", 128 * i, 128 * i + 128), a("RW" + h, 128, 256))
         for i in range(ne):
             tt(a("EQ" + h, 128 * i, 128 * i + 128), a("CF" + h), a(MB, 128 * i, 128 * i + 128), OP.is_equal)
         mm(a(PP, 0, 160), a("CF" + h), a("RI"), True, False)
-        mm(a(PP, 0, 160), a("TG" + h), a("RP"), False, True)
-        mov(CFG["pw"], a("P" + h), a(PP, 0, 160))
+        mm(a(PP, 0, 160), a("W" + h, 128, 256), a("RP"), False, True)
+        act(a("P" + h), a(PP, 0, 160))
         for rk in range(2, DEPTH[e - 1] + 2 if e > 1 else 0):
             src = a("RK" + h, 160 * (rk - 2) + 20 - rk, 160 * (rk - 1), 20)
             if e > 4 and rk == 2:
@@ -394,34 +369,18 @@ def program():
     def heavy(h, e):
         E, Wp = EB[int(h)], WP[int(h)]
         k0 = len(ops)
-        mm(a(E, 0, 180), a("TG" + h), a("RET"), True, False)
+        mm(a(E, 0, 180), a("W" + h, 128, 256), a("RET"), True, False)
         for i in range(min(e, 4)):
             mm(a(E, 0, 160), a("EQ" + h, 128 * i, 128 * i + 128), a("RN"), False, False)
-
-        def lanes(n, k):
-            return a(n + h, 80 + 5 * k, 80 + 5 * k + 2033, 16)
-        if not SCAN:
-            for c in range(4):
-                for m in range(4):
-                    tt(a("A" + h, 512 * m + 128 * c, 512 * m + 128 * c + 128), a("G" + h, 512 * c + m, 512 * c + 512, 4),
-                       a(Wp, 128 * c, 128 * c + 128), OP.max)
-            for k in range(16):
-                mm(a(E, 19 - k, 160, 20), a("G" + h, k, 2048, 16), a("RS", 0, 8), False, False)
+        for c in range(4):
             for m in range(4):
-                for q in range(4):
-                    mm(a(E, 19 - m - 4 * q, 160, 20), a("A" + h, 512 * m + q, 512 * m + 512, 4), a("RS", 8, 16), False, m + q == 6)
-        for k in range(16 * SCAN):
-            mm(a(E, 19 - k, 160, 20), lanes("G", k), a("RS", 0, 8), False, False)
-        tops = []
-        for c in range(4 * SCAN):
-            for k in range(c, 16, 4):
-                scan(lanes("A", k), lanes("G", k), a("W" + h), ax("RP", 0, (0, 1)), OP.min, OP.max)
-                if c > 1:
-                    ops[-1]["after"] = tops[c - 2]
-            tt(a("A" + h, 80 + 5 * c, 2160, 20), a("G" + h, 80 + 5 * c, 2160, 20), a(Wp, 0, 104), OP.max)
-            tops.append(len(ops) - 1)
-            for k in range(c, 16, 4):
-                mm(a(E, 19 - k, 160, 20), lanes("A", k), a("RS", 8, 16), False, k == 15)
+                tt(a("A" + h, 512 * m + 128 * c, 512 * m + 128 * c + 128), a("G" + h, 512 * c + m, 512 * c + 512, 4),
+                   a(Wp, 128 * c, 128 * c + 128), OP.max)
+        for k in range(16):
+            mm(a(E, 19 - k, 160, 20), a("G" + h, k, 2048, 16), a("RS", 0, 8), False, False)
+        for m in range(4):
+            for q in range(4):
+                mm(a(E, 19 - m - 4 * q, 160, 20), a("A" + h, 512 * m + q, 512 * m + 512, 4), a("RS", 8, 16), False, m + q == 6)
         for o in ops[k0 + 1:-1]:
             o["free"] = k0
 
@@ -437,8 +396,8 @@ def program():
             tt(a(s, 0, 32), a(n, 64, 96), a("KI"), OP.is_equal)
             tt(a2("SM" + h, 0, 4), a3(MC, 0, 4), a(s, 0, 32), OP.mult)
             ts(a2("JQ" + h, 1, 5), a(n, 0, 32), 0.0, OP.is_ge, 64.0, OP.mult)
-            ts(a3("M" + h, 1, 4), a3(MC, 1, 4), 4096.0, OP.min)
-            rows(h, one=CFG["one"])
+            ts(a3("M" + h, 1, 4), a3(MC, 1, 4), 2048.0, OP.min, -2048.0, OP.add)
+            both_lists(h)
             ts(a("YO" + h), a(n, 32, 64), (1 << 22) - 1, OP.bitwise_and)
             prev = a(BB)
             for rk in range(2, DEPTH[e] + 2):
@@ -448,34 +407,50 @@ def program():
             if e >= 4:
                 ts(a(s, 96, 104), a(BB, 19, 160, 20), 4.0 * LV, OP.is_ge, 4.5 * LV, OP.mult)
             return
-        act(a("FU" + h), ind(a(BB), a("LI", 2, 10)), AF.Sign, bias=0.5 - 4.0 * LV)
-        ts(a3("M" + h, 1, 5), a3(MC, 1, 5), 2047.0, OP.min)
+        ts(a("FU" + h), ind(a(BB), a("LI", 2, 10)), 4.0 * LV, OP.is_ge)
+        ts(a3("M" + h, 0, 5), a3(MC, 0, 5), 2047.0, OP.min)
         o = 128 * int(h)
-        mm(a(MBS[int(h)], 0, 128), ("M" + h, (ALL,)), a("IH"), True, rnd == 0)
+        mm(a(MBS[int(h)], 0, 128), ("M" + h, (ALL,)), a("IH"))
+        act(a("MX", o, o + 128), a(MBS[int(h)], 0, 128))
         if rnd == 1:
             ts(a3("M2" + h, 1, 5), a3(MC, 1, 5), 4096.0, OP.is_ge, -2048.0, OP.mult)
-            mm(a(MBS[int(h)], 0, 128), ("M2" + h, (ALL,)), a("IH"), False, True)
-        act(a("MX", o, o + 128), a(MBS[int(h)], 0, 128))
+            mm(a(PPS[int(h)], 0, 128), ("M" + h, (ALL,)), a("IH"), True, False)
+            mm(a(PPS[int(h)], 0, 128), ("M2" + h, (ALL,)), a("IH"), False, True)
+            act(a("MY", o, o + 128), a(PPS[int(h)], 0, 128))
         if rnd == 0:
             ts(a3("VA" + h, 0, 5), a3(MC, 0, 5), 4096.0, OP.is_lt)
             tt(a(s, 64, 104), a3("VA" + h, 0, 5), a3("VA" + h, 1, 6), OP.subtract)
             tt(a2("SM" + h, 0, 5), a3("M" + h, 0, 5), a(s, 64, 104), OP.mult)
-            rows(h, False)
+            rows(h, True, False)
 
     def commit(rnd):
         z = str(rnd)
         MB, RB, LB, PP = WP[0], EB[1], MBS[0], MBS[1]
-        mm(a(MB, 0, 256), a("UT", 128, 256), a("UT", 0, 256), True, False)
-        mm(a(MB, 128, 256), a("UT", 128, 256), a("UT", 0, 128), False, False)
-        mm(a(MB, 0, 256), a("FU0"), a("UT", 0, 256), False, False)
-        mm(a(MB, 128, 256), a("FU1"), a("UT", 0, 128), False, True)
-        for c in range(3):
-            act(a("RK1", 0, 256), a(MB, 0, 256), AF.Sign, bias=col("cf", 40 + c), scale=-0.5, accum_out=col("cf", 64 + c))
-        ts(a("LN", 0, 3), a("cf", 64, 67), 0.5, OP.mult, 128.0, OP.add)
+        if rnd == 0:
+            mm(a(MB, 0, 128), a("FU0"), a("UT", 0, 128))
+            for c in range(3):
+                act(ax("EW", c, (0, 128)), a(MB, 0, 128), AF.Sign, bias=col("cf", 40 + c), scale=-1.0, accum_out=col("cf", 64 + c))
+            act(a("cf", 68, 71), a("cf", 64, 67), AF.Identity, scale=0.5, bias=128.0)
+            mm(a(WP[1], 0, 128), a("FU0"), a("UT", 128, 256), True, False)
+            mm(a(WP[1], 0, 128), a("FU1"), a("UT", 0, 128), False, True)
+            for c in range(3):
+                act(ax("EW", 3 + c, (0, 128)), a(WP[1], 0, 128), AF.Sign, bias=col("cf", 40 + c), scale=-1.0, accum_out=col("cf", 72 + c))
+            for c in range(3):
+                ts(col("LN", c), col("cf", 72 + c), 0.5, OP.mult, col("cf", 68 + c), OP.add)
+        else:
+            for bank in (MB, WP[1]):
+                mm(a(bank, 0, 256), a("FU0"), a("UT", 0, 256), True, False)
+                mm(a(bank, 128, 256), a("FU1"), a("UT", 0, 128), False, True)
+            for c in range(2):
+                act(a("RK1", 256 * c, 256 * c + 256), a(MB, 0, 256), AF.Sign, bias=col("cf", 40 + c), scale=-1.0, accum_out=col("cf", 64 + c))
+            ts(a("EQ0", 0, 256), a(WP[1], 0, 256), col("cf", 42), OP.is_lt)
+            rec("V", "tensor_reduce", (col("cf", 67), a("EQ0", 0, 256), AX.X, OP.add), [col("cf", 67)], [a("EQ0", 0, 256)], 256)
+            cp(col("LN", 2), col("cf", 67))
+            ts(a("LN", 0, 2), a("cf", 64, 66), 0.5, OP.mult, 128.0, OP.add)
         cp(a("MS"), ind(a("MX"), a("LN", 0, 3)))
         if rnd == 1:
             for j in range(5):
-                dma("Y", ("ym", (ALL, slice(256 * j, 256 * j + 256))), ("MX", (slice(j, 128, 16), slice(0, 256))), 2500)
+                dma("Y", ("ym", (ALL, slice(256 * j, 256 * j + 256))), ("MY", (slice(j, 128, 16), slice(0, 256))), 2500)
         for j in range(5):
             mm(a(RB, j, 240, 5), a("SEL", 128 * j, 128 * j + 128), a("MS"))
         cp(a("BR", 0, 6, 2), a(RB, 0, 240))
@@ -501,9 +476,15 @@ def program():
         tt(a("GO"), a("RK0", 4, 240, 5), a("pw", 48, 96), OP.is_lt)
         for b in range(16):
             mm(a(LB, 32, 35), a("BIG", 15 - b, 143 - b), a("GO", b, 48, 16), b == 0, b == 15)
-        tt(a("XT"), ind(a("X", 0, 2048), lv), a("CG"), OP.add)
+        if rnd == 0:
+            act(a("EQ1", 0, 240), ind(a("X", 0, 2048), lv))
+            mm(a(WP[0], 0, 240), a("IB"), a("CG"), True, False)
+            mm(a(WP[0], 0, 240), a("IB"), a("EQ1", 0, 240), False, True)
+            act(a("XT"), a(WP[0], 0, 240))
+        else:
+            tt(a("XT"), ind(a("X", 0, 2048), lv), a("CG"), OP.add)
         ts(a("XN"), a("XT"), 255, OP.bitwise_and)
-        act(a("LR", 32, 47), lv) if CFG.get("us") else cp(a("LR", 32, 47), lv)
+        cp(a("LR", 32, 47), lv)
         tt(a("LR", 0, 15), a("LR", 32, 47), a("JJ", 0, 15), OP.subtract)
         tt(a("ZM", 0, 96), a("XN", 0, 96), a("XN", 96, 192), OP.max)
         tt(a("ZM", 96, 144), a("ZM", 0, 48), a("ZM", 48, 96), OP.max)
@@ -536,23 +517,30 @@ def program():
             act(a("ZZ", 48, 96), ind(a("LD1"), a("LI", 10, 13)))
             dma("S", ("yz", (ALL, ALL)), a("ZZ", 48, 96), 2500)
 
-    def start(h, m0, t):
-        ms(a2("SM" + h, 1, 5), 0.0)
+    def start(h, m0, t, first):
         ms(a2("JQ" + h, 1, 5), 80.0)
-        if m0[0] != "MC" + h:
+        if first:
             cp(a3("MC" + h, 0, 1), m0)
-        cp(a2("SM" + h, 0, 1), m0)
-        ts(a2("JQ" + h, 0, 1), t, col("cf", 23) if SCAN else 0.0, OP.add)
-        act(a3("M" + h, 0, 1), m0)
+            cp(a2("SM" + h, 0, 1), m0)
+        else:
+            ms(a2("SM" + h, 4, 5), 0.0)
+        cp(a2("JQ" + h, 0, 1), t)
+        act(a3("M" + h, 0, 1), m0, AF.Identity, bias=-2048.0)
         act(a3("M" + h, 5, 6), t)
-        rows(h, one=CFG["one1"])
+        rows(h, first, True)
 
     def new_lanes(h):
-        n, MC, LB = "n" + h, "MC" + h, PPS[int(h)]
-        act(a("XG" + h), ind(a("X", 0, 2048), a("L" + h, 0, 8)))
+        n, MC, LB, QB = "n" + h, "MC" + h, PPS[int(h)], WP[int(h)]
+        (cp if h == "1" else act)(a("XG" + h), ind(a("X", 0, 2048), a("L" + h, 0, 8)))
         if h == "0":
             act(a("XG0", 0, 48), ind(a("LD0"), a("LI", 10, 13)))
-        mm(a(LB, 64, 72), a("XG" + h), a("WD"))
+        mm(a(QB, 0, 8), a("BD"), a("WD", 8, 16), True, False)
+        for b in range(16):
+            mm(a(QB, 0, 8), a("BW", 15 - b, 143 - b), a("XG" + h, b, 128, 16), False, b == 15)
+        ts(a(n, 96, 104), a(QB, 0, 8), 37.0, OP.mult, col("cf", 38) if h == "1" else rr, OP.add)
+        ts(a(n, 104, 112), a(n, 96, 104), 2047, OP.bitwise_and)
+        cp(a("L" + h, 16, 24), a(n, 104, 112))
+        mm(a(LB, 64, 72), a("XG" + h), a("WD", 0, 8))
 
         def k(c):
             return a(n, 8 * c, 8 * c + 8)
@@ -564,35 +552,46 @@ def program():
         tt(k(2), k(1), k(1), OP.mult)
         ts(k(4), k(2), col("cf", 60 + int(h)), OP.add)
         ts(k(5), k(4), 5, OP.logical_shift_right, 63, OP.bitwise_and)
-        start(h, a3(MC, 0, 1), k(5))
+        start(h, a3(MC, 0, 1), k(5), False)
+
+    def mark(k0, e):
+        for o in ops[k0:]:
+            o["step"] = e
 
     low = (slice(0, 32), ALL)
-    cp(("CF0", low), ("BG", low))
-    mm(a(EB[0], 0, 32), ("CF0", low), ("IH", (slice(0, 32), slice(0, 32))))
+    cp(("CB", low), ("BG", low))
+    mm(a(EB[0], 0, 32), ("CB", low), ("IH", (slice(0, 32), slice(0, 32))))
     cp(a("s0", 128, 160), a(EB[0], 0, 32))
     for h in "01":
-        start(h, a("s0", 128 + int(h), 144, 2), a("s0", 144 + int(h), 160, 2))
+        start(h, a("s0", 128 + int(h), 144, 2), a("s0", 144 + int(h), 160, 2), True)
     for rnd in range(2):
         order = "01" if rnd == 0 else "10"
         for h in order:
             if rnd:
                 new_lanes(h)
             ms(a("YO" + h), 1 << 21)
-            prep(h, 1, CFG["g1"] if h == order[0] else CFG["gv"])
+            k0 = len(ops)
+            prep(h, 1, FIRST[rnd] if h == order[0] else 0, rnd == 1)
+            mark(k0, 1)
         for e in range(1, 7):
             for h in order:
+                k0 = len(ops)
                 heavy(h, e)
+                if e == 6:
+                    mark(k0, e)
                 post(h, e, rnd)
                 if e < 6:
-                    prep(h, e + 1, CFG["g6"] if e == 5 and h == order[1] else CFG["gv"])
+                    mark(k0, e)
+                    k0 = len(ops)
+                    prep(h, e + 1, LAST[order.index(h)] if e == 5 else 0)
+                    mark(k0, e + 1)
             if rnd == 0 and e == 1:
                 late_constants()
         commit(rnd)
     return ops
 
 
-def plan():
-    ops = program()
+def depend(ops):
     hist = {}
     prevg = []
     for k, o in enumerate(ops):
@@ -625,99 +624,152 @@ def plan():
             deps.setdefault(o["after"], False)
         deps.pop(k, None)
         o["deps"] = deps
+
+
+def kind(o):
+    x = o["args"][1 if o["eng"] == "P" else 0]
+    if not isinstance(x, tuple):
+        return ""
+    name = x[0].rstrip("01")
+    if name == "n":
+        name += str(x[1][1].start // 32)
+    if name == "W" and x[1][1].start:
+        name = "TG" + (o["args"][2][0] if o["eng"] == "P" else "")
+    if name == "CU" and o["step"] == 1:
+        name = "CU1"
+    if name == "A" and o["call"] == "tensor_tensor":
+        name = "J"
+    return o["eng"] + name + ("" if "step" in o else "_")
+
+
+def plan():
+    ops = program()
+    depend(ops)
     n = len(ops)
+    cost = [o["cost"] for o in ops]
+    tail = [o.get("lat", 0) for o in ops]
+    before = [[(j, cost[j] + (0 if not hard else tail[j] + (SELF if ops[j]["eng"] == o["eng"] and "sem" not in ops[j] else HOP)))
+               for j, hard in o["deps"].items()] for o in ops]
     kids = [[] for _ in range(n)]
-    for k, o in enumerate(ops):
-        for j in o["deps"]:
-            kids[j].append(k)
-
-    def role(o):
-        x = o["args"][1 if o["eng"] == "P" else 0]
-        if not isinstance(x, tuple):
-            return ""
-        name = x[0].rstrip("01")
-        if name == "n":
-            name += str(x[1][1].start // 32)
-        if o["eng"] == "P" and name == "TG":
-            name += o["args"][2][0]
-        if name == "A" and o["call"] == "tensor_tensor":
-            name = "J"
-        return o["eng"] + name
-
-    def lat(j, k):
-        return ops[j].get("lat", 0) + (0 if not ops[k]["deps"][j] else SELF if ops[k]["eng"] == ops[j]["eng"] and "sem" not in ops[j] else HOP)
-
-    def run(prio):
-        left = [len(o["deps"]) for o in ops]
-        ready = [0.0] * n
-        t = [0.0] * n
-        pool = {e: [] for e in "VSPGYR"}
-        free = {e: 0.0 for e in pool}
-        order = {e: [] for e in pool}
-        for k, o in enumerate(ops):
-            if left[k] == 0:
-                pool[o["eng"]].append(k)
-        pick = {}
-        for _ in range(n):
-            best = None
-            for e in pool:
-                if pool[e]:
-                    if e not in pick:
-                        t0 = max(free[e], min(ready[k] for k in pool[e]))
-                        now = sorted((k for k in pool[e] if ready[k] <= t0 + 30), key=lambda k: (prio[k], -k))
-                        k = now[-1]
-                        if e in CFG["look"]:
-                            soon = [j for j in pool[e] if t0 + 30 < ready[j] < t0 + ops[k]["cost"] - 30
-                                    and prio[j] - prio[k] > ready[j] - t0 + 100]
-                            if soon:
-                                j = min(soon, key=lambda j: ready[j])
-                                fit = [i for i in now if t0 + ops[i]["cost"] <= ready[j] + 30]
-                                k = fit[-1] if fit else j
-                                t0 = max(t0, ready[k])
-                        pick[e] = (t0, e, k)
-                    if best is None or pick[e][0] < best[0]:
-                        best = pick[e]
-            t0, e, k = best
-            del pick[e]
-            t[k] = max(free[e], ready[k])
-            free[e] = t[k] + ops[k]["cost"]
-            pool[e].remove(k)
-            order[e].append(k)
-            for c in kids[k]:
-                ready[c] = max(ready[c], free[e] + lat(k, c))
-                left[c] -= 1
-                if left[c] == 0:
-                    pool[ops[c]["eng"]].append(c)
-                    pick.pop(ops[c]["eng"], None)
-        return max(t[k] + ops[k]["cost"] + ops[k].get("lat", 0) for k in range(n)), t, order
-    far = [0.0] * n
-    for k in range(n - 1, -1, -1):
-        far[k] = ops[k]["cost"] + max([far[c] + lat(k, c) for c in kids[k]] + [ops[k].get("lat", 0)])
-    roles = [role(o) for o in ops]
-    if "hook" in CFG:
-        return CFG["hook"](run, far, roles)
-    end, t, order = run([p + CFG["up"].get(x, 0) for p, x in zip(far, roles)])
-    busy = {e: sum(ops[k]["cost"] for k in order[e]) for e in order}
     for k in range(n):
-        ops[k]["t"] = t[k]
-    pos = {}
-    for e in order:
-        for p, k in enumerate(order[e]):
-            pos[k] = p
+        for j, w in before[k]:
+            kids[j].append((k, w))
+    prio = [0.0] * n
+    for k in range(n - 1, -1, -1):
+        prio[k] = max([prio[c] + w for c, w in kids[k]] + [cost[k] + tail[k]])
+    prio = [p + URGE.get(kind(o), 0) for p, o in zip(prio, ops)]
+    left = [len(b) for b in before]
+    ready = [0.0] * n
+    pool = {e: [] for e in "VSPGYR"}
+    free = {e: 0.0 for e in pool}
+    order = {e: [] for e in pool}
+    for k, o in enumerate(ops):
+        if left[k] == 0:
+            pool[o["eng"]].append(k)
+    pick = {}
+    for _ in range(n):
+        best = None
+        for e in pool:
+            if pool[e]:
+                if e not in pick:
+                    t0 = max(free[e], min(ready[k] for k in pool[e]))
+                    now = sorted((k for k in pool[e] if ready[k] <= t0 + 30), key=lambda k: (prio[k], -k))
+                    k = now[-1]
+                    if e in "VS":
+                        soon = [j for j in pool[e] if t0 + 30 < ready[j] < t0 + cost[k] - 30 and prio[j] - prio[k] > ready[j] - t0 + 100]
+                        if soon:
+                            j = min(soon, key=lambda j: ready[j])
+                            fit = [i for i in now if t0 + cost[i] <= ready[j] + 30]
+                            k = fit[-1] if fit else j
+                            t0 = max(t0, ready[k])
+                    pick[e] = (t0, e, k)
+                if best is None or pick[e][0] < best[0]:
+                    best = pick[e]
+        t0, e, k = best
+        del pick[e]
+        t0 = max(free[e], ready[k])
+        free[e] = t0 + cost[k]
+        pool[e].remove(k)
+        order[e].append(k)
+        for c, w in kids[k]:
+            ready[c] = max(ready[c], t0 + w)
+            left[c] -= 1
+            if left[c] == 0:
+                pool[ops[c]["eng"]].append(c)
+                pick.pop(ops[c]["eng"], None)
+
+    def play(order):
+        t = [None] * n
+        at = {e: 0 for e in order}
+        free = {e: 0.0 for e in order}
+        moved = True
+        while moved:
+            moved = False
+            for e, q in order.items():
+                p, f = at[e], free[e]
+                while p < len(q) and all(t[j] is not None for j, w in before[q[p]]):
+                    k = q[p]
+                    t[k] = max([t[j] + w for j, w in before[k]] + [f])
+                    f = t[k] + cost[k]
+                    p += 1
+                if p > at[e]:
+                    at[e], free[e], moved = p, f, True
+        if None in t:
+            return 1e12, None
+        return max(t[k] + cost[k] + tail[k] for k in range(n)), t
+    end, t = play(order)
+    tried = set()
+    for _ in range(POLISH):
+        place = {k: p for q in order.values() for p, k in enumerate(q)}
+        k = max(range(n), key=lambda k: t[k] + cost[k] + tail[k])
+        move = None
+        while move is None:
+            j = next((j for j, w in before[k] if abs(t[j] + w - t[k]) < 1), None)
+            if j is None:
+                if place[k] == 0:
+                    break
+                q = order[ops[k]["eng"]]
+                j = q[place[k] - 1]
+                due = max([t[i] + w for i, w in before[k]] + [0.0])
+                p = place[k]
+                while p > 0 and t[q[p - 1]] >= due - 130 and q[p - 1] not in ops[k]["deps"]:
+                    p -= 1
+                for to in (p, place[k] - 1):
+                    if to < place[k] and (k, q[to]) not in tried and q[to] not in ops[k]["deps"]:
+                        move = (k, to)
+                        break
+            k = j
+        if move is None:
+            break
+        k, to = move
+        e = ops[k]["eng"]
+        tried.add((k, order[e][to]))
+        q = list(order[e])
+        q.insert(to, q.pop(place[k]))
+        new = dict(order)
+        new[e] = q
+        v, tv = play(new)
+        if v < end - 1:
+            end, t, order = v, tv, new
+    busy = {e: sum(cost[k] for k in order[e]) for e in order}
+    pos = {k: p for q in order.values() for p, k in enumerate(q)}
     need = set()
-    for e in "VSPGY":
-        seen = {}
-        for k in order[e]:
-            last = {}
-            for j, hard in ops[k]["deps"].items():
-                if hard:
-                    key = ops[j].get("sem", ops[j]["eng"])
-                    if pos[j] > seen.get(key, -1) and pos[j] > pos.get(last.get(key), -1):
-                        last[key] = j
-            for key in last:
-                seen[key] = pos[last[key]]
-                need.add(last[key])
-            ops[k]["waits"] = list(last.values())
+    seen = {e: {} for e in order}
+    known = {}
+    for k in sorted(range(n), key=lambda k: (t[k], pos[k])):
+        o = ops[k]
+        o["t"] = t[k]
+        o["waits"] = []
+        mine = seen[o["eng"]]
+        for j in sorted((j for j, hard in o["deps"].items() if hard), key=lambda j: -t[j]):
+            key = ops[j].get("sem", ops[j]["eng"])
+            if pos[j] > mine.get(key, -1) and o["eng"] != "R":
+                o["waits"].append(j)
+                need.add(j)
+                mine[key] = pos[j]
+                for x, p in known[j].items():
+                    mine[x] = max(mine.get(x, -1), p)
+        known[k] = dict(mine) if o["eng"] != "R" else {}
     total = {}
     for e in "VSPG":
         c = 0
@@ -741,7 +793,7 @@ def rank_program(g, core, T, topo):
     ops, order, total, end, busy = PLAN[0]
     n = len(T.cores)
     peers = [T.cores[(rank + 1 + m) % n] for m in range(n - 1)]
-    per = 2
+    per = 2 * len(topo.engines(core, peers[0]))
 
     def real(x):
         if not isinstance(x, tuple):
@@ -758,7 +810,7 @@ def rank_program(g, core, T, topo):
             for j in o["waits"]:
                 p = ops[j]
                 if p["eng"] == "R":
-                    q.wait_ge(T.sem[p["sem"]], per * (n - 1))
+                    q.wait_ge(T.sem[p["sem"]], per)
                 elif "sem" in p:
                     q.wait_ge(T.sem[p["sem"]], 16)
                 else:
@@ -767,14 +819,16 @@ def rank_program(g, core, T, topo):
             kw = {key: real(v) for key, v in o["kw"].items()}
             if c == "send":
                 z = str(args[0])
-                tr = []
-                for m, d in enumerate(peers):
-                    rid, pid = topo.addr(d, core)
-                    eng = topo.engines(core, d)[per * m:per * m + per]
-                    tr.append(RemoteDMATransfer(dst_ids=[DstId(rid=rid, pnc=pid)], dma_engine_mask=sum(1 << x for x in eng),
-                                                remote_sem=T.sem["arr" + z], src=T["ZS" + z][:, 16 * m:16 * m + 16],
-                                                dst=T["LD" + z][:, 16 * m:16 * m + 16]))
-                g.remote_dma_fused(tr, local_sem=T.sem.sent)
+                for group in ((0, 1), (2,)):
+                    tr = []
+                    for i, m in enumerate(group):
+                        rid, pid = topo.addr(peers[m], core)
+                        eng = topo.engines(core, peers[m])
+                        eng = eng[i * len(eng) // len(group):(i + 1) * len(eng) // len(group)]
+                        tr.append(RemoteDMATransfer(dst_ids=[DstId(rid=rid, pnc=pid)], dma_engine_mask=sum(1 << x for x in eng),
+                                                    remote_sem=T.sem["arr" + z], src=T["ZS" + z][:, 16 * m:16 * m + 16],
+                                                    dst=T["LD" + z][:, 16 * m:16 * m + 16]))
+                    g.remote_dma_fused(tr, local_sem=T.sem.sent)
                 continue
             if c == "dma_start":
                 q.dma_start(*args).then_inc(T.sem[o["sem"]], 16)
@@ -782,8 +836,8 @@ def rank_program(g, core, T, topo):
             f = {"tensor_copy": lambda: q.tensor_copy(*args), "tensor_tensor": lambda: q.tensor_tensor(*args),
                  "tensor_scalar": lambda: q.tensor_scalar(*args), "memset": lambda: q.memset(*args),
                  "tensor_tensor_scan": lambda: q.tensor_tensor_scan(*args), "activation": lambda: q.activation(*args, **kw),
-                 "matmul": lambda: q.matmul(*args), "iota": lambda: q.iota(*args, **kw),
-                 "affine_select": lambda: q.affine_select(*args)}[c]()
+                 "tensor_reduce": lambda: q.tensor_reduce(*args), "matmul": lambda: q.matmul(*args),
+                 "iota": lambda: q.iota(*args, **kw), "affine_select": lambda: q.affine_select(*args)}[c]()
             if "mark" in o:
                 f.then_inc(T.sem["c" + e], 1)
     for o in ops:
@@ -792,4 +846,4 @@ def rank_program(g, core, T, topo):
     for s in total:
         if total[s]:
             g.wait_ge(T.sem[s], total[s])
-    g.wait_ge(T.sem.sent, 2 * per * (n - 1))
+    g.wait_ge(T.sem.sent, 2 * per)

import numpy as np
from concourse.bass import DstId, RemoteDMATransfer
from concourse.mybir import AluOpType as OP, ActivationFunctionType as AF, AxisListType as AX

F, H, B, I, U = "float32", "float16", "bfloat16", "int32", "uint16"
LV = 1 << 19
SC = float(1 << 22)
DEPTH = {1: 4, 2: 3, 3: 3, 4: 2, 5: 1, 6: 0}
GC, PE = 1.56, 0.5
HOP, SELF = 210, 200
CUTS, CUTS1 = (0, 64, 96), (0, 32, 64, 96)
FIRST, LAST = (48, 64), (8, 32)
URGE = {"SG": -4650, "SW": 700, "STG": 850, "SRW": 1050, "SCG_": -2100,
        "VCF": 1500, "VJ": -800, "VJQ": -1450, "VEQ": 50, "VP": -3250, "VCU": -650, "VCU1": -900, "VFU_": 1450, "VBB_": -650,
        "Vn1_": 550, "VMC_": 3650, "VSM_": -1400, "VJQ_": -1100, "VLR_": -3550, "Vcf_": 200, "VXT_": -500, "VL_": 500,
        "PG": -550, "PA": -1000, "PEQ": 6000, "PSN": -1950, "PTGRET": 1050, "PBIG_": -800, "PIB_": 650, "PXG_": 1700}
POLISH = 500


def _scratch():
    s = {}

    def sb(n, dt, *sh):
        s[n] = ("sbuf", [128] + list(sh), dt)
    sb("X", B, 2304); sb("NB", I, 2304); sb("WT", B, 768); sb("TH", B, 384); sb("CH", B, 320); sb("SW", B, 64)
    sb("PA", I, 64); sb("PB", I, 64); sb("WI", I, 4); sb("BG", I, 128); sb("CB", H, 128)
    sb("q1", I, 192); sb("q4", F, 64); sb("ci", I, 28); sb("cf", F, 80); sb("io", F, 200); sb("gi", B, 9, 20)
    sb("t1", F, 160); sb("t2", F, 160); sb("t3", F, 160); sb("own", B, 9, 20); sb("r16", F, 16)
    sb("IH", H, 128); sb("NI", H, 128); sb("IB", B, 128); sb("BD", B, 128); sb("SEL", H, 768); sb("SN", H, 512)
    sb("BIG", H, 288); sb("I2", H, 128); sb("RI", H, 160); sb("RN", B, 160); sb("RS", B, 16); sb("RET", B, 9, 20)
    sb("RP", B, 8, 20); sb("KN", F, 32); sb("KL", F, 32); sb("KI", I, 32); sb("LI", U, 16); sb("UT", H, 256)
    sb("WD", B, 16); sb("BW", B, 144); sb("JJ", F, 16); sb("CJ", B, 240); sb("pw", F, 96); sb("RZ", B, 240)
    for h in "01":
        sb("G" + h, B, 2048); sb("A" + h, B, 2048); sb("CU" + h, U, 128); sb("CF" + h, H, 128); sb("W" + h, B, 256)
        sb("TG" + h, B, 128); sb("EQ" + h, B, 512); sb("P" + h, F, 160); sb("BB" + h, F, 160); sb("RK" + h, F, 640)
        sb("RW" + h, H, 256); sb("L" + h, U, 24); sb("SM" + h, H, 17, 8); sb("JQ" + h, H, 17, 8); sb("M" + h, H, 8, 16)
        sb("M2" + h, H, 8, 16); sb("FU" + h, H, 128); sb("MC" + h, I, 8, 5); sb("YO" + h, I, 32)
        sb("s" + h, F, 160); sb("n" + h, I, 128); sb("VA" + h, F, 8, 6); sb("XG" + h, B, 128)
        sb("ZS" + h, B, 48); sb("LD" + h, B, 48)
    sb("MX", F, 272); sb("MY", F, 256); sb("LN", U, 4); sb("MS", H, 48); sb("BR", H, 6, 80)
    sb("LR", F, 64); sb("LU", U, 2, 16); sb("OF", U, 16); sb("EW", B, 15, 240)
    sb("GO", H, 48); sb("CG", B, 240); sb("XT", I, 240); sb("XN", I, 240); sb("ZM", B, 144)
    sb("NG", H, 192); sb("HG", F, 48); sb("DH", H, 96); sb("ND", I, 192); sb("ZZ", B, 96)
    for k in range(8):
        s["ps%d" % k] = ("psum", [128, 512], F)
    return s


SCRATCH = _scratch()
SEMAPHORES = ["cV", "cS", "cP", "cG", "sent", "arr0", "arr1"] + ["d%d" % k for k in range(20)]
ALL = slice(None)
WP, EB, PPS, MBS = ("ps0", "ps1"), ("ps2", "ps3"), ("ps4", "ps5"), ("ps6", "ps7")


def a(n, lo=None, hi=None, st=None):
    return (n, (ALL, slice(lo, hi, st)))


def ax(n, *ix):
    return (n, (ALL,) + tuple(slice(*i) if isinstance(i, tuple) else i for i in ix))


def a3(n, lo, hi):
    return (n, (ALL, ALL, slice(lo, hi)))


def a2(n, lo, hi):
    return (n, (ALL, slice(1, 17, 2), slice(lo, hi)))


def col(n, c):
    return a(n, c, c + 1)


def ind(win, off):
    return ("*", win, off)


_SPANS = {}


def _span(ap):
    key = repr(ap)
    if key not in _SPANS:
        n, ix = ap
        sh = SCRATCH[n][1][1:]
        el = np.arange(int(np.prod(sh))).reshape(sh)[tuple(ix[1:])].reshape(-1)
        bits = 0
        for e in el.tolist():
            bits |= 1 << e
        if SCRATCH[n][0] == "sbuf":
            bits = bits << 4096 if ix[0].start else bits if ix[0].stop == 16 else bits | bits << 4096
        _SPANS[key] = (n, bits, len(el))
    return _SPANS[key]


def program():
    ops = []
    nd = [0]

    def rec(eng, call, args, outs, ins, cost, **kw):
        ops.append(dict(eng=eng, call=call, args=args, outs=outs, ins=ins, cost=cost, kw=kw))

    def parts(ap):
        return [ap[1], ap[2]] if ap[0] == "*" else [ap]

    def cnt(ap):
        return 16 * _span(ap[2])[2] if ap[0] == "*" else _span(ap)[2]

    def two(*aps):
        return all(p[0] != "*" and SCRATCH[p[0]][2] in (H, B, U) for p in aps)

    def vcost(out, src, m):
        if out[0] == "*":
            return 60 + 3.5 * cnt(out)
        if src[0] == "*":
            return 60 + GC * cnt(src)
        return max(64, m * cnt(src))

    def sides(out, *srcs):
        o = parts(out)
        return o[:1], o[1:] + [p for s in srcs if isinstance(s, tuple) for p in parts(s)]

    def cp(out, src):
        o, i = sides(out, src)
        rec("V", "tensor_copy", (out, src), o, i, vcost(out, src, 0.5 if two(out, src) else 1))

    def tt(out, x, y, op):
        o, i = sides(out, x, y)
        rec("V", "tensor_tensor", (out, x, y, op), o, i, vcost(out, x, 1 if "ps" in (x[0][:2], y[0][:2]) else 2))

    def ts(out, x, s1, op0, s2=None, op1=None):
        o, i = sides(out, x, s1, s2)
        rec("V", "tensor_scalar", (out, x, s1, s2, op0) + ((op1,) if op1 is not None else ()), o, i,
            vcost(out, x, 0.5 if two(out, x) else 1))

    def scan(out, d0, d1, init, op0, op1):
        rec("V", "tensor_tensor_scan", (out, d0, d1, init, op0, op1), [out], [d0, d1], vcost(out, d0, 1))

    def ms(out, v):
        rec("V", "memset", (out, v), [out], [], max(64, cnt(out) * (0.5 if two(out) else 1)))

    def act(out, src, f=AF.Copy, **kw):
        o, i = sides(out, src, *[kw[k] for k in kw if k != "accum_out"])
        if "accum_out" in kw:
            o = o + [kw["accum_out"]]
        rec("S", "activation", (out, src, f), o, i, 78 + GC * cnt(src) if src[0] == "*" else max(64, cnt(src)), **kw)

    def mm(out, l, r, st=True, sp=True):
        rec("P", "matmul", (out, l, r, st, sp), [out], [l, r], PE * max(min(64, cnt(l)), cnt(r)))

    def iota(out, pat, base=0, cm=0):
        kw = {} if SCRATCH[out[0]][2] == I else {"allow_small_or_imprecise_dtypes": True}
        rec("G", "iota", (out, pat, base, cm), [out], [], 160 + 2 * cnt(out), **kw)

    def gcopy(out, src):
        rec("G", "affine_select", (out, src, [[0, cnt(src)]], OP.is_ge, 0.0, 0, 0), [out], [src], 210 + 2 * cnt(src))

    def dma(eng, out, src, cost):
        rec(eng, "dma_start", (out, src), [out] if out[0] in SCRATCH else [], [src] if src[0] in SCRATCH else [], 70)
        ops[-1]["sem"] = "d%d" % nd[0]
        ops[-1]["lat"] = cost
        nd[0] += 1

    ms(a("PB"), 0)
    k0 = len(ops)
    dma("Y", ("BG", (slice(0, 16), ALL)), ("beg", (ALL, ALL)), 2600)
    dma("Y", ("BG", (slice(16, 32), ALL)), ("tau", (ALL, ALL)), 2600)
    dma("Y", a("NB", 0, 2048), ("nb", (ALL, ALL)), 6000)
    dma("Y", a("CH"), ("chg", (ALL, ALL)), 7000)
    dma("Y", a("SW", 0, 64), ("swp", (ALL, ALL)), 7000)
    dma("Y", col("WI", 0), ("wt", (ALL, ALL)), 7000)
    k1 = len(ops)
    dma("S", a("WT", 320, 384), ("feat", (ALL, slice(0, 64))), 3000)
    dma("S", a("WT", 64, 256), ("feat", (ALL, slice(64, 256))), 3000)
    dma("S", a("PA"), ("par", (ALL, ALL)), 2800)
    dma("S", a("X", 0, 2048), ("x", (ALL, ALL)), 6200)
    dma("S", ("PB", (slice(0, 124), ALL)), ("par", (slice(4, 128), ALL)), 3500)
    for k in range(k0 + 1, len(ops)):
        if k != k1:
            ops[k]["after"] = k - 1

    def io(lo, hi, st=None):
        return a("io", 32 + lo, 32 + hi, st)
    iota(col("ci", 0), [[0, 1]], 0, 1)
    iota(a("io"), [[1, 200]], -32)
    iota(a("RK0", 0, 128), [[8, 2], [16, 8], [1, 8]])
    iota(a("t1", 0, 128), [[16, 8], [0, 16]])
    iota(("gi", (ALL,)), [[16, 9], [0, 20]])
    iota(a("KN"), [[0, 8], [LV // 32, 4]], LV // 32)
    iota(a("KI"), [[0, 8], [4096, 4]])
    for c, m in enumerate((15, 112, 12, 120)):
        ts(col("ci", 1 + c), col("ci", 0), m, OP.bitwise_and)
    cp(a("cf", 0, 5), a("ci", 0, 5))
    pp, rr, pg = col("cf", 0), col("cf", 1), col("cf", 2)
    ts(a("BIG", 144, 288), io(-7, 137), col("cf", 4), OP.is_equal)
    ts(a("I2"), a("RK0", 0, 128), pp, OP.is_equal)
    ts(a("r16"), io(0, 16), rr, OP.is_equal)

    def r(k):
        return col("r16", k)
    ts(a("IH"), io(0, 128), pp, OP.is_equal)
    ts(a("BD"), a("t1", 0, 128), pg, OP.is_equal)
    ts(a("cf", 76, 80), a("r16", 0, 4), 1.0, OP.mult, r(15), OP.add)
    for i in range(4):
        act(a("SN", 128 * i, 128 * i + 128), a("BD"), AF.Identity, scale=col("cf", 76 + i))
    ts(a("q1", 0, 64), a("PA"), 0xF00, OP.bitwise_and)
    ts(a("q1", 64, 128), a("PB"), 0xFF, OP.bitwise_and)
    ts(a("q1", 128, 192), a("PA"), 3, OP.bitwise_and)
    ts(col("cf", 6), rr, 4.5, OP.is_lt)
    ts(col("cf", 7), rr, 4.5, OP.is_gt)
    act(a("q4"), a("q1", 128, 192), AF.Identity, scale=col("cf", 6))
    act(a("s0", 0, 64), a("q1", 64, 128), AF.Identity, scale=col("cf", 7))
    tt(a("s0", 64, 128), a("q4"), a("q1", 0, 64), OP.add)
    tt(a("q4"), a("s0", 64, 128), a("s0", 0, 64), OP.add)
    tt(a("cf", 24, 28), a("r16", 5, 9), a("r16", 9, 13), OP.add)
    act(col("cf", 12), col("cf", 27))
    tt(a("cf", 9, 12), a("cf", 24, 27), a("r16", 2, 5), OP.add)
    ts(col("cf", 5), r(14), r(0), OP.add)
    act(a("cf", 16, 21), io(1, 6), AF.Identity, scale=r(13), bias=col("cf", 5))
    act(col("cf", 21), col("cf", 16))
    act(col("cf", 28), r(15), AF.Identity, scale=-16384.0, bias=col("cf", 20))
    for b in (5, 1, 2, 3, 0, 4):
        j = {1: 2, 2: 3, 3: 4, 5: 1}.get(b)
        act(a("TH", 64 * b, 64 * b + 64), a("q4"), AF.Identity, scale=col("cf", 8 + j) if j else 0.0,
            bias=col("cf", 16 + b if j else 28))
    ms(a("WT", 0, 64), 0.0); ms(a("WT", 256, 320), 0.0)
    e0, e1 = a("EQ0", 0, 384), a("EQ1", 0, 384)
    mm(a(WP[0], 0, 384), a("BD"), a("WT", 0, 384))
    act(e0, a(WP[0], 0, 384))
    tt(e1, a(WP[0], 0, 384), e0, OP.subtract)
    act(a("IB"), a("IH"))
    act(a("TG0"), a("IH"), AF.Identity, scale=r(1))
    act(a("TG1"), a("IH"), AF.Identity, scale=r(0))
    for i, (d, x) in enumerate((("IB", a("TH")), ("TG0", e0), ("TG1", e1))):
        mm(a(WP[1], 0, 384), a(d), x, i == 0, i == 2)
    ts(col("cf", 29), pg, 1.25, OP.mult, rr, OP.subtract)
    ts(a("RI"), io(-19, 141), col("cf", 29), OP.is_equal)
    act(a("RN", 0, 160), a("RI"), AF.Identity, scale=-SC * 65536)
    ts(a("RS", 0, 8), io(0, 128, 16), pg, OP.is_equal, SC, OP.mult)
    act(a("RS", 8, 16), a("RS", 0, 8), AF.Identity, scale=-2.0)
    ts(("own", (ALL,)), ("gi", (ALL,)), pg, OP.is_equal)
    ts(col("cf", 30), col("cf", 7), r(13), OP.subtract, r(14), OP.subtract)
    ts(col("cf", 15), r(0), r(1), OP.add)
    ts(col("cf", 22), col("cf", 30), col("cf", 15), OP.add)
    ts(a3("RET", 0, 4), a3("own", 0, 4), col("cf", 15), OP.mult, SC, OP.mult)
    ts(a3("RET", 4, 20), a3("own", 4, 20), col("cf", 22), OP.mult, SC, OP.mult)
    ts(col("cf", 32), col("cf", 6), col("cf", 15), OP.subtract, 4096.0, OP.mult)
    act(col("cf", 33), r(13), AF.Identity, scale=float(LV), bias=col("cf", 32))
    act(col("cf", 31), r(14), AF.Identity, scale=16384.0)
    iota(a("t2", 0, 128), [[0, 8], [1, 16]])
    act(a("t3", 0, 128), a("t2", 0, 128), AF.Identity, scale=col("cf", 31), bias=col("cf", 33))
    ms(ax("RP", ALL, (0, 4)), 0.0)
    tt(ax("RP", ALL, (4, 20)), a("t3", 0, 128), ax("own", (0, 8), (4, 20)), OP.mult)
    act(a("KN"), a("KN"), AF.Identity, scale=32.0)
    act(col("cf", 14), col("cf", 3), AF.Identity, scale=5.0, bias=19.0)
    ts(a("LI", 0, 2), io(0, 2), 80.0, OP.mult, col("cf", 14), OP.add)
    act(a("WT", 384, 768), a(WP[1], 0, 384))
    for h in "01":
        for n in ("SM", "JQ", "M"):
            ms((n + h, (ALL,)), 0.0)
        ms(a3("M" + h, 15, 16), 2048.0)

    def late_constants():
        for i in range(6):
            act(a("SEL", 128 * i, 128 * i + 128), a("BD"), AF.Identity, scale=r(i))
        ts(a("LI", 2, 10), io(0, 8), 20.0, OP.mult, 19.0, OP.add)
        ts(a("BIG", 0, 144), io(-15, 129), pg, OP.is_equal, 0.0625, OP.mult)
        act(a("NI"), a("IH"), AF.Identity, scale=-1.0)
        act(a("KL"), a("KN"))
        iota(a("KL", 0, 32, 4), [[0, 8]], -int(SC))
        iota(a("KL", 1, 32, 4), [[0, 8]], 5 * LV // 2)
        iota(("VA0", (ALL,)), [[0, 8], [0, 6]]); iota(("VA1", (ALL,)), [[0, 8], [0, 6]])
        ms(("M20", (ALL,)), 0.0); ms(("M21", (ALL,)), 0.0)
        ts(a("UT", 0, 128), io(0, 128), pp, OP.is_ge)
        ms(a("UT", 128, 256), 1.0)
        act(col("cf", 34), col("WI", 0), AF.Identity, scale=1.0 / SC)
        act(a("WD", 0, 8), a("RS", 0, 8), AF.Identity, scale=col("cf", 34))
        act(col("cf", 39), col("WI", 0), AF.Identity, scale=16.0)
        act(a("BW"), a("BIG", 0, 144), AF.Identity, scale=col("cf", 39))
        iota(a("ci", 12, 20), [[pow(37, -1, 128), 8]])
        ts(a("ci", 20, 28), a("ci", 12, 20), 127, OP.bitwise_and)
        act(a("WD", 8, 16), a("ci", 20, 28))
        act(col("cf", 38), rr, AF.Identity, bias=128.0)
        iota(col("cf", 35), [[0, 1]], 128, 1)
        iota(a("cf", 60, 62), [[4096, 2]], 0, 32)
        act(col("cf", 36), rr, AF.Identity, bias=0.5)
        act(a("cf", 40, 43), io(0, 3), AF.Identity, scale=16.0, bias=col("cf", 36))
        iota(a("t2", 0, 48), [[0, 48]])
        act(a("t1", 0, 48), a("t2", 0, 48), AF.Identity, bias=0.25)
        scan(a("pw", 0, 48), a("t1", 0, 48), a("t2", 0, 48), 4.0, OP.mult, OP.add)
        act(a("pw", 48, 96), a("pw", 0, 48), AF.Identity, scale=2.0)
        tt(a("t3", 0, 16), a("pw", 0, 16), a("r16"), OP.mult)
        act(a("t3", 16, 32), a("t3", 0, 16), AF.Identity, accum_out=col("t3", 32))
        act(a("cf", 44, 47), a("pw", 0, 48, 16), AF.Identity, scale=col("t3", 32))
        act(col("cf", 37), rr, AF.Identity, bias=2048.0)
        act(a("JJ"), io(0, 16), AF.Identity, scale=16.0, bias=col("cf", 37))
        iota(a("CJ"), [[0, 48], [4, 5]])
        iota(a("RZ"), [[0, 240]], 1)
        iota(a("RZ", 0, 240, 5), [[0, 48]])
        act(col("cf", 8), col("cf", 6), AF.Identity, scale=-1.0)
        act(a("MX", 256, 272), io(0, 16), AF.Identity, scale=0.0, bias=col("cf", 8))
        ts(a("ci", 6, 9), a("cf", 40, 43), -1.5, OP.add, 1.0 / 3, OP.mult)
        act(a("cf", 48, 51), a("ci", 6, 9), AF.Identity, scale=-47.0, bias=-8.0)
        act(a("cf", 52, 55), a("cf", 40, 43), AF.Identity, scale=16.0)
        tt(a("cf", 56, 59), a("cf", 48, 51), a("cf", 52, 55), OP.add)
        cp(a("LI", 10, 13), a("cf", 56, 59))

    def turn(bank, lo, name):
        mm(a(bank, lo, lo + 64), (name, (ALL, slice(1, 17))), a("I2", 0, 64), True, False)
        mm(a(bank, lo, lo + 64), (name, (ALL, slice(0, 16))), a("I2", 64, 128), False, True)

    def to_list(h, bank, lo, hi):
        for b in range(8):
            mm(a(bank, 256, 256 + hi - lo), a("BIG", 151 - b, 279 - b), a("RW" + h, 8 * lo + b, 8 * hi, 8), b == 0, b == 7)
        cp(a("L" + h, lo, hi), a(bank, 256, 256 + hi - lo))

    def rows(h, parents, templates):
        RB, MB = PPS[int(h)], MBS[int(h)]
        if parents:
            turn(RB, 0, "SM" + h)
            act(a("RW" + h, 0, 64), a(RB, 0, 64))
            to_list(h, RB, 0, 8)
        if templates:
            turn(MB, 0, "JQ" + h)
            mm(a(MB, 64, 192), ("M" + h, (ALL,)), a("IH"))
            act(a("RW" + h, 64, 256), a(MB, 0, 192))
            to_list(h, RB, 8, 16)

    def both_lists(h):
        RB, MB = PPS[int(h)], MBS[int(h)]
        turn(RB, 64, "JQ" + h)
        turn(RB, 0, "SM" + h)
        act(a("RW" + h, 0, 128), a(RB, 0, 128))
        to_list(h, RB, 0, 16)
        mm(a(MB, 0, 128), ("M" + h, (ALL,)), a("IH"))
        act(a("RW" + h, 128, 256), a(MB, 0, 128))

    def prep(h, e, gv, direct=False):
        PP, MB, Wp = PPS[int(h)], MBS[int(h)], WP[int(h)]
        cp(a("CU" + h), ind(a("NB", 0, 2048), a("L" + h, 16, 24) if direct else a("L" + h, 0, 8)))
        act(a("W" + h, 0, 128), ind(a("WT", 0, 384), a("L" + h, 8, 16)))
        act(a("W" + h, 128, 256), ind(a("WT", 384, 768), a("L" + h, 8, 16)))
        for q in range(4):
            mm(a(Wp, q, 512, 4), a("IB"), a("W" + h, 0, 128))
        cuts = [c for c in (CUTS1 if e == 1 else CUTS) if c < 128 - gv] + [128 - gv]
        for lo, hi in zip(cuts, cuts[1:]):
            act(a("G" + h, 16 * lo, 16 * hi), ind(a("X", 0, 2048), a("CU" + h, lo, hi)))
            ops[-1]["stage"] = 1
        for lo in range(128 - gv, 128, 32):
            hi = min(128, lo + 32)
            cp(a("G" + h, 16 * lo, 16 * hi), ind(a("X", 0, 2048), a("CU" + h, lo, hi)))
        cp(a("CF" + h), a("CU" + h))
        ne = min(e, 4)
        for i in range(ne):
            mm(a(MB, 128 * i, 128 * i + 128), a("SN", 128 * i, 128 * i + 128), a("RW" + h, 128, 256))
        for i in range(ne):
            tt(a("EQ" + h, 128 * i, 128 * i + 128), a("CF" + h), a(MB, 128 * i, 128 * i + 128), OP.is_equal)
        mm(a(PP, 0, 160), a("CF" + h), a("RI"), True, False)
        mm(a(PP, 0, 160), a("W" + h, 128, 256), a("RP"), False, True)
        act(a("P" + h), a(PP, 0, 160))
        for rk in range(2, DEPTH[e - 1] + 2 if e > 1 else 0):
            src = a("RK" + h, 160 * (rk - 2) + 20 - rk, 160 * (rk - 1), 20)
            if e > 4 and rk == 2:
                tt(a("P" + h, 3, 160, 20), src, a("s" + h, 96, 104), OP.max)
            else:
                gcopy(a("P" + h, 5 - rk, 160, 20), src)

    def heavy(h, e):
        E, Wp = EB[int(h)], WP[int(h)]
        k0 = len(ops)
        mm(a(E, 0, 180), a("W" + h, 128, 256), a("RET"), True, False)
        for i in range(min(e, 4)):
            mm(a(E, 0, 160), a("EQ" + h, 128 * i, 128 * i + 128), a("RN"), False, False)
        for c in range(4):
            for m in range(4):
                tt(a("A" + h, 512 * m + 128 * c, 512 * m + 128 * c + 128), a("G" + h, 512 * c + m, 512 * c + 512, 4),
                   a(Wp, 128 * c, 128 * c + 128), OP.max)
        for k in range(16):
            mm(a(E, 19 - k, 160, 20), a("G" + h, k, 2048, 16), a("RS", 0, 8), False, False)
        for m in range(4):
            for q in range(4):
                mm(a(E, 19 - m - 4 * q, 160, 20), a("A" + h, 512 * m + q, 512 * m + 512, 4), a("RS", 8, 16), False, m + q == 6)
        for o in ops[k0 + 1:-1]:
            o["free"] = k0

    def post(h, e, rnd):
        E = EB[int(h)]
        s, n, MC, BB = "s" + h, "n" + h, "MC" + h, "BB" + h
        scan(a(BB), a(E, 0, 160), a("P" + h), 0.0, OP.max, OP.min)
        tt(a(n, 0, 32), ind(a(BB), a("LI", 0, 2)), a("KL" if e == 6 else "KN"), OP.subtract)
        tt(a(n, 32, 64), a(n, 0, 32), a("YO" + h), OP.min)
        ts(a3(MC, 1, 5), a(n, 32, 64), (1 << 21) | 2047, OP.bitwise_and)
        if e < 6:
            ts(a(n, 64, 96), a(n, 0, 32), 0x3000, OP.bitwise_and)
            tt(a(s, 0, 32), a(n, 64, 96), a("KI"), OP.is_equal)
            tt(a2("SM" + h, 0, 4), a3(MC, 0, 4), a(s, 0, 32), OP.mult)
            ts(a2("JQ" + h, 1, 5), a(n, 0, 32), 0.0, OP.is_ge, 64.0, OP.mult)
            ts(a3("M" + h, 1, 4), a3(MC, 1, 4), 2048.0, OP.min, -2048.0, OP.add)
            both_lists(h)
            ts(a("YO" + h), a(n, 32, 64), (1 << 22) - 1, OP.bitwise_and)
            prev = a(BB)
            for rk in range(2, DEPTH[e] + 2):
                out = a("RK" + h, 160 * (rk - 2), 160 * (rk - 1))
                scan(out, a(E, rk - 1, rk + 159), prev, 0.0, OP.max, OP.min)
                prev = out
            if e >= 4:
                ts(a(s, 96, 104), a(BB, 19, 160, 20), 4.0 * LV, OP.is_ge, 4.5 * LV, OP.mult)
            return
        ts(a("FU" + h), ind(a(BB), a("LI", 2, 10)), 4.0 * LV, OP.is_ge)
        ts(a3("M" + h, 0, 5), a3(MC, 0, 5), 2047.0, OP.min)
        o = 128 * int(h)
        mm(a(MBS[int(h)], 0, 128), ("M" + h, (ALL,)), a("IH"))
        act(a("MX", o, o + 128), a(MBS[int(h)], 0, 128))
        if rnd == 1:
            ts(a3("M2" + h, 1, 5), a3(MC, 1, 5), 4096.0, OP.is_ge, -2048.0, OP.mult)
            mm(a(PPS[int(h)], 0, 128), ("M" + h, (ALL,)), a("IH"), True, False)
            mm(a(PPS[int(h)], 0, 128), ("M2" + h, (ALL,)), a("IH"), False, True)
            act(a("MY", o, o + 128), a(PPS[int(h)], 0, 128))
        if rnd == 0:
            ts(a3("VA" + h, 0, 5), a3(MC, 0, 5), 4096.0, OP.is_lt)
            tt(a(s, 64, 104), a3("VA" + h, 0, 5), a3("VA" + h, 1, 6), OP.subtract)
            tt(a2("SM" + h, 0, 5), a3("M" + h, 0, 5), a(s, 64, 104), OP.mult)
            rows(h, True, False)

    def commit(rnd):
        z = str(rnd)
        MB, RB, LB, PP = WP[0], EB[1], MBS[0], MBS[1]
        if rnd == 0:
            mm(a(MB, 0, 128), a("FU0"), a("UT", 0, 128))
            for c in range(3):
                act(ax("EW", c, (0, 128)), a(MB, 0, 128), AF.Sign, bias=col("cf", 40 + c), scale=-1.0, accum_out=col("cf", 64 + c))
            act(a("cf", 68, 71), a("cf", 64, 67), AF.Identity, scale=0.5, bias=128.0)
            mm(a(WP[1], 0, 128), a("FU0"), a("UT", 128, 256), True, False)
            mm(a(WP[1], 0, 128), a("FU1"), a("UT", 0, 128), False, True)
            for c in range(3):
                act(ax("EW", 3 + c, (0, 128)), a(WP[1], 0, 128), AF.Sign, bias=col("cf", 40 + c), scale=-1.0, accum_out=col("cf", 72 + c))
            for c in range(3):
                ts(col("LN", c), col("cf", 72 + c), 0.5, OP.mult, col("cf", 68 + c), OP.add)
        else:
            for bank in (MB, WP[1]):
                mm(a(bank, 0, 256), a("FU0"), a("UT", 0, 256), True, False)
                mm(a(bank, 128, 256), a("FU1"), a("UT", 0, 128), False, True)
            for c in range(2):
                act(a("RK1", 256 * c, 256 * c + 256), a(MB, 0, 256), AF.Sign, bias=col("cf", 40 + c), scale=-1.0, accum_out=col("cf", 64 + c))
            ts(a("EQ0", 0, 256), a(WP[1], 0, 256), col("cf", 42), OP.is_lt)
            rec("V", "tensor_reduce", (col("cf", 67), a("EQ0", 0, 256), AX.X, OP.add), [col("cf", 67)], [a("EQ0", 0, 256)], 256)
            cp(col("LN", 2), col("cf", 67))
            ts(a("LN", 0, 2), a("cf", 64, 66), 0.5, OP.mult, 128.0, OP.add)
        cp(a("MS"), ind(a("MX"), a("LN", 0, 3)))
        if rnd == 1:
            for j in range(5):
                dma("Y", ("ym", (ALL, slice(256 * j, 256 * j + 256))), ("MY", (slice(j, 128, 16), slice(0, 256))), 2500)
        for j in range(5):
            mm(a(RB, j, 240, 5), a("SEL", 128 * j, 128 * j + 128), a("MS"))
        cp(a("BR", 0, 6, 2), a(RB, 0, 240))
        mm(a(EB[0], 0, 240), a("BD"), a("CJ"), True, False)
        for j in range(5):
            mm(a(EB[0], j, 240, 5), a("SEL", 640, 768), a("MS"), False, j == 4)
        act(a("BR", 1, 6, 2), a(EB[0], 0, 240))
        for b in range(16):
            mm(a(LB, 0, 30), a("BIG", 15 - b, 143 - b), a3("BR", 5 * b, 5 * b + 5), b == 0, b == 15)
        for c in range(3):
            cp(ax("LU", ALL, (c, 15, 3)), a(LB, 10 * c, 10 * c + 10))
        lv, lt = ax("LU", 0, (0, 15)), ax("LU", 1, (0, 15))
        act(a("CG"), ind(a("CH"), lt))
        if rnd == 0:
            act(a("NG"), ind(a("NB", 0, 2048), ax("LU", 0, (0, 12))))
            act(a("HG"), ind(a("SW"), ax("LU", 1, (0, 3))))
        for c in range(3):
            for j in range(5):
                ew = ax("EW", 5 * c + j, (80 * c, 240))
                ts(ew, a("BR", 2 * c, 6, 2), col(LB, 10 * c + j), OP.is_equal, col("cf", 44 + c), OP.mult)
                mm(a(PP, 80 * c, 240), a("BD"), ew, c + j == 0, c + j == 6)
        scan(a("RK0", 0, 240), a("RZ"), a(PP, 0, 240), 0.0, OP.mult, OP.max)
        tt(a("GO"), a("RK0", 4, 240, 5), a("pw", 48, 96), OP.is_lt)
        for b in range(16):
            mm(a(LB, 32, 35), a("BIG", 15 - b, 143 - b), a("GO", b, 48, 16), b == 0, b == 15)
        if rnd == 0:
            act(a("EQ1", 0, 240), ind(a("X", 0, 2048), lv))
            mm(a(WP[0], 0, 240), a("IB"), a("CG"), True, False)
            mm(a(WP[0], 0, 240), a("IB"), a("EQ1", 0, 240), False, True)
            act(a("XT"), a(WP[0], 0, 240))
        else:
            tt(a("XT"), ind(a("X", 0, 2048), lv), a("CG"), OP.add)
        ts(a("XN"), a("XT"), 255, OP.bitwise_and)
        cp(a("LR", 32, 47), lv)
        tt(a("LR", 0, 15), a("LR", 32, 47), a("JJ", 0, 15), OP.subtract)
        tt(a("ZM", 0, 96), a("XN", 0, 96), a("XN", 96, 192), OP.max)
        tt(a("ZM", 96, 144), a("ZM", 0, 48), a("ZM", 48, 96), OP.max)
        tt(a("ZZ", 0, 48), a("ZM", 96, 144), a("XN", 192, 240), OP.max)
        for m in range(3):
            tt(a("ZS" + z, 16 * m, 16 * m + 16), a("ZZ", m, 48, 3), a("GO", m, 48, 3), OP.mult)
        rec("G", "send", (rnd,), [], [a("ZS" + z)], 1500)
        for c in range(3):
            ts(a("LR", 16 + c, 31, 3), a("LR", c, 15, 3), col(LB, 32 + c), OP.mult)
        tt(a("LR", 48, 63), a("LR", 16, 31), a("JJ", 0, 15), OP.add)
        cp(a("OF", 0, 15), a("LR", 48, 63))
        cp(ind(a("X"), a("OF", 0, 15)), a("XN"))
        if rnd == 0:
            D, N = WP[1], RB
            for p in range(2):
                mm(a(D, 48 * p, 48 * p + 48), a("IH"), a("NG", 96 * p + 48, 96 * p + 96), True, False)
                mm(a(D, 48 * p, 48 * p + 48), a("NI"), a("NG", 96 * p, 96 * p + 48), False, True)
            for p in range(2):
                tt(a("DH", 48 * p, 48 * p + 48), a(D, 48 * p, 48 * p + 48), a("HG"), OP.mult)
            mm(a(N, 0, 192), a("IH"), a("NG"), True, False)
            for j in range(4):
                mm(a(N, 48 * j, 48 * j + 48), a("NI" if j % 2 else "IH"), a("DH", 48 * (j // 2), 48 * (j // 2) + 48), False, j == 3)
            act(a("ND"), a(N, 0, 192))
            cp(ind(a("NB"), a("OF", 0, 12)), a("ND"))
        rec("R", "arrive", (rnd,), [a("LD" + z)], [a("ZS" + z)], 0)
        ops[-1]["sem"] = "arr" + z
        ops[-1]["lat"] = 5000
        if rnd == 1:
            dma("Y", ("yx", (ALL, ALL)), a("X", 0, 512), 2500)
            act(a("ZZ", 48, 96), ind(a("LD1"), a("LI", 10, 13)))
            dma("S", ("yz", (ALL, ALL)), a("ZZ", 48, 96), 2500)

    def start(h, m0, t, first):
        ms(a2("JQ" + h, 1, 5), 80.0)
        if first:
            cp(a3("MC" + h, 0, 1), m0)
            cp(a2("SM" + h, 0, 1), m0)
        else:
            ms(a2("SM" + h, 4, 5), 0.0)
        cp(a2("JQ" + h, 0, 1), t)
        act(a3("M" + h, 0, 1), m0, AF.Identity, bias=-2048.0)
        act(a3("M" + h, 5, 6), t)
        rows(h, first, True)

    def new_lanes(h):
        n, MC, LB, QB = "n" + h, "MC" + h, PPS[int(h)], WP[int(h)]
        (cp if h == "1" else act)(a("XG" + h), ind(a("X", 0, 2048), a("L" + h, 0, 8)))
        if h == "0":
            act(a("XG0", 0, 48), ind(a("LD0"), a("LI", 10, 13)))
        mm(a(QB, 0, 8), a("BD"), a("WD", 8, 16), True, False)
        for b in range(16):
            mm(a(QB, 0, 8), a("BW", 15 - b, 143 - b), a("XG" + h, b, 128, 16), False, b == 15)
        ts(a(n, 96, 104), a(QB, 0, 8), 37.0, OP.mult, col("cf", 38) if h == "1" else rr, OP.add)
        ts(a(n, 104, 112), a(n, 96, 104), 2047, OP.bitwise_and)
        cp(a("L" + h, 16, 24), a(n, 104, 112))
        mm(a(LB, 64, 72), a("XG" + h), a("WD", 0, 8))

        def k(c):
            return a(n, 8 * c, 8 * c + 8)
        lane = col("cf", 35 if h == "1" else 0)
        cp(k(0), a(LB, 64, 72))
        ts(k(3), a(LB, 64, 72), 37.0, OP.mult, lane, OP.add)
        ts(k(1), k(0), 4095, OP.bitwise_and)
        ts(a3(MC, 0, 1), k(3), 2047, OP.bitwise_and)
        tt(k(2), k(1), k(1), OP.mult)
        ts(k(4), k(2), col("cf", 60 + int(h)), OP.add)
        ts(k(5), k(4), 5, OP.logical_shift_right, 63, OP.bitwise_and)
        start(h, a3(MC, 0, 1), k(5), False)

    def mark(k0, e):
        for o in ops[k0:]:
            o["step"] = e

    low = (slice(0, 32), ALL)
    cp(("CB", low), ("BG", low))
    mm(a(EB[0], 0, 32), ("CB", low), ("IH", (slice(0, 32), slice(0, 32))))
    cp(a("s0", 128, 160), a(EB[0], 0, 32))
    for h in "01":
        start(h, a("s0", 128 + int(h), 144, 2), a("s0", 144 + int(h), 160, 2), True)
    for rnd in range(2):
        order = "01" if rnd == 0 else "10"
        for h in order:
            if rnd:
                new_lanes(h)
            ms(a("YO" + h), 1 << 21)
            k0 = len(ops)
            prep(h, 1, FIRST[rnd] if h == order[0] else 0, rnd == 1)
            mark(k0, 1)
        for e in range(1, 7):
            for h in order:
                k0 = len(ops)
                heavy(h, e)
                if e == 6:
                    mark(k0, e)
                post(h, e, rnd)
                if e < 6:
                    mark(k0, e)
                    k0 = len(ops)
                    prep(h, e + 1, LAST[order.index(h)] if e == 5 else 0)
                    mark(k0, e + 1)
            if rnd == 0 and e == 1:
                late_constants()
        commit(rnd)
    return ops


def depend(ops):
    hist = {}
    prevg = []
    for k, o in enumerate(ops):
        deps = {}
        acc = [(_span(p), True) for p in o["outs"]] + [(_span(p), False) for p in o["ins"]]
        for (n, bits, c), wr in acc:
            ps = SCRATCH[n][0] == "psum"
            for (j, b2, w2) in hist.get(n, []):
                same = ops[j]["eng"] == o["eng"]
                if ps:
                    if same and o["eng"] == "P":
                        if "free" not in o or ops[j].get("free") != o["free"]:
                            deps.setdefault(j, False)
                    elif not same or ((wr or w2) and bits & b2):
                        deps[j] = True
                elif (wr or w2) and bits & b2:
                    deps[j] = True
        for (n, bits, c), wr in acc:
            old = hist.get(n, [])
            if SCRATCH[n][0] == "psum":
                old = (old if "free" in o else []) if o["eng"] == "P" else [t for t in old if t[2] or ops[t[0]]["eng"] == o["eng"]]
            elif wr and "sem" not in o:
                old = [t for t in old if t[1] & ~bits]
            hist[n] = old + [(k, bits, wr)]
        if "stage" in o:
            if prevg:
                deps.setdefault(prevg[-1], False)
            prevg.append(k)
        if "after" in o:
            deps.setdefault(o["after"], False)
        deps.pop(k, None)
        o["deps"] = deps


def kind(o):
    x = o["args"][1 if o["eng"] == "P" else 0]
    if not isinstance(x, tuple):
        return ""
    name = x[0].rstrip("01")
    if name == "n":
        name += str(x[1][1].start // 32)
    if name == "W" and x[1][1].start:
        name = "TG" + (o["args"][2][0] if o["eng"] == "P" else "")
    if name == "CU" and o["step"] == 1:
        name = "CU1"
    if name == "A" and o["call"] == "tensor_tensor":
        name = "J"
    return o["eng"] + name + ("" if "step" in o else "_")


def plan():
    ops = program()
    depend(ops)
    n = len(ops)
    cost = [o["cost"] for o in ops]
    tail = [o.get("lat", 0) for o in ops]
    before = [[(j, cost[j] + (0 if not hard else tail[j] + (SELF if ops[j]["eng"] == o["eng"] and "sem" not in ops[j] else HOP)))
               for j, hard in o["deps"].items()] for o in ops]
    kids = [[] for _ in range(n)]
    for k in range(n):
        for j, w in before[k]:
            kids[j].append((k, w))
    prio = [0.0] * n
    for k in range(n - 1, -1, -1):
        prio[k] = max([prio[c] + w for c, w in kids[k]] + [cost[k] + tail[k]])
    prio = [p + URGE.get(kind(o), 0) for p, o in zip(prio, ops)]
    left = [len(b) for b in before]
    ready = [0.0] * n
    pool = {e: [] for e in "VSPGYR"}
    free = {e: 0.0 for e in pool}
    order = {e: [] for e in pool}
    for k, o in enumerate(ops):
        if left[k] == 0:
            pool[o["eng"]].append(k)
    pick = {}
    for _ in range(n):
        best = None
        for e in pool:
            if pool[e]:
                if e not in pick:
                    t0 = max(free[e], min(ready[k] for k in pool[e]))
                    now = sorted((k for k in pool[e] if ready[k] <= t0 + 30), key=lambda k: (prio[k], -k))
                    k = now[-1]
                    if e in "VS":
                        soon = [j for j in pool[e] if t0 + 30 < ready[j] < t0 + cost[k] - 30 and prio[j] - prio[k] > ready[j] - t0 + 100]
                        if soon:
                            j = min(soon, key=lambda j: ready[j])
                            fit = [i for i in now if t0 + cost[i] <= ready[j] + 30]
                            k = fit[-1] if fit else j
                            t0 = max(t0, ready[k])
                    pick[e] = (t0, e, k)
                if best is None or pick[e][0] < best[0]:
                    best = pick[e]
        t0, e, k = best
        del pick[e]
        t0 = max(free[e], ready[k])
        free[e] = t0 + cost[k]
        pool[e].remove(k)
        order[e].append(k)
        for c, w in kids[k]:
            ready[c] = max(ready[c], t0 + w)
            left[c] -= 1
            if left[c] == 0:
                pool[ops[c]["eng"]].append(c)
                pick.pop(ops[c]["eng"], None)

    def play(order):
        t = [None] * n
        at = {e: 0 for e in order}
        free = {e: 0.0 for e in order}
        moved = True
        while moved:
            moved = False
            for e, q in order.items():
                p, f = at[e], free[e]
                while p < len(q) and all(t[j] is not None for j, w in before[q[p]]):
                    k = q[p]
                    t[k] = max([t[j] + w for j, w in before[k]] + [f])
                    f = t[k] + cost[k]
                    p += 1
                if p > at[e]:
                    at[e], free[e], moved = p, f, True
        if None in t:
            return 1e12, None
        return max(t[k] + cost[k] + tail[k] for k in range(n)), t
    end, t = play(order)
    tried = set()
    for _ in range(POLISH):
        place = {k: p for q in order.values() for p, k in enumerate(q)}
        k = max(range(n), key=lambda k: t[k] + cost[k] + tail[k])
        move = None
        while move is None:
            j = next((j for j, w in before[k] if abs(t[j] + w - t[k]) < 1), None)
            if j is None:
                if place[k] == 0:
                    break
                q = order[ops[k]["eng"]]
                j = q[place[k] - 1]
                due = max([t[i] + w for i, w in before[k]] + [0.0])
                p = place[k]
                while p > 0 and t[q[p - 1]] >= due - 130 and q[p - 1] not in ops[k]["deps"]:
                    p -= 1
                for to in (p, place[k] - 1):
                    if to < place[k] and (k, q[to]) not in tried and q[to] not in ops[k]["deps"]:
                        move = (k, to)
                        break
            k = j
        if move is None:
            break
        k, to = move
        e = ops[k]["eng"]
        tried.add((k, order[e][to]))
        q = list(order[e])
        q.insert(to, q.pop(place[k]))
        new = dict(order)
        new[e] = q
        v, tv = play(new)
        if v < end - 1:
            end, t, order = v, tv, new
    busy = {e: sum(cost[k] for k in order[e]) for e in order}
    pos = {k: p for q in order.values() for p, k in enumerate(q)}
    need = set()
    seen = {e: {} for e in order}
    known = {}
    for k in sorted(range(n), key=lambda k: (t[k], pos[k])):
        o = ops[k]
        o["t"] = t[k]
        o["waits"] = []
        mine = seen[o["eng"]]
        for j in sorted((j for j, hard in o["deps"].items() if hard), key=lambda j: -t[j]):
            key = ops[j].get("sem", ops[j]["eng"])
            if pos[j] > mine.get(key, -1) and o["eng"] != "R":
                o["waits"].append(j)
                need.add(j)
                mine[key] = pos[j]
                for x, p in known[j].items():
                    mine[x] = max(mine.get(x, -1), p)
        known[k] = dict(mine) if o["eng"] != "R" else {}
    total = {}
    for e in "VSPG":
        c = 0
        for k in order[e]:
            if k in need and "sem" not in ops[k]:
                c += 1
                ops[k]["mark"] = c
        total["c" + e] = c
    return ops, order, total, end, busy


PLAN = []


def rank_program(g, core, T, topo):
    rank = T.rank_of(core)
    if rank is None:
        return
    if not PLAN:
        PLAN.append(plan())
    ops, order, total, end, busy = PLAN[0]
    n = len(T.cores)
    peers = [T.cores[(rank + 1 + m) % n] for m in range(n - 1)]
    per = 2 * len(topo.engines(core, peers[0]))

    def real(x):
        if not isinstance(x, tuple):
            return x
        if x[0] == "*":
            return real(x[1]).indirect(real(x[2]))
        return T[x[0]][x[1]]

    queue = {"V": g.vector, "S": g.scalar, "P": g.tensor, "G": g, "Y": g.sync}
    for e in "YGVSP":
        q = queue[e]
        for k in order[e]:
            o = ops[k]
            for j in o["waits"]:
                p = ops[j]
                if p["eng"] == "R":
                    q.wait_ge(T.sem[p["sem"]], per)
                elif "sem" in p:
                    q.wait_ge(T.sem[p["sem"]], 16)
                else:
                    q.wait_ge(T.sem["c" + p["eng"]], p["mark"])
            c, args = o["call"], [real(x) for x in o["args"]]
            kw = {key: real(v) for key, v in o["kw"].items()}
            if c == "send":
                z = str(args[0])
                for group in ((0, 1), (2,)):
                    tr = []
                    for i, m in enumerate(group):
                        rid, pid = topo.addr(peers[m], core)
                        eng = topo.engines(core, peers[m])
                        eng = eng[i * len(eng) // len(group):(i + 1) * len(eng) // len(group)]
                        tr.append(RemoteDMATransfer(dst_ids=[DstId(rid=rid, pnc=pid)], dma_engine_mask=sum(1 << x for x in eng),
                                                    remote_sem=T.sem["arr" + z], src=T["ZS" + z][:, 16 * m:16 * m + 16],
                                                    dst=T["LD" + z][:, 16 * m:16 * m + 16]))
                    g.remote_dma_fused(tr, local_sem=T.sem.sent)
                continue
            if c == "dma_start":
                q.dma_start(*args).then_inc(T.sem[o["sem"]], 16)
                continue
            f = {"tensor_copy": lambda: q.tensor_copy(*args), "tensor_tensor": lambda: q.tensor_tensor(*args),
                 "tensor_scalar": lambda: q.tensor_scalar(*args), "memset": lambda: q.memset(*args),
                 "tensor_tensor_scan": lambda: q.tensor_tensor_scan(*args), "activation": lambda: q.activation(*args, **kw),
                 "tensor_reduce": lambda: q.tensor_reduce(*args), "matmul": lambda: q.matmul(*args),
                 "iota": lambda: q.iota(*args, **kw), "affine_select": lambda: q.affine_select(*args)}[c]()
            if "mark" in o:
                f.then_inc(T.sem["c" + e], 1)
    for o in ops:
        if o["call"] == "dma_start":
            g.wait_ge(T.sem[o["sem"]], 16)
    for s in total:
        if total[s]:
            g.wait_ge(T.sem[s], total[s])
    g.wait_ge(T.sem.sent, 2 * per)
